import numpy as np
import ml_dtypes


def mxq(x, axis, fmt="e4m3"):
    dtype, down = {"e4m3": (ml_dtypes.float8_e4m3fn, 7), "e5m2": (ml_dtypes.float8_e5m2, 14)}[fmt]
    v = np.moveaxis(np.asarray(x, np.float32).astype(ml_dtypes.bfloat16).astype(np.float64), axis, -1)
    blocks = v.reshape(v.shape[:-1] + (-1, 32))
    amax = np.abs(blocks).max(-1, keepdims=True)
    byte = np.maximum(np.where(amax > 0, np.frexp(amax)[1] - 1 + 127, 0) - down, 1)
    scale = np.exp2(byte - 127.0)
    codes = (blocks / scale).astype(np.float32).astype(dtype).astype(np.float64)
    return np.moveaxis((codes * scale).reshape(v.shape), -1, axis)


WIDE = False


def mx_kscale(k):
    if not WIDE:
        return np.ones(k)
    levels = np.array([10, -10, 5, -5, 0])
    if k % 512:
        return np.exp2(np.random.permutation(np.resize(levels, k // 32))).repeat(32)
    a = np.empty((k // 512, 16))
    for p in range(k // 512):
        a[p, :8] = np.random.permutation(np.resize(levels, 8))
        for g in range(8):
            far = levels[np.abs(levels - a[p, g]) >= 10]
            a[p, g + 8] = far[np.random.randint(len(far))]
    return np.exp2(a.ravel()).repeat(32)


def f64(x):
    return np.asarray(x).astype(np.float64)


def striped(idx):
    return np.tile(idx.reshape(-1, 16).T, (8, 1)).astype(np.uint16)


def unstriped(offs):
    return offs[:16].T.reshape(-1).astype(np.int64)


E2M1 = np.array([0.0, 0.5, 1.0, 1.5, 2.0, 3.0, 4.0, 6.0, -0.0, -0.5, -1.0, -1.5, -2.0, -3.0, -4.0, -6.0])


def pack_weight(w, fmt):
    k, n = w.shape
    w = f64(np.asarray(w, np.float32).astype(ml_dtypes.bfloat16)).reshape(k // 32, 32, n)
    amax = np.abs(w).max(1)
    if fmt == "e4m3":
        byte = np.frexp(amax)[1] - 1 + 127 - 7
    else:
        mant, ex = np.frexp(amax / 6.0)
        byte = np.where(mant > 0.5, ex, ex - 1) + 127
    byte = np.clip(np.where(amax > 0, byte, 1), 1, 254)
    scaled = (w * np.exp2(127.0 - byte)[:, None, :]).reshape(k, n).astype(np.float32)
    by_word = np.ascontiguousarray(scaled.reshape(k // 512, 128, 4, n).transpose(0, 1, 3, 2))
    if fmt == "e4m3":
        words = by_word.astype(ml_dtypes.float8_e4m3fn).view(np.uint8)
    else:
        c = by_word.astype(ml_dtypes.float4_e2m1fn).view(np.uint8) & 0xF
        words = (c[..., 0::2] | (c[..., 1::2] << 4)).reshape(k // 512, 128, 2 * n)
    return np.ascontiguousarray(words), np.ascontiguousarray(byte.astype(np.uint8).reshape(k // 512, 16, n))


def unpack_weight(words, scales, fmt):
    g, _, n = scales.shape
    words = np.ascontiguousarray(words).reshape(g, 128, n, -1)
    if fmt == "e4m3":
        vals = words.view(ml_dtypes.float8_e4m3fn).astype(np.float64)
    else:
        nib = np.empty((g, 128, n, 4), np.uint8)
        nib[..., 0::2] = words & 0xF
        nib[..., 1::2] = words >> 4
        vals = E2M1[nib]
    vals = vals * np.repeat(np.exp2(scales.astype(np.float64) - 127.0), 8, axis=1)[..., None]
    return vals.transpose(0, 1, 3, 2).reshape(g * 512, n)


def gelu(v):
    return 0.5 * v * (1.0 + np.tanh(np.sqrt(2.0 / np.pi) * (v + 0.044715 * v**3)))


def striped8(idx):
    return np.concatenate([v.reshape(-1, 16).T for v in idx]).astype(np.uint16)


def unstriped8(offs):
    return np.stack([offs[16 * g:16 * g + 16].T.reshape(-1) for g in range(8)]).astype(np.int64)


def runs(v, idx8):
    k = np.arange(v.shape[0])
    return v[k[:, None], idx8[k % 512 // 64]]


def put_heads(h, wgs, idx8, t2):
    r = np.arange(h.shape[0])
    page = np.zeros((h.shape[0], t2))
    page[r[:, None], idx8[r % 512 // 64]] = wgs[r // 4 % 128] * h
    return page


K, T, S, H, N, T2 = 1024, 2048, 1024, 512, 1024, 2048

def setup_inputs():
    n = np.random.standard_normal
    s = mx_kscale(K)[:, None]
    u = mx_kscale(H)[:, None]
    tab_words, tab_scales = pack_weight(n((K, T)) * s, "e4m3")
    wab = n((K, 2 * H)) / np.sqrt(K) / s * np.tile(u.T, (1, 2))
    eps = np.random.uniform(0.1, 0.5, H) * np.square(u[:, 0])
    wc_words, wc_scales = pack_weight(1.5 * n((H, N)) / np.sqrt(H) / u, "e2m1")
    wgo = np.repeat(np.random.uniform(0.5, 2.0, (8, S)), 16, axis=0)
    return {
        "tab_words": tab_words, "tab_scales": tab_scales,
        "offs": striped8(np.stack([np.random.permutation(T)[:S] for _ in range(8)])),
        "wab": wab.astype(np.float32),
        "eps": eps.astype(np.float32),
        "wc_words": wc_words, "wc_scales": wc_scales,
        "wgo": wgo.astype(np.float32),
        "offs2": striped8(np.stack([np.random.permutation(T2)[:S] for _ in range(8)])),
    }

def reference(tab_words, tab_scales, offs, wab, eps, wc_words, wc_scales, wgo, offs2):
    v = runs(unpack_weight(tab_words, tab_scales, "e4m3"), unstriped8(offs))
    sq = np.square(mxq(f64(wab), 0, "e4m3").T @ v)
    h = np.sqrt(sq[:H] + sq[H:] + f64(eps)[:, None])
    c = unpack_weight(wc_words, wc_scales, "e2m1").T @ mxq(h, 0, "e4m3")
    y = np.log1p(np.abs(c))
    return put_heads(y, f64(wgo), unstriped8(offs2), T2)

@@ -1,0 +1,310 @@
+from contextlib import ExitStack
+
+import concourse.mybir as mybir
+from concourse.masks import make_identity
+
+K, T, S, H, N, T2 = 1024, 2048, 1024, 512, 1024, 2048
+FLOPS = 2 * K * 2 * H * S + 2 * H * N * S
+
+F32 = mybir.dt.float32
+BF16 = mybir.dt.bfloat16
+I32 = mybir.dt.int32
+U32 = mybir.dt.uint32
+U16 = mybir.dt.uint16
+U8 = mybir.dt.uint8
+FP8X4 = mybir.dt.float8_e4m3fn_x4
+FP4X4 = mybir.dt.float4_e2m1fn_x4
+ACT = mybir.ActivationFunctionType
+MULT = mybir.AluOpType.mult
+
+P = 128
+BANK = 512
+LATER = ("w1", "w2", "w3", "tab0", "eps")
+SCALAR_CAST_COLUMNS = {(0, 0): 512, (0, 1): 512, (1, 0): 256, (1, 1): 192}
+VECTOR_SQUARED = (2,)
+
+
+def tile_list_bell_envelope_chart_kernel(
+    tc, tab_words, tab_scales, offs, wab, eps, wc_words, wc_scales, wgo, offs2, out
+):
+    nc = tc.nc
+    with ExitStack() as ctx:
+        lists = ctx.enter_context(tc.tile_pool(name="lists", bufs=1))
+        sb = ctx.enter_context(tc.tile_pool(name="sb", bufs=1))
+        ring = ctx.enter_context(tc.tile_pool(name="ring", bufs=2))
+        psum = ctx.enter_context(tc.psum_pool(name="psum", bufs=1))
+
+        def held(name, shape, dtype, tag=None):
+            pool = later[0] if tag in LATER else sb
+            return pool.tile(shape, dtype, name=name, tag=tag or name, align_bytes=64)
+
+        later = []
+
+        banks = [psum.tile([P, BANK], F32, name="bank%d" % b) for b in range(8)]
+        pick = lists.tile([P, S // 16], U16, name="pick")
+        place = lists.tile([P, S // 16], U16, name="place")
+
+        scale_window = held("scale_window", [P, T], U8)
+        warm_out = held("warm_out", [P, 1], F32)
+        nc.gpsimd.memset(scale_window[:].bitcast(I32), 0)
+        with tc.tile_pool(name="first", bufs=1) as first:
+            warm = first.tile([P, 1], F32, name="warm")
+            nc.vector.memset(warm[:], 1.0)
+            nc.scalar.activation(warm_out[:, 0:1], warm[:], ACT.Sqrt)
+        later.append(ctx.enter_context(tc.tile_pool(name="later", bufs=1)))
+        ident = held("ident", [P, P], F32)
+        make_identity(nc, ident[:])
+
+        w_raw = {}
+        tab = {}
+
+        def load_w(a, f, lo, hi):
+            if lo == 0:
+                w_raw[a, f] = held("w_raw%d%d" % (a, f), [P, 4, H], F32, tag="w%d" % (2 * a + f))
+            rows = wab[512 * a : 512 * (a + 1), H * f : H * (f + 1)].rearrange("(p i) c -> p i c", i=4)
+            nc.sync.dma_start(w_raw[a, f][:, lo:hi, :], rows[:, lo:hi, :])
+
+        def load_tab(a):
+            tab[a] = held("tab%d" % a, [P, T], I32, tag="tab%d" % a)
+            nc.sync.dma_start(tab[a][:], tab_words[a].rearrange("p t i -> p (t i)").bitcast(I32))
+
+        nc.sync.dma_start(pick[:], offs)
+        nc.sync.dma_start(place[:], offs2)
+        load_w(0, 0, 0, 4)
+        for a in range(2):
+            rows = tab_scales[a].bitcast(I32).rearrange("(g e) t -> e g t", e=2)
+            for e in range(2):
+                nc.sync.dma_start(scale_window[4 * a + e : P : 16, :].bitcast(I32), rows[e])
+        load_w(0, 1, 0, 4)
+        load_tab(0)
+        load_w(1, 0, 0, 4)
+        eps_sb = held("eps_sb", [P, 4], F32, tag="eps")
+        nc.sync.dma_start(eps_sb[:], eps.rearrange("(p i) -> p i", i=4))
+        load_w(1, 1, 0, 4)
+
+        pages = {}
+
+        def clear_page(page, engine, tag=None):
+            pages[page] = held("page%d" % page, [P, T2], F32, tag=tag)
+            engine.memset(pages[page][:], 0.0)
+
+        for page in range(4):
+            clear_page(page, nc.vector if page < 2 else nc.gpsimd)
+
+        picked_scales = held("picked_scales", [P, S], U8, tag="tab1")
+        v_scales = held("v_scales", [P, S], U8)
+        nc.vector.tensor_copy(picked_scales[:], scale_window[:].indirect(pick[:]))
+        nc.vector.tensor_copy(v_scales[:].bitcast(I32), picked_scales[:].bitcast(I32))
+        for a in range(2):
+            for e in range(2):
+                nc.sync.dma_start(
+                    v_scales[4 * a + 2 + e : P : 32, :].bitcast(I32),
+                    v_scales[16 + 4 * a + e : P : 32, :].bitcast(I32),
+                )
+        load_tab(1)
+
+        eps_rows = held("eps_rows", [P, BANK], F32)
+        for i in range(4):
+            nc.tensor.transpose(
+                banks[7][:, P * i : P * (i + 1)], eps_sb[:, i : i + 1].to_broadcast([P, P]), ident[:]
+            )
+        nc.scalar.copy(eps_rows[:], banks[7][:])
+
+        w_codes = {}
+        w_scales = {}
+
+        def quantise_w(a, f):
+            grouped = held("w_bf%d%d" % (a, f), [P, H, 4], BF16)
+            split = SCALAR_CAST_COLUMNS[a, f]
+            for lo, hi, copy in ((0, split, nc.scalar.copy), (split, H, nc.vector.tensor_copy)):
+                if hi > lo:
+                    copy(
+                        grouped[:, lo:hi, :].rearrange("p (c u) i -> p c i u", u=4),
+                        w_raw[a, f][:, :, lo:hi].rearrange("p i (c u) -> p c i u", u=4),
+                    )
+            w_codes[a, f] = held("w_codes%d%d" % (a, f), [P, H], U32, tag=("scale_window" if a + f == 0 else None))
+            w_scales[a, f] = held("w_scales%d%d" % (a, f), [P, H], U8)
+            nc.vector.quantize_mx(
+                out=w_codes[a, f][:].bitcast(FP8X4),
+                scales=w_scales[a, f][:],
+                in_=grouped[:].rearrange("p c i -> p (c i)"),
+            )
+
+        v_codes = [held("v_codes%d" % a, [P, S], U32) for a in range(2)]
+
+        def gather_words(a, lo, hi):
+            nc.vector.tensor_copy(
+                v_codes[a][:, lo:hi], tab[a][:].bitcast(U32).indirect(pick[:, lo // 16 : hi // 16])
+            )
+
+        def filter_pass(jt, f, a, bank):
+            cols = slice(P * jt, P * (jt + 1))
+            nc.tensor.matmul_mx(
+                out=banks[bank][:],
+                lhsT=v_codes[a][:, cols].bitcast(FP8X4),
+                lhsT_scale=v_scales[4 * a : P, cols],
+                rhs=w_codes[a, f][:].bitcast(FP8X4),
+                rhs_scale=w_scales[a, f][:],
+                start=(a == 0),
+                stop=(a == 1),
+            )
+
+        squares = {}
+
+        def square(jt, f, bank):
+            if f == 0:
+                pair = held("squares%d" % jt, [P, 2 * BANK], F32, tag="sq%d" % (jt % 4))
+                squares[jt, 0] = pair[:, 0:BANK]
+                squares[jt, 1] = pair[:, BANK:]
+            source = banks[bank][:].rearrange("j (p i) -> j i p", i=4)
+            if jt in VECTOR_SQUARED:
+                plain = ring.tile([P, BANK], F32, name="plain")
+                nc.vector.tensor_copy(plain[:].rearrange("j (i p) -> j i p", i=4), source)
+                nc.vector.tensor_tensor(squares[jt, f], plain[:], plain[:], MULT)
+            else:
+                nc.scalar.activation(squares[jt, f].rearrange("j (i p) -> j i p", i=4), source, ACT.Square)
+
+        def filters(jt, bank_a, bank_b):
+            for f, bank in ((0, bank_a), (1, bank_b)):
+                filter_pass(jt, f, 0, bank)
+                filter_pass(jt, f, 1, bank)
+                square(jt, f, bank)
+
+        def add_turned(source, bank, first, last):
+            for i in range(4):
+                cols = slice(P * i, P * (i + 1))
+                nc.tensor.matmul(
+                    banks[bank][:, cols], source[:, cols], ident[:], is_transpose=True,
+                    start=(first and i == 0), stop=(last and i == 3),
+                )
+
+        def envelope(jt, bank, h_bf):
+            add_turned(eps_rows, bank, True, False)
+            add_turned(squares[jt, 0], bank, False, False)
+            add_turned(squares[jt, 1], bank, False, True)
+            nc.scalar.activation(
+                h_bf.rearrange("p (j i) -> p j i", i=4), banks[bank][:].rearrange("p (i j) -> p j i", i=4), ACT.Sqrt
+            )
+
+        h_codes = held("h_codes", [P, S], U32)
+        h_scales = held("h_scales", [P, S], U8)
+
+        def quantise_h(lo, hi, h_bf):
+            nc.vector.quantize_mx(out=h_codes[:, lo:hi].bitcast(FP8X4), scales=h_scales[:, lo:hi], in_=h_bf)
+
+        out_pages = out.rearrange("(b p i) t -> b i p t", b=2, i=4)
+
+        def features(page_list, lo, hi, bank, y, tag=None):
+            width = hi - lo
+            total = width * len(page_list)
+            for n, page in enumerate(page_list):
+                nc.tensor.matmul_mx(
+                    out=banks[bank][:, width * n : width * (n + 1)],
+                    lhsT=wc_codes[:, 2 * P * page : 2 * P * (page + 1)].bitcast(FP4X4),
+                    lhsT_scale=wc_planes[:, P * page : P * (page + 1)],
+                    rhs=h_codes[:, lo:hi].bitcast(FP8X4),
+                    rhs_scale=h_scales[:, lo:hi],
+                    start=True,
+                    stop=True,
+                )
+            if tag is None:
+                size = ring.tile([P, BANK], F32, name="size")
+            else:
+                size = held("size_" + tag, [P, BANK], F32, tag=tag)
+            nc.scalar.activation(size[:, 0:total], banks[bank][:, 0:total], ACT.Abs)
+            nc.scalar.activation(y, size[:, 0:total], ACT.Ln, bias=1.0)
+
+        def scatter(page_list, lo, hi, y):
+            width = hi - lo
+            for n, page in enumerate(page_list):
+                nc.vector.tensor_tensor(
+                    pages[page][:].indirect(place[:, lo // 16 : hi // 16]),
+                    y[:, width * n : width * (n + 1)],
+                    wgo_sb[:, lo:hi],
+                    MULT,
+                )
+
+        quantise_w(0, 0)
+        gather_words(0, 0, S)
+        quantise_w(0, 1)
+        wc_raw = held("wc_raw", [P, 2 * N], U8, tag="w_bf01")
+        nc.sync.dma_start(wc_raw[:].bitcast(I32), wc_words[0].bitcast(I32))
+        wc_scale_raw = held("wc_scale_raw", [P, N], U8, tag="w1")
+        nc.vector.memset(wc_scale_raw[:].bitcast(I32), 0)
+        for d in range(4):
+            nc.sync.dma_start(
+                wc_scale_raw[32 * d : 32 * d + 4, :].bitcast(I32),
+                wc_scales[0, 4 * d : 4 * d + 4, :].bitcast(I32),
+            )
+        quantise_w(1, 0)
+        wgo_sb = held("wgo_sb", [P, S], F32, tag="w_bf10")
+        nc.sync.dma_start(wgo_sb[:], wgo)
+        quantise_w(1, 1)
+        for jt in range(2):
+            for f in range(2):
+                filter_pass(jt, f, 0, 2 * jt + f)
+        gather_words(1, 0, 256)
+        for jt in range(2):
+            for f in range(2):
+                filter_pass(jt, f, 1, 2 * jt + f)
+                square(jt, f, 2 * jt + f)
+        gather_words(1, 256, 512)
+        gather_words(1, 512, S)
+        wc_codes = held("wc_codes", [P, 2 * N], U8, tag="tab1")
+        nc.vector.tensor_copy(
+            wc_codes[:].bitcast(U16).rearrange("p (b i m) -> p b i m", b=2, i=4),
+            wc_raw[:].bitcast(U16).rearrange("p (b m i) -> p b i m", b=2, i=4),
+        )
+        wc_planes = held("wc_planes", [P, N], U8, tag="w_bf01")
+        nc.vector.tensor_copy(
+            wc_planes[:].rearrange("p (b i m) -> p b i m", b=2, i=4),
+            wc_scale_raw[:].rearrange("p (b m i) -> p b i m", b=2, i=4),
+        )
+        h_first = [held("h_first0", [P, BANK], BF16), held("h_first1", [P, BANK], BF16, tag="page4")]
+        for jt in range(2):
+            envelope(jt, 4 + jt, h_first[jt][:])
+            quantise_h(P * jt, P * (jt + 1), h_first[jt][:])
+        log_warm = held("log_warm", [P, 1], F32, tag="sq3")
+        nc.scalar.activation(log_warm[:], h_first[1][:, 0:1], ACT.Ln)
+        clear_page(4, nc.gpsimd)
+        filters(2, 6, 7)
+
+        groups = ([0], [1, 2], [3, 4], [5, 6])
+
+        y1 = held("y1", [P, 8 * 256], F32, tag="w0")
+        for n, group in enumerate(groups):
+            y = y1[:, 256 * group[0] : 256 * (group[-1] + 1)]
+            features(group, 0, 256, 2 + n, y, tag=("page%d" % (5 + n) if n < 3 else None))
+            if n < 3:
+                clear_page(5 + n, nc.gpsimd)
+            scatter(group, 0, 256, y)
+        filters(3, 0, 1)
+        filters(4, 6, 7)
+        h_second = held("h_second", [P, 2 * BANK], BF16)
+        for jt in (2, 3):
+            envelope(jt, 2 + jt, h_second[:, BANK * (jt - 2) : BANK * (jt - 1)])
+        quantise_h(256, 512, h_second[:])
+        features([7], 0, 256, 4, y1[:, 256 * 7 :])
+        scatter([7], 0, 256, y1[:, 256 * 7 :])
+        filters(5, 2, 3)
+
+        y2 = held("y2", [P, 8 * 256], F32, tag="w1")
+        for n, group in enumerate(groups):
+            y = y2[:, 256 * group[0] : 256 * (group[-1] + 1)]
+            features(group, 256, 512, (6 + n) % 8, y)
+            scatter(group, 256, 512, y)
+        filters(6, 2, 3)
+        filters(7, 4, 5)
+        h_third = held("h_third", [P, 4 * BANK], BF16)
+        for jt in range(4, 8):
+            envelope(jt, (2 + jt) % 8, h_third[:, BANK * (jt - 4) : BANK * (jt - 3)])
+        quantise_h(512, S, h_third[:])
+        features([7], 256, 512, 0, y2[:, 256 * 7 :])
+        scatter([7], 256, 512, y2[:, 256 * 7 :])
+
+        y3 = [held("y3%d" % b, [P, 4 * 512], F32, tag="w%d" % (2 + b)) for b in range(2)]
+        for page in range(8):
+            y = y3[page // 4][:, 512 * (page % 4) : 512 * (page % 4 + 1)]
+            features([page], 512, S, (2, 3, 4, 5, 6, 7, 1, 0)[page], y)
+            scatter([page], 512, S, y)
+            nc.sync.dma_start(out_pages[page // 4, page % 4], pages[page][:])

@@ -20,7 +20,7 @@ MULT = mybir.AluOpType.mult
 P = 128
 BANK = 512
 LATER = ("w1", "w2", "w3", "tab0", "eps")
-SCALAR_CAST_COLUMNS = {(0, 0): 512, (0, 1): 512, (1, 0): 256, (1, 1): 192}
+SCALAR_CAST_COLUMNS = {(0, 0): 512, (0, 1): 512, (1, 0): 256, (1, 1): 256}
 VECTOR_SQUARED = (2,)
 
 
@@ -75,8 +75,8 @@ def tile_list_bell_envelope_chart_kernel(
             rows = tab_scales[a].bitcast(I32).rearrange("(g e) t -> e g t", e=2)
             for e in range(2):
                 nc.sync.dma_start(scale_window[4 * a + e : P : 16, :].bitcast(I32), rows[e])
-        load_w(0, 1, 0, 4)
         load_tab(0)
+        load_w(0, 1, 0, 4)
         load_w(1, 0, 0, 4)
         eps_sb = held("eps_sb", [P, 4], F32, tag="eps")
         nc.sync.dma_start(eps_sb[:], eps.rearrange("(p i) -> p i", i=4))
@@ -88,13 +88,15 @@ def tile_list_bell_envelope_chart_kernel(
             pages[page] = held("page%d" % page, [P, T2], F32, tag=tag)
             engine.memset(pages[page][:], 0.0)
 
-        for page in range(4):
-            clear_page(page, nc.vector if page < 2 else nc.gpsimd)
+        for page in range(3):
+            clear_page(page, nc.vector)
 
-        picked_scales = held("picked_scales", [P, S], U8, tag="tab1")
+        picked_scales = [held("picked_scales%d" % n, [P, BANK], U8, tag=("v_codes0", "tab1")[n]) for n in range(2)]
         v_scales = held("v_scales", [P, S], U8)
-        nc.vector.tensor_copy(picked_scales[:], scale_window[:].indirect(pick[:]))
-        nc.vector.tensor_copy(v_scales[:].bitcast(I32), picked_scales[:].bitcast(I32))
+        for n in range(2):
+            nc.vector.tensor_copy(picked_scales[n][:], scale_window[:].indirect(pick[:, 32 * n : 32 * (n + 1)]))
+        for n in range(2):
+            nc.vector.tensor_copy(v_scales[:, BANK * n : BANK * (n + 1)].bitcast(I32), picked_scales[n][:].bitcast(I32))
         for a in range(2):
             for e in range(2):
                 nc.sync.dma_start(
@@ -229,17 +231,17 @@ def tile_list_bell_envelope_chart_kernel(
         quantise_w(0, 1)
         wc_raw = held("wc_raw", [P, 2 * N], U8, tag="w_bf01")
         nc.sync.dma_start(wc_raw[:].bitcast(I32), wc_words[0].bitcast(I32))
-        wc_scale_raw = held("wc_scale_raw", [P, N], U8, tag="w1")
+        quantise_w(1, 0)
+        wgo_sb = held("wgo_sb", [P, S], F32, tag="w_bf10")
+        nc.sync.dma_start(wgo_sb[:], wgo)
+        quantise_w(1, 1)
+        wc_scale_raw = held("wc_scale_raw", [P, N], U8, tag="w3")
         nc.vector.memset(wc_scale_raw[:].bitcast(I32), 0)
         for d in range(4):
             nc.sync.dma_start(
                 wc_scale_raw[32 * d : 32 * d + 4, :].bitcast(I32),
                 wc_scales[0, 4 * d : 4 * d + 4, :].bitcast(I32),
             )
-        quantise_w(1, 0)
-        wgo_sb = held("wgo_sb", [P, S], F32, tag="w_bf10")
-        nc.sync.dma_start(wgo_sb[:], wgo)
-        quantise_w(1, 1)
         for jt in range(2):
             for f in range(2):
                 filter_pass(jt, f, 0, 2 * jt + f)
@@ -260,13 +262,13 @@ def tile_list_bell_envelope_chart_kernel(
             wc_planes[:].rearrange("p (b i m) -> p b i m", b=2, i=4),
             wc_scale_raw[:].rearrange("p (b m i) -> p b i m", b=2, i=4),
         )
-        h_first = [held("h_first0", [P, BANK], BF16), held("h_first1", [P, BANK], BF16, tag="page4")]
+        h_first = [held("h_first0", [P, BANK], BF16), held("h_first1", [P, BANK], BF16, tag="page3")]
         for jt in range(2):
             envelope(jt, 4 + jt, h_first[jt][:])
             quantise_h(P * jt, P * (jt + 1), h_first[jt][:])
         log_warm = held("log_warm", [P, 1], F32, tag="sq3")
         nc.scalar.activation(log_warm[:], h_first[1][:, 0:1], ACT.Ln)
-        clear_page(4, nc.gpsimd)
+        clear_page(3, nc.gpsimd)
         filters(2, 6, 7)
 
         groups = ([0], [1, 2], [3, 4], [5, 6])
@@ -274,9 +276,8 @@ def tile_list_bell_envelope_chart_kernel(
         y1 = held("y1", [P, 8 * 256], F32, tag="w0")
         for n, group in enumerate(groups):
             y = y1[:, 256 * group[0] : 256 * (group[-1] + 1)]
-            features(group, 0, 256, 2 + n, y, tag=("page%d" % (5 + n) if n < 3 else None))
-            if n < 3:
-                clear_page(5 + n, nc.gpsimd)
+            features(group, 0, 256, 2 + n, y, tag="page%d" % (4 + n))
+            clear_page(4 + n, nc.gpsimd)
             scatter(group, 0, 256, y)
         filters(3, 0, 1)
         filters(4, 6, 7)

@@ -16,12 +16,12 @@ FP8X4 = mybir.dt.float8_e4m3fn_x4
 FP4X4 = mybir.dt.float4_e2m1fn_x4
 ACT = mybir.ActivationFunctionType
 MULT = mybir.AluOpType.mult
+MAX = mybir.AluOpType.max
 
 P = 128
 BANK = 512
-LATER = ("w1", "w2", "w3", "tab0", "eps")
-SCALAR_CAST_COLUMNS = {(0, 0): 512, (0, 1): 512, (1, 0): 256, (1, 1): 256}
-VECTOR_SQUARED = (2,)
+HALF = 256
+SCALAR_CAST_COLUMNS = {"a0": 512, "a1": 512, "b0lo": 256, "b1lo": 0, "b0hi": 0, "b1hi": 0}
 
 
 def tile_list_bell_envelope_chart_kernel(
@@ -34,140 +34,138 @@ def tile_list_bell_envelope_chart_kernel(
         ring = ctx.enter_context(tc.tile_pool(name="ring", bufs=2))
         psum = ctx.enter_context(tc.psum_pool(name="psum", bufs=1))
 
-        def held(name, shape, dtype, tag=None):
-            pool = later[0] if tag in LATER else sb
+        def held(pool, name, shape, dtype, tag=None):
             return pool.tile(shape, dtype, name=name, tag=tag or name, align_bytes=64)
-
-        later = []
 
         banks = [psum.tile([P, BANK], F32, name="bank%d" % b) for b in range(8)]
         pick = lists.tile([P, S // 16], U16, name="pick")
         place = lists.tile([P, S // 16], U16, name="place")
 
-        scale_window = held("scale_window", [P, T], U8)
-        warm_out = held("warm_out", [P, 1], F32)
+        scale_window = held(sb, "scale_window", [P, T], U8)
+        warm_out = held(sb, "warm_out", [P, 1], F32)
         nc.gpsimd.memset(scale_window[:].bitcast(I32), 0)
         with tc.tile_pool(name="first", bufs=1) as first:
             warm = first.tile([P, 1], F32, name="warm")
             nc.vector.memset(warm[:], 1.0)
             nc.scalar.activation(warm_out[:, 0:1], warm[:], ACT.Sqrt)
-        later.append(ctx.enter_context(tc.tile_pool(name="later", bufs=1)))
-        ident = held("ident", [P, P], F32)
+        second = ctx.enter_context(tc.tile_pool(name="second", bufs=1))
+        ident = held(sb, "ident", [P, P], F32)
         make_identity(nc, ident[:])
 
         w_raw = {}
         tab = {}
 
-        def load_w(a, f, lo, hi):
-            if lo == 0:
-                w_raw[a, f] = held("w_raw%d%d" % (a, f), [P, 4, H], F32, tag="w%d" % (2 * a + f))
-            rows = wab[512 * a : 512 * (a + 1), H * f : H * (f + 1)].rearrange("(p i) c -> p i c", i=4)
-            nc.sync.dma_start(w_raw[a, f][:, lo:hi, :], rows[:, lo:hi, :])
+        def load_w(pool, name, a, lo, hi):
+            w_raw[name] = held(pool, "raw_" + name, [P, 4, hi - lo], F32)
+            rows = wab[512 * a : 512 * (a + 1), lo:hi].rearrange("(p i) c -> p i c", i=4)
+            nc.sync.dma_start(w_raw[name][:], rows)
 
-        def load_tab(a):
-            tab[a] = held("tab%d" % a, [P, T], I32, tag="tab%d" % a)
+        def load_tab(pool, a):
+            tab[a] = held(pool, "tab%d" % a, [P, T], I32)
             nc.sync.dma_start(tab[a][:], tab_words[a].rearrange("p t i -> p (t i)").bitcast(I32))
 
         nc.sync.dma_start(pick[:], offs)
         nc.sync.dma_start(place[:], offs2)
-        load_w(0, 0, 0, 4)
+        load_w(sb, "a0", 0, 0, H)
         for a in range(2):
             rows = tab_scales[a].bitcast(I32).rearrange("(g e) t -> e g t", e=2)
             for e in range(2):
                 nc.sync.dma_start(scale_window[4 * a + e : P : 16, :].bitcast(I32), rows[e])
-        load_tab(0)
-        load_w(0, 1, 0, 4)
-        load_w(1, 0, 0, 4)
-        eps_sb = held("eps_sb", [P, 4], F32, tag="eps")
+        load_tab(second, 0)
+        eps_sb = held(second, "eps_sb", [P, 4], F32)
         nc.sync.dma_start(eps_sb[:], eps.rearrange("(p i) -> p i", i=4))
-        load_w(1, 1, 0, 4)
+        load_w(second, "a1", 1, 0, H)
+        load_tab(second, 1)
 
         pages = {}
 
         def clear_page(page, engine, tag=None):
-            pages[page] = held("page%d" % page, [P, T2], F32, tag=tag)
+            pages[page] = held(sb, "page%d" % page, [P, T2], F32, tag=tag)
             engine.memset(pages[page][:], 0.0)
 
-        for page in range(3):
-            clear_page(page, nc.vector)
+        clear_page(0, nc.vector)
+        clear_page(1, nc.vector)
+        clear_page(2, nc.gpsimd)
+        clear_page(3, nc.gpsimd)
 
-        picked_scales = [held("picked_scales%d" % n, [P, BANK], U8, tag=("v_codes0", "tab1")[n]) for n in range(2)]
-        v_scales = held("v_scales", [P, S], U8)
-        for n in range(2):
-            nc.vector.tensor_copy(picked_scales[n][:], scale_window[:].indirect(pick[:, 32 * n : 32 * (n + 1)]))
-        for n in range(2):
-            nc.vector.tensor_copy(v_scales[:, BANK * n : BANK * (n + 1)].bitcast(I32), picked_scales[n][:].bitcast(I32))
+        v_scales = held(sb, "v_scales", [P, S], U8)
+        with tc.tile_pool(name="picked", bufs=1) as picked_pool:
+            picked = held(picked_pool, "picked_scales", [P, S], U8)
+            nc.vector.tensor_copy(picked[:], scale_window[:].indirect(pick[:]))
+            nc.vector.tensor_copy(v_scales[:].bitcast(I32), picked[:].bitcast(I32))
+        third = ctx.enter_context(tc.tile_pool(name="third", bufs=1))
         for a in range(2):
             for e in range(2):
                 nc.sync.dma_start(
                     v_scales[4 * a + 2 + e : P : 32, :].bitcast(I32),
                     v_scales[16 + 4 * a + e : P : 32, :].bitcast(I32),
                 )
-        load_tab(1)
-
-        eps_rows = held("eps_rows", [P, BANK], F32)
-        for i in range(4):
-            nc.tensor.transpose(
-                banks[7][:, P * i : P * (i + 1)], eps_sb[:, i : i + 1].to_broadcast([P, P]), ident[:]
+        for half, lo in (("lo", H), ("hi", H + HALF)):
+            for a in range(2):
+                load_w(third, "b%d%s" % (a, half), a, lo, lo + HALF)
+        wc_raw = held(third, "wc_raw", [P, 2 * N], U8)
+        nc.sync.dma_start(wc_raw[:].bitcast(I32), wc_words[0].bitcast(I32))
+        wc_scale_raw = held(third, "wc_scale_raw", [P, N], U8)
+        nc.gpsimd.memset(wc_scale_raw[:].bitcast(I32), 0)
+        for d in range(4):
+            nc.sync.dma_start(
+                wc_scale_raw[32 * d : 32 * d + 4, :].bitcast(I32),
+                wc_scales[0, 4 * d : 4 * d + 4, :].bitcast(I32),
             )
-        nc.scalar.copy(eps_rows[:], banks[7][:])
 
-        w_codes = {}
-        w_scales = {}
 
-        def quantise_w(a, f):
-            grouped = held("w_bf%d%d" % (a, f), [P, H, 4], BF16)
-            split = SCALAR_CAST_COLUMNS[a, f]
-            for lo, hi, copy in ((0, split, nc.scalar.copy), (split, H, nc.vector.tensor_copy)):
+        w_codes = {name: held(third, "codes_" + name, [P, H], U32) for name in ("a0", "b0", "a1", "b1")}
+        w_scales = {name: held(sb, "scales_" + name, [P, H], U8) for name in ("a0", "b0", "a1", "b1")}
+
+        def quantise_w(pool, name, target, first_col, width):
+            grouped = held(pool, "bf_" + name, [P, width, 4], BF16, tag="bf" + name[1])
+            split = SCALAR_CAST_COLUMNS[name]
+            for lo, hi, copy in ((0, split, nc.scalar.copy), (split, width, nc.vector.tensor_copy)):
                 if hi > lo:
                     copy(
                         grouped[:, lo:hi, :].rearrange("p (c u) i -> p c i u", u=4),
-                        w_raw[a, f][:, :, lo:hi].rearrange("p i (c u) -> p c i u", u=4),
+                        w_raw[name][:, :, lo:hi].rearrange("p i (c u) -> p c i u", u=4),
                     )
-            w_codes[a, f] = held("w_codes%d%d" % (a, f), [P, H], U32, tag=("scale_window" if a + f == 0 else None))
-            w_scales[a, f] = held("w_scales%d%d" % (a, f), [P, H], U8)
+            cols = slice(first_col, first_col + width)
             nc.vector.quantize_mx(
-                out=w_codes[a, f][:].bitcast(FP8X4),
-                scales=w_scales[a, f][:],
+                out=w_codes[target][:, cols].bitcast(FP8X4),
+                scales=w_scales[target][:, cols],
                 in_=grouped[:].rearrange("p c i -> p (c i)"),
             )
 
-        v_codes = [held("v_codes%d" % a, [P, S], U32) for a in range(2)]
+        v_codes = {}
 
-        def gather_words(a, lo, hi):
-            nc.vector.tensor_copy(
-                v_codes[a][:, lo:hi], tab[a][:].bitcast(U32).indirect(pick[:, lo // 16 : hi // 16])
-            )
+        def gather_words(pool, a, lo, hi, tag=None):
+            words = held(pool, "v_codes%d_%d" % (a, lo), [P, hi - lo], U32, tag=tag)
+            nc.vector.tensor_copy(words[:], tab[a][:].bitcast(U32).indirect(pick[:, lo // 16 : hi // 16]))
+            for jt in range(lo // P, hi // P):
+                v_codes[a, jt] = words[:, P * jt - lo : P * (jt + 1) - lo]
 
-        def filter_pass(jt, f, a, bank):
-            cols = slice(P * jt, P * (jt + 1))
+        def filter_pass(jt, f, a, bank, lo=0, hi=H, at=0):
+            name = f + str(a)
             nc.tensor.matmul_mx(
-                out=banks[bank][:],
-                lhsT=v_codes[a][:, cols].bitcast(FP8X4),
-                lhsT_scale=v_scales[4 * a : P, cols],
-                rhs=w_codes[a, f][:].bitcast(FP8X4),
-                rhs_scale=w_scales[a, f][:],
+                out=banks[bank][:, at : at + hi - lo],
+                lhsT=v_codes[a, jt].bitcast(FP8X4),
+                lhsT_scale=v_scales[4 * a : P, P * jt : P * (jt + 1)],
+                rhs=w_codes[name][:, lo:hi].bitcast(FP8X4),
+                rhs_scale=w_scales[name][:, lo:hi],
                 start=(a == 0),
                 stop=(a == 1),
             )
 
         squares = {}
 
-        def square(jt, f, bank):
-            if f == 0:
-                pair = held("squares%d" % jt, [P, 2 * BANK], F32, tag="sq%d" % (jt % 4))
-                squares[jt, 0] = pair[:, 0:BANK]
-                squares[jt, 1] = pair[:, BANK:]
-            source = banks[bank][:].rearrange("j (p i) -> j i p", i=4)
-            if jt in VECTOR_SQUARED:
-                plain = ring.tile([P, BANK], F32, name="plain")
-                nc.vector.tensor_copy(plain[:].rearrange("j (i p) -> j i p", i=4), source)
-                nc.vector.tensor_tensor(squares[jt, f], plain[:], plain[:], MULT)
-            else:
-                nc.scalar.activation(squares[jt, f].rearrange("j (i p) -> j i p", i=4), source, ACT.Square)
+        def square(jt, f, bank, lo=0, hi=H, at=0):
+            if (jt, f) not in squares:
+                squares[jt, f] = held(sb, "squares%d%s" % (jt, f), [P, BANK], F32, tag="sq%d%s" % (jt, f))
+            nc.scalar.activation(
+                squares[jt, f][:, 0:BANK].rearrange("j (i p) -> j i p", i=4)[:, :, lo // 4 : hi // 4],
+                banks[bank][:, at : at + hi - lo].rearrange("j (p i) -> j i p", i=4),
+                ACT.Square,
+            )
 
         def filters(jt, bank_a, bank_b):
-            for f, bank in ((0, bank_a), (1, bank_b)):
+            for f, bank in (("a", bank_a), ("b", bank_b)):
                 filter_pass(jt, f, 0, bank)
                 filter_pass(jt, f, 1, bank)
                 square(jt, f, bank)
@@ -181,131 +179,173 @@ def tile_list_bell_envelope_chart_kernel(
                 )
 
         def envelope(jt, bank, h_bf):
-            add_turned(eps_rows, bank, True, False)
-            add_turned(squares[jt, 0], bank, False, False)
-            add_turned(squares[jt, 1], bank, False, True)
+            terms = [eps_rows, squares[jt, "a"], squares[jt, "b"]]
+            if jt >= 2:
+                terms = terms[::-1]
+            for n, term in enumerate(terms):
+                add_turned(term, bank, n == 0, n == 2)
             nc.scalar.activation(
                 h_bf.rearrange("p (j i) -> p j i", i=4), banks[bank][:].rearrange("p (i j) -> p j i", i=4), ACT.Sqrt
             )
 
-        h_codes = held("h_codes", [P, S], U32)
-        h_scales = held("h_scales", [P, S], U8)
+        h_codes = {}
+        h_scales = {}
 
-        def quantise_h(lo, hi, h_bf):
-            nc.vector.quantize_mx(out=h_codes[:, lo:hi].bitcast(FP8X4), scales=h_scales[:, lo:hi], in_=h_bf)
+        def quantise_h(start, lo, hi, h_bf, width):
+            if start not in h_codes:
+                h_codes[start] = held(sb, "h_codes%d" % start, [P, width], U32)
+                h_scales[start] = held(sb, "h_scales%d" % start, [P, width], U8)
+            cols = slice(lo - start, hi - start)
+            nc.vector.quantize_mx(out=h_codes[start][:, cols].bitcast(FP8X4), scales=h_scales[start][:, cols], in_=h_bf)
 
         out_pages = out.rearrange("(b p i) t -> b i p t", b=2, i=4)
 
-        def features(page_list, lo, hi, bank, y, tag=None):
-            width = hi - lo
-            total = width * len(page_list)
-            for n, page in enumerate(page_list):
-                nc.tensor.matmul_mx(
-                    out=banks[bank][:, width * n : width * (n + 1)],
-                    lhsT=wc_codes[:, 2 * P * page : 2 * P * (page + 1)].bitcast(FP4X4),
-                    lhsT_scale=wc_planes[:, P * page : P * (page + 1)],
-                    rhs=h_codes[:, lo:hi].bitcast(FP8X4),
-                    rhs_scale=h_scales[:, lo:hi],
-                    start=True,
-                    stop=True,
-                )
+        def products(pieces, start, bank):
+            at = 0
+            for page, lo, hi in pieces:
+                for width in (512, 256, 128):
+                    if hi - lo >= width:
+                        nc.tensor.matmul_mx(
+                            out=banks[bank][:, at : at + width],
+                            lhsT=wc_codes[:, 2 * P * page : 2 * P * (page + 1)].bitcast(FP4X4),
+                            lhsT_scale=wc_planes[:, P * page : P * (page + 1)],
+                            rhs=h_codes[start][:, lo - start : lo - start + width].bitcast(FP8X4),
+                            rhs_scale=h_scales[start][:, lo - start : lo - start + width],
+                            start=True,
+                            stop=True,
+                        )
+                        lo = lo + width
+                        at = at + width
+            return at
+
+        def features(pieces, start, bank, y, tag=None):
+            total = products(pieces, start, bank)
             if tag is None:
                 size = ring.tile([P, BANK], F32, name="size")
             else:
-                size = held("size_" + tag, [P, BANK], F32, tag=tag)
+                size = held(sb, "size_" + tag, [P, BANK], F32, tag=tag)
             nc.scalar.activation(size[:, 0:total], banks[bank][:, 0:total], ACT.Abs)
             nc.scalar.activation(y, size[:, 0:total], ACT.Ln, bias=1.0)
 
-        def scatter(page_list, lo, hi, y):
-            width = hi - lo
-            for n, page in enumerate(page_list):
+        def scatter(pieces, y):
+            at = 0
+            for page, lo, hi in pieces:
                 nc.vector.tensor_tensor(
                     pages[page][:].indirect(place[:, lo // 16 : hi // 16]),
-                    y[:, width * n : width * (n + 1)],
+                    y[:, at : at + hi - lo],
                     wgo_sb[:, lo:hi],
                     MULT,
                 )
+                at = at + hi - lo
 
-        quantise_w(0, 0)
-        gather_words(0, 0, S)
-        quantise_w(0, 1)
-        wc_raw = held("wc_raw", [P, 2 * N], U8, tag="w_bf01")
-        nc.sync.dma_start(wc_raw[:].bitcast(I32), wc_words[0].bitcast(I32))
-        quantise_w(1, 0)
-        wgo_sb = held("wgo_sb", [P, S], F32, tag="w_bf10")
+        with tc.tile_pool(name="rounded", bufs=1) as rounded:
+            quantise_w(rounded, "a0", "a0", 0, H)
+            eps_rows = held(sb, "eps_rows", [P, BANK], F32, tag="raw_a0")
+            for i in range(4):
+                nc.tensor.transpose(
+                    banks[7][:, P * i : P * (i + 1)], eps_sb[:, i : i + 1].to_broadcast([P, P]), ident[:]
+                )
+            nc.scalar.copy(eps_rows[:], banks[7][:])
+            gather_words(third, 0, 0, S)
+            quantise_w(rounded, "a1", "a1", 0, H)
+        fourth = ctx.enter_context(tc.tile_pool(name="fourth", bufs=1))
+        wgo_sb = held(fourth, "wgo_sb", [P, S], F32)
         nc.sync.dma_start(wgo_sb[:], wgo)
-        quantise_w(1, 1)
-        wc_scale_raw = held("wc_scale_raw", [P, N], U8, tag="w3")
-        nc.vector.memset(wc_scale_raw[:].bitcast(I32), 0)
-        for d in range(4):
-            nc.sync.dma_start(
-                wc_scale_raw[32 * d : 32 * d + 4, :].bitcast(I32),
-                wc_scales[0, 4 * d : 4 * d + 4, :].bitcast(I32),
-            )
+        gather_words(fourth, 1, 0, HALF)
+        gather_words(fourth, 1, HALF, 2 * HALF)
+        quantise_w(fourth, "b0lo", "b0", 0, HALF)
+        first_squares = held(third, "first_squares", [P, 3 * BANK], F32, tag="raw_b0lo")
+        for jt in range(3):
+            squares[jt, "a"] = first_squares[:, BANK * jt : BANK * (jt + 1)]
+        for jt in range(3):
+            for a in range(2):
+                filter_pass(jt, "a", a, jt)
+            square(jt, "a", jt)
+        quantise_w(fourth, "b1lo", "b1", 0, HALF)
         for jt in range(2):
-            for f in range(2):
-                filter_pass(jt, f, 0, 2 * jt + f)
-        gather_words(1, 0, 256)
+            for a in range(2):
+                filter_pass(jt, "b", a, jt, 0, HALF)
+            square(jt, "b", jt, 0, HALF)
+        for a in range(2):
+            quantise_w(fourth, "b%dhi" % a, "b%d" % a, HALF, HALF)
+            for jt in range(2):
+                filter_pass(jt, "b", a, 4 + jt, HALF, H)
         for jt in range(2):
-            for f in range(2):
-                filter_pass(jt, f, 1, 2 * jt + f)
-                square(jt, f, 2 * jt + f)
-        gather_words(1, 256, 512)
-        gather_words(1, 512, S)
-        wc_codes = held("wc_codes", [P, 2 * N], U8, tag="tab1")
+            square(jt, "b", 4 + jt, HALF, H)
+        wc_codes = held(fourth, "wc_codes", [P, 2 * N], U8, tag="bf1")
         nc.vector.tensor_copy(
             wc_codes[:].bitcast(U16).rearrange("p (b i m) -> p b i m", b=2, i=4),
             wc_raw[:].bitcast(U16).rearrange("p (b m i) -> p b i m", b=2, i=4),
         )
-        wc_planes = held("wc_planes", [P, N], U8, tag="w_bf01")
+        wc_planes = held(third, "wc_planes", [P, N], U8, tag="wc_raw")
         nc.vector.tensor_copy(
             wc_planes[:].rearrange("p (b i m) -> p b i m", b=2, i=4),
             wc_scale_raw[:].rearrange("p (b m i) -> p b i m", b=2, i=4),
         )
-        h_first = [held("h_first0", [P, BANK], BF16), held("h_first1", [P, BANK], BF16, tag="page3")]
+        gather_words(third, 1, 2 * HALF, S, tag="wc_scale_raw")
+        h_first = [held(sb, "h_first0", [P, BANK], BF16, tag="page6"), held(sb, "h_first1", [P, BANK], BF16, tag="page4")]
         for jt in range(2):
-            envelope(jt, 4 + jt, h_first[jt][:])
-            quantise_h(P * jt, P * (jt + 1), h_first[jt][:])
-        log_warm = held("log_warm", [P, 1], F32, tag="sq3")
-        nc.scalar.activation(log_warm[:], h_first[1][:, 0:1], ACT.Ln)
-        clear_page(3, nc.gpsimd)
-        filters(2, 6, 7)
+            envelope(jt, 6 + jt, h_first[jt][:])
+            quantise_h(0, P * jt, P * (jt + 1), h_first[jt][:], 256)
+        log_warm = held(sb, "log_warm", [P, 1], F32, tag="page7")
+        nc.scalar.activation(log_warm[:], h_first[1][:, 0:1], ACT.Ln, bias=h_first[0][:, 0:1])
+        clear_page(4, nc.gpsimd)
 
-        groups = ([0], [1, 2], [3, 4], [5, 6])
-
-        y1 = held("y1", [P, 8 * 256], F32, tag="w0")
+        y1 = held(second, "y1", [P, 8 * 256], F32, tag="tab1")
+        products([(0, 0, P)], 0, 1)
+        negated = held(sb, "negated", [P, P], F32)
+        nc.vector.tensor_scalar(negated[:], banks[1][:, 0:P], -1.0, None, MULT)
+        size = held(sb, "size_first", [P, P], F32, tag="page5")
+        nc.vector.tensor_tensor(size[:], banks[1][:, 0:P], negated[:], MAX)
+        nc.scalar.activation(y1[:, 0:P], size[:], ACT.Ln, bias=1.0)
+        scatter([(0, 0, P)], y1[:, 0:P])
+        for page in (5, 6, 7):
+            clear_page(page, nc.gpsimd)
+        groups = (
+            [(0, P, 256), (1, 0, 256)],
+            [(2, 0, 256), (3, 0, 256)],
+            [(4, 0, 256), (5, 0, 256)],
+            [(6, 0, 256)],
+        )
+        at = P
         for n, group in enumerate(groups):
-            y = y1[:, 256 * group[0] : 256 * (group[-1] + 1)]
-            features(group, 0, 256, 2 + n, y, tag="page%d" % (4 + n))
-            clear_page(4 + n, nc.gpsimd)
-            scatter(group, 0, 256, y)
-        filters(3, 0, 1)
-        filters(4, 6, 7)
-        h_second = held("h_second", [P, 2 * BANK], BF16)
-        for jt in (2, 3):
-            envelope(jt, 2 + jt, h_second[:, BANK * (jt - 2) : BANK * (jt - 1)])
-        quantise_h(256, 512, h_second[:])
-        features([7], 0, 256, 4, y1[:, 256 * 7 :])
-        scatter([7], 0, 256, y1[:, 256 * 7 :])
-        filters(5, 2, 3)
+            total = sum(hi - lo for page, lo, hi in group)
+            features(group, 0, 0, y1[:, at : at + total], tag=("late_squares", None, None, "h_second")[n])
+            scatter(group, y1[:, at : at + total])
+            at = at + total
+        late = ((2, "b", 7), (3, "a", 6), (3, "b", 4), (4, "a", 5), (4, "b", 2))
+        late_squares = held(sb, "late_squares", [P, len(late) * BANK], F32)
+        for n, (jt, f, bank) in enumerate(late):
+            squares[jt, f] = late_squares[:, BANK * n : BANK * (n + 1)]
+            for a in range(2):
+                filter_pass(jt, f, a, bank)
+            square(jt, f, bank)
+        h_second = held(sb, "h_second", [P, 3 * BANK], BF16)
+        for jt, bank in ((2, 3), (3, 1), (4, 4)):
+            envelope(jt, bank, h_second[:, BANK * (jt - 2) : BANK * (jt - 1)])
+        quantise_h(256, 256, 512, h_second[:, 0 : 2 * BANK], 384)
+        quantise_h(256, 512, 640, h_second[:, 2 * BANK :], 384)
+        features([(7, 0, 256)], 0, 4, y1[:, 256 * 7 :], tag="sq5a")
+        scatter([(7, 0, 256)], y1[:, 256 * 7 :])
 
-        y2 = held("y2", [P, 8 * 256], F32, tag="w1")
-        for n, group in enumerate(groups):
-            y = y2[:, 256 * group[0] : 256 * (group[-1] + 1)]
-            features(group, 256, 512, (6 + n) % 8, y)
-            scatter(group, 256, 512, y)
-        filters(6, 2, 3)
-        filters(7, 4, 5)
-        h_third = held("h_third", [P, 4 * BANK], BF16)
-        for jt in range(4, 8):
-            envelope(jt, (2 + jt) % 8, h_third[:, BANK * (jt - 4) : BANK * (jt - 3)])
-        quantise_h(512, S, h_third[:])
-        features([7], 256, 512, 0, y2[:, 256 * 7 :])
-        scatter([7], 256, 512, y2[:, 256 * 7 :])
+        y2 = [held(second, "y2a", [P, 4 * 384], F32, tag="raw_a1"), held(second, "y2b", [P, 4 * 384], F32, tag="tab0")]
+        for page in range(7):
+            y = y2[page // 4][:, 384 * (page % 4) : 384 * (page % 4 + 1)]
+            features([(page, 256, 640)], 256, 4, y, tag={0: "sq5b", 6: "h_third"}.get(page))
+            scatter([(page, 256, 640)], y)
+        for jt in (5, 6, 7):
+            filters(jt, 6, 7)
+        h_third = held(sb, "h_third", [P, 3 * BANK], BF16)
+        for jt in (5, 6, 7):
+            envelope(jt, jt - 4, h_third[:, BANK * (jt - 5) : BANK * (jt - 4)])
+        quantise_h(640, 640, 896, h_third[:, 0 : 2 * BANK], 384)
+        quantise_h(640, 896, S, h_third[:, 2 * BANK :], 384)
+        features([(7, 256, 640)], 256, 3, y2[1][:, 384 * 3 :])
+        scatter([(7, 256, 640)], y2[1][:, 384 * 3 :])
 
-        y3 = [held("y3%d" % b, [P, 4 * 512], F32, tag="w%d" % (2 + b)) for b in range(2)]
+        y3 = [held(second, "y3a", [P, 4 * 384], F32, tag="tab1"), held(second, "y3b", [P, 4 * 384], F32, tag="raw_a1")]
         for page in range(8):
-            y = y3[page // 4][:, 512 * (page % 4) : 512 * (page % 4 + 1)]
-            features([page], 512, S, (2, 3, 4, 5, 6, 7, 1, 0)[page], y)
-            scatter([page], 512, S, y)
+            y = y3[page // 4][:, 384 * (page % 4) : 384 * (page % 4 + 1)]
+            features([(page, 640, S)], 640, 3, y)
+            scatter([(page, 640, S)], y)
             nc.sync.dma_start(out_pages[page // 4, page % 4], pages[page][:])

@@ -21,7 +21,7 @@ MAX = mybir.AluOpType.max
 P = 128
 BANK = 512
 HALF = 256
-SCALAR_CAST_COLUMNS = {"a0": 512, "a1": 512, "b0lo": 256, "b1lo": 0, "b0hi": 0, "b1hi": 0}
+SCALAR_CAST_COLUMNS = {"a0": 512, "a1lo": 256, "a1hi": 256, "b0lo": 256, "b1lo": 0, "b0hi": 0, "b1hi": 0}
 
 
 def tile_list_bell_envelope_chart_kernel(
@@ -74,8 +74,8 @@ def tile_list_bell_envelope_chart_kernel(
         load_tab(second, 0)
         eps_sb = held(second, "eps_sb", [P, 4], F32)
         nc.sync.dma_start(eps_sb[:], eps.rearrange("(p i) -> p i", i=4))
-        load_w(second, "a1", 1, 0, H)
         load_tab(second, 1)
+        load_w(second, "a1lo", 1, 0, HALF)
 
         pages = {}
 
@@ -100,6 +100,7 @@ def tile_list_bell_envelope_chart_kernel(
                     v_scales[4 * a + 2 + e : P : 32, :].bitcast(I32),
                     v_scales[16 + 4 * a + e : P : 32, :].bitcast(I32),
                 )
+        load_w(third, "a1hi", 1, HALF, H)
         for half, lo in (("lo", H), ("hi", H + HALF)):
             for a in range(2):
                 load_w(third, "b%d%s" % (a, half), a, lo, lo + HALF)
@@ -117,8 +118,8 @@ def tile_list_bell_envelope_chart_kernel(
         w_codes = {name: held(third, "codes_" + name, [P, H], U32) for name in ("a0", "b0", "a1", "b1")}
         w_scales = {name: held(sb, "scales_" + name, [P, H], U8) for name in ("a0", "b0", "a1", "b1")}
 
-        def quantise_w(pool, name, target, first_col, width):
-            grouped = held(pool, "bf_" + name, [P, width, 4], BF16, tag="bf" + name[1])
+        def round_w(name, grouped):
+            width = grouped.shape[1]
             split = SCALAR_CAST_COLUMNS[name]
             for lo, hi, copy in ((0, split, nc.scalar.copy), (split, width, nc.vector.tensor_copy)):
                 if hi > lo:
@@ -126,12 +127,19 @@ def tile_list_bell_envelope_chart_kernel(
                         grouped[:, lo:hi, :].rearrange("p (c u) i -> p c i u", u=4),
                         w_raw[name][:, :, lo:hi].rearrange("p i (c u) -> p c i u", u=4),
                     )
-            cols = slice(first_col, first_col + width)
+
+        def pack_w(grouped, target, first_col):
+            cols = slice(first_col, first_col + grouped.shape[1])
             nc.vector.quantize_mx(
                 out=w_codes[target][:, cols].bitcast(FP8X4),
                 scales=w_scales[target][:, cols],
-                in_=grouped[:].rearrange("p c i -> p (c i)"),
+                in_=grouped.rearrange("p c i -> p (c i)"),
             )
+
+        def quantise_w(pool, name, target, first_col, width):
+            grouped = held(pool, "bf_" + name, [P, width, 4], BF16, tag="bf" + name[1])
+            round_w(name, grouped[:])
+            pack_w(grouped[:], target, first_col)
 
         v_codes = {}
 
@@ -141,7 +149,7 @@ def tile_list_bell_envelope_chart_kernel(
             for jt in range(lo // P, hi // P):
                 v_codes[a, jt] = words[:, P * jt - lo : P * (jt + 1) - lo]
 
-        def filter_pass(jt, f, a, bank, lo=0, hi=H, at=0):
+        def filter_pass(jt, f, a, bank, lo=0, hi=H, at=0, first=None, last=None):
             name = f + str(a)
             nc.tensor.matmul_mx(
                 out=banks[bank][:, at : at + hi - lo],
@@ -149,8 +157,8 @@ def tile_list_bell_envelope_chart_kernel(
                 lhsT_scale=v_scales[4 * a : P, P * jt : P * (jt + 1)],
                 rhs=w_codes[name][:, lo:hi].bitcast(FP8X4),
                 rhs_scale=w_scales[name][:, lo:hi],
-                start=(a == 0),
-                stop=(a == 1),
+                start=(a == 0) if first is None else first,
+                stop=(a == 1) if last is None else last,
             )
 
         squares = {}
@@ -247,25 +255,31 @@ def tile_list_bell_envelope_chart_kernel(
                 )
             nc.scalar.copy(eps_rows[:], banks[7][:])
             gather_words(third, 0, 0, S)
-            quantise_w(rounded, "a1", "a1", 0, H)
+            gather_words(third, 1, 0, S)
+            grouped = held(rounded, "bf_a1", [P, H, 4], BF16, tag="bf1")
+            round_w("a1lo", grouped[:, 0:HALF, :])
+            round_w("a1hi", grouped[:, HALF:H, :])
+            pack_w(grouped[:], "a1", 0)
         fourth = ctx.enter_context(tc.tile_pool(name="fourth", bufs=1))
         wgo_sb = held(fourth, "wgo_sb", [P, S], F32)
         nc.sync.dma_start(wgo_sb[:], wgo)
-        gather_words(fourth, 1, 0, HALF)
-        gather_words(fourth, 1, HALF, 2 * HALF)
-        quantise_w(fourth, "b0lo", "b0", 0, HALF)
-        first_squares = held(third, "first_squares", [P, 3 * BANK], F32, tag="raw_b0lo")
-        for jt in range(3):
+        quantise_w(third, "b0lo", "b0", 0, HALF)
+        first_squares = held(third, "first_squares", [P, 4 * BANK], F32, tag="raw_b0lo")
+        for jt in range(4):
             squares[jt, "a"] = first_squares[:, BANK * jt : BANK * (jt + 1)]
         for jt in range(3):
             for a in range(2):
                 filter_pass(jt, "a", a, jt)
             square(jt, "a", jt)
         quantise_w(fourth, "b1lo", "b1", 0, HALF)
+        for a in range(2):
+            for jt in range(2):
+                filter_pass(jt, "b", a, 3, 0, HALF, at=HALF * jt, first=(a, jt) == (0, 0), last=(a, jt) == (1, 1))
         for jt in range(2):
-            for a in range(2):
-                filter_pass(jt, "b", a, jt, 0, HALF)
-            square(jt, "b", jt, 0, HALF)
+            square(jt, "b", 3, 0, HALF, at=HALF * jt)
+        for a in range(2):
+            filter_pass(3, "a", a, 0)
+        square(3, "a", 0)
         for a in range(2):
             quantise_w(fourth, "b%dhi" % a, "b%d" % a, HALF, HALF)
             for jt in range(2):
@@ -282,7 +296,6 @@ def tile_list_bell_envelope_chart_kernel(
             wc_planes[:].rearrange("p (b i m) -> p b i m", b=2, i=4),
             wc_scale_raw[:].rearrange("p (b m i) -> p b i m", b=2, i=4),
         )
-        gather_words(third, 1, 2 * HALF, S, tag="wc_scale_raw")
         h_first = [held(sb, "h_first0", [P, BANK], BF16, tag="page6"), held(sb, "h_first1", [P, BANK], BF16, tag="page4")]
         for jt in range(2):
             envelope(jt, 6 + jt, h_first[jt][:])
@@ -313,7 +326,7 @@ def tile_list_bell_envelope_chart_kernel(
             features(group, 0, 0, y1[:, at : at + total], tag=("late_squares", None, None, "h_second")[n])
             scatter(group, y1[:, at : at + total])
             at = at + total
-        late = ((2, "b", 7), (3, "a", 6), (3, "b", 4), (4, "a", 5), (4, "b", 2))
+        late = ((2, "b", 7), (3, "b", 6), (4, "a", 5), (4, "b", 4))
         late_squares = held(sb, "late_squares", [P, len(late) * BANK], F32)
         for n, (jt, f, bank) in enumerate(late):
             squares[jt, f] = late_squares[:, BANK * n : BANK * (n + 1)]
@@ -321,29 +334,29 @@ def tile_list_bell_envelope_chart_kernel(
                 filter_pass(jt, f, a, bank)
             square(jt, f, bank)
         h_second = held(sb, "h_second", [P, 3 * BANK], BF16)
-        for jt, bank in ((2, 3), (3, 1), (4, 4)):
+        for jt, bank in ((2, 3), (3, 1), (4, 2)):
             envelope(jt, bank, h_second[:, BANK * (jt - 2) : BANK * (jt - 1)])
         quantise_h(256, 256, 512, h_second[:, 0 : 2 * BANK], 384)
         quantise_h(256, 512, 640, h_second[:, 2 * BANK :], 384)
-        features([(7, 0, 256)], 0, 4, y1[:, 256 * 7 :], tag="sq5a")
+        features([(7, 0, 256)], 0, 2, y1[:, 256 * 7 :], tag="sq5a")
         scatter([(7, 0, 256)], y1[:, 256 * 7 :])
 
-        y2 = [held(second, "y2a", [P, 4 * 384], F32, tag="raw_a1"), held(second, "y2b", [P, 4 * 384], F32, tag="tab0")]
+        y2 = [held(sb, "y2a", [P, 4 * 384], F32, tag="y_other"), held(second, "y2b", [P, 4 * 384], F32, tag="tab0")]
         for page in range(7):
             y = y2[page // 4][:, 384 * (page % 4) : 384 * (page % 4 + 1)]
-            features([(page, 256, 640)], 256, 4, y, tag={0: "sq5b", 6: "h_third"}.get(page))
+            features([(page, 256, 640)], 256, 2, y, tag={0: "sq5b", 6: "h_third"}.get(page))
             scatter([(page, 256, 640)], y)
         for jt in (5, 6, 7):
             filters(jt, 6, 7)
         h_third = held(sb, "h_third", [P, 3 * BANK], BF16)
         for jt in (5, 6, 7):
-            envelope(jt, jt - 4, h_third[:, BANK * (jt - 5) : BANK * (jt - 4)])
+            envelope(jt, (1, 4, 3)[jt - 5], h_third[:, BANK * (jt - 5) : BANK * (jt - 4)])
         quantise_h(640, 640, 896, h_third[:, 0 : 2 * BANK], 384)
         quantise_h(640, 896, S, h_third[:, 2 * BANK :], 384)
         features([(7, 256, 640)], 256, 3, y2[1][:, 384 * 3 :])
         scatter([(7, 256, 640)], y2[1][:, 384 * 3 :])
 
-        y3 = [held(second, "y3a", [P, 4 * 384], F32, tag="tab1"), held(second, "y3b", [P, 4 * 384], F32, tag="raw_a1")]
+        y3 = [held(second, "y3a", [P, 4 * 384], F32, tag="tab1"), held(sb, "y3b", [P, 4 * 384], F32, tag="y_other")]
         for page in range(8):
             y = y3[page // 4][:, 384 * (page % 4) : 384 * (page % 4 + 1)]
             features([(page, 640, S)], 640, 3, y)

@@ -189,7 +189,7 @@ def tile_list_bell_envelope_chart_kernel(
         def envelope(jt, bank, h_bf):
             terms = [eps_rows, squares[jt, "a"], squares[jt, "b"]]
             if jt >= 2:
-                terms = terms[::-1]
+                terms = [squares[jt, "b"], eps_rows, squares[jt, "a"]]
             for n, term in enumerate(terms):
                 add_turned(term, bank, n == 0, n == 2)
             nc.scalar.activation(
@@ -315,16 +315,20 @@ def tile_list_bell_envelope_chart_kernel(
         for page in (5, 6, 7):
             clear_page(page, nc.gpsimd)
         groups = (
-            [(0, P, 256), (1, 0, 256)],
+            [(1, 0, 256), (0, P, 256)],
             [(2, 0, 256), (3, 0, 256)],
             [(4, 0, 256), (5, 0, 256)],
-            [(6, 0, 256)],
+            [(6, 0, 256), (7, 0, P)],
         )
         at = P
         for n, group in enumerate(groups):
             total = sum(hi - lo for page, lo, hi in group)
+            if n == 3:
+                products([(7, P, 256)], 0, 0)
+                size_last = held(sb, "size_last", [P, P], F32)
+                nc.scalar.activation(size_last[:], banks[0][:, 0:P], ACT.Abs)
             features(group, 0, 0, y1[:, at : at + total], tag=("late_squares", None, None, "h_second")[n])
-            scatter(group, y1[:, at : at + total])
+            scatter(group if n < 3 else [(6, 0, P)], y1[:, at : at + total])
             at = at + total
         late = ((2, "b", 7), (3, "b", 6), (4, "a", 5), (4, "b", 4))
         late_squares = held(sb, "late_squares", [P, len(late) * BANK], F32)
@@ -338,13 +342,17 @@ def tile_list_bell_envelope_chart_kernel(
             envelope(jt, bank, h_second[:, BANK * (jt - 2) : BANK * (jt - 1)])
         quantise_h(256, 256, 512, h_second[:, 0 : 2 * BANK], 384)
         quantise_h(256, 512, 640, h_second[:, 2 * BANK :], 384)
-        features([(7, 0, 256)], 0, 2, y1[:, 256 * 7 :], tag="sq5a")
-        scatter([(7, 0, 256)], y1[:, 256 * 7 :])
+        last = held(sb, "last", [P, 256 + P], F32, tag="late_squares")
+        nc.scalar.copy(last[:, 0:256], wgo_sb[:, 0:256])
+        nc.scalar.activation(last[:, 256:], size_last[:], ACT.Ln, bias=1.0)
+        nc.vector.tensor_tensor(pages[7][:].indirect(place[:, 0:8]), y1[:, 256 * 7 : 256 * 7 + P], last[:, 0:P], MULT)
+        nc.vector.tensor_tensor(pages[6][:].indirect(place[:, 8:16]), y1[:, 256 * 6 + P : 256 * 7], last[:, P:256], MULT)
+        nc.vector.tensor_tensor(pages[7][:].indirect(place[:, 8:16]), last[:, 256:], wgo_sb[:, P:256], MULT)
 
         y2 = [held(sb, "y2a", [P, 4 * 384], F32, tag="y_other"), held(second, "y2b", [P, 4 * 384], F32, tag="tab0")]
         for page in range(7):
             y = y2[page // 4][:, 384 * (page % 4) : 384 * (page % 4 + 1)]
-            features([(page, 256, 640)], 256, 2, y, tag={0: "sq5b", 6: "h_third"}.get(page))
+            features([(page, 256, 640)], 256, 2, y, tag={0: "sq5a", 1: "sq5b", 6: "h_third"}.get(page))
             scatter([(page, 256, 640)], y)
         for jt in (5, 6, 7):
             filters(jt, 6, 7)

@@ -64,9 +64,9 @@ def tile_list_bell_envelope_chart_kernel(
             tab[a] = held(pool, "tab%d" % a, [P, T], I32)
             nc.sync.dma_start(tab[a][:], tab_words[a].rearrange("p t i -> p (t i)").bitcast(I32))
 
+        load_w(sb, "a0", 0, 0, H)
         nc.sync.dma_start(pick[:], offs)
         nc.sync.dma_start(place[:], offs2)
-        load_w(sb, "a0", 0, 0, H)
         for a in range(2):
             rows = tab_scales[a].bitcast(I32).rearrange("(g e) t -> e g t", e=2)
             for e in range(2):
@@ -85,8 +85,7 @@ def tile_list_bell_envelope_chart_kernel(
 
         clear_page(0, nc.vector)
         clear_page(1, nc.vector)
-        clear_page(2, nc.gpsimd)
-        clear_page(3, nc.gpsimd)
+        clear_page(2, nc.vector)
 
         v_scales = held(sb, "v_scales", [P, S], U8)
         with tc.tile_pool(name="picked", bufs=1) as picked_pool:
@@ -255,7 +254,7 @@ def tile_list_bell_envelope_chart_kernel(
                 )
             nc.scalar.copy(eps_rows[:], banks[7][:])
             gather_words(third, 0, 0, S)
-            gather_words(third, 1, 0, S)
+            gather_words(third, 1, 0, 2 * HALF)
             grouped = held(rounded, "bf_a1", [P, H, 4], BF16, tag="bf1")
             round_w("a1lo", grouped[:, 0:HALF, :])
             round_w("a1hi", grouped[:, HALF:H, :])
@@ -296,24 +295,26 @@ def tile_list_bell_envelope_chart_kernel(
             wc_planes[:].rearrange("p (b i m) -> p b i m", b=2, i=4),
             wc_scale_raw[:].rearrange("p (b m i) -> p b i m", b=2, i=4),
         )
-        h_first = [held(sb, "h_first0", [P, BANK], BF16, tag="page6"), held(sb, "h_first1", [P, BANK], BF16, tag="page4")]
+        gather_words(third, 1, 2 * HALF, 3 * HALF, tag="wc_scale_raw")
+        h_first = [held(sb, "h_first0", [P, BANK], BF16, tag="page4"), held(sb, "h_first1", [P, BANK], BF16, tag="page3")]
         for jt in range(2):
             envelope(jt, 6 + jt, h_first[jt][:])
             quantise_h(0, P * jt, P * (jt + 1), h_first[jt][:], 256)
-        log_warm = held(sb, "log_warm", [P, 1], F32, tag="page7")
+        log_warm = held(sb, "log_warm", [P, 1], F32, tag="page5")
         nc.scalar.activation(log_warm[:], h_first[1][:, 0:1], ACT.Ln, bias=h_first[0][:, 0:1])
-        clear_page(4, nc.gpsimd)
+        for page in (3, 4, 5):
+            clear_page(page, nc.gpsimd)
 
-        y1 = held(second, "y1", [P, 8 * 256], F32, tag="tab1")
+        y1 = held(second, "y1", [P, 8 * 256], F32, tag="tab0")
         products([(0, 0, P)], 0, 1)
         negated = held(sb, "negated", [P, P], F32)
         nc.vector.tensor_scalar(negated[:], banks[1][:, 0:P], -1.0, None, MULT)
-        size = held(sb, "size_first", [P, P], F32, tag="page5")
+        size = held(sb, "size_first", [P, P], F32, tag="page6")
         nc.vector.tensor_tensor(size[:], banks[1][:, 0:P], negated[:], MAX)
+        gather_words(sb, 1, 3 * HALF, S, tag="negated")
         nc.scalar.activation(y1[:, 0:P], size[:], ACT.Ln, bias=1.0)
         scatter([(0, 0, P)], y1[:, 0:P])
-        for page in (5, 6, 7):
-            clear_page(page, nc.gpsimd)
+        clear_page(6, nc.gpsimd)
         groups = (
             [(1, 0, 256), (0, P, 256)],
             [(2, 0, 256), (3, 0, 256)],
@@ -327,7 +328,9 @@ def tile_list_bell_envelope_chart_kernel(
                 products([(7, P, 256)], 0, 0)
                 size_last = held(sb, "size_last", [P, P], F32)
                 nc.scalar.activation(size_last[:], banks[0][:, 0:P], ACT.Abs)
-            features(group, 0, 0, y1[:, at : at + total], tag=("late_squares", None, None, "h_second")[n])
+            features(group, 0, 0, y1[:, at : at + total], tag=("late_squares", "page7", None, "h_second")[n])
+            if n == 1:
+                clear_page(7, nc.gpsimd)
             scatter(group if n < 3 else [(6, 0, P)], y1[:, at : at + total])
             at = at + total
         late = ((2, "b", 7), (3, "b", 6), (4, "a", 5), (4, "b", 4))
@@ -349,7 +352,7 @@ def tile_list_bell_envelope_chart_kernel(
         nc.vector.tensor_tensor(pages[6][:].indirect(place[:, 8:16]), y1[:, 256 * 6 + P : 256 * 7], last[:, P:256], MULT)
         nc.vector.tensor_tensor(pages[7][:].indirect(place[:, 8:16]), last[:, 256:], wgo_sb[:, P:256], MULT)
 
-        y2 = [held(sb, "y2a", [P, 4 * 384], F32, tag="y_other"), held(second, "y2b", [P, 4 * 384], F32, tag="tab0")]
+        y2 = [held(sb, "y2a", [P, 4 * 384], F32, tag="y_other"), held(second, "y2b", [P, 4 * 384], F32, tag="tab1")]
         for page in range(7):
             y = y2[page // 4][:, 384 * (page % 4) : 384 * (page % 4 + 1)]
             features([(page, 256, 640)], 256, 2, y, tag={0: "sq5a", 1: "sq5b", 6: "h_third"}.get(page))
@@ -364,7 +367,7 @@ def tile_list_bell_envelope_chart_kernel(
         features([(7, 256, 640)], 256, 3, y2[1][:, 384 * 3 :])
         scatter([(7, 256, 640)], y2[1][:, 384 * 3 :])
 
-        y3 = [held(second, "y3a", [P, 4 * 384], F32, tag="tab1"), held(sb, "y3b", [P, 4 * 384], F32, tag="y_other")]
+        y3 = [held(second, "y3a", [P, 4 * 384], F32, tag="tab0"), held(sb, "y3b", [P, 4 * 384], F32, tag="y_other")]
         for page in range(8):
             y = y3[page // 4][:, 384 * (page % 4) : 384 * (page % 4 + 1)]
             features([(page, 640, S)], 640, 3, y)

@@ -20,8 +20,14 @@ MAX = mybir.AluOpType.max
 
 P = 128
 BANK = 512
-HALF = 256
-SCALAR_CAST_COLUMNS = {"a0": 512, "a1lo": 256, "a1hi": 256, "b0lo": 256, "b1lo": 0, "b0hi": 0, "b1hi": 0}
+HALF = H // 2
+PAGES = 8
+
+PHASE1, PHASE2, PHASE3 = (0, 256), (256, 640), (640, S)
+WIDTH1 = PHASE1[1] - PHASE1[0]
+WIDTH23 = PHASE2[1] - PHASE2[0]
+
+EARLY_PAGES = 3
 
 
 def tile_list_bell_envelope_chart_kernel(
@@ -42,23 +48,25 @@ def tile_list_bell_envelope_chart_kernel(
         place = lists.tile([P, S // 16], U16, name="place")
 
         scale_window = held(sb, "scale_window", [P, T], U8)
-        warm_out = held(sb, "warm_out", [P, 1], F32)
         nc.gpsimd.memset(scale_window[:].bitcast(I32), 0)
+        one = held(sb, "one", [P, 1], F32)
         with tc.tile_pool(name="first", bufs=1) as first:
-            warm = first.tile([P, 1], F32, name="warm")
-            nc.vector.memset(warm[:], 1.0)
-            nc.scalar.activation(warm_out[:, 0:1], warm[:], ACT.Sqrt)
+            one_made = first.tile([P, 1], F32, name="one_made")
+            nc.vector.memset(one_made[:], 1.0)
+            nc.vector.tensor_copy(one[:], one_made[:])
         second = ctx.enter_context(tc.tile_pool(name="second", bufs=1))
+        root_warm = held(sb, "root_warm", [P, 1], F32)
+        nc.scalar.activation(root_warm[:], one[:], ACT.Sqrt)
         ident = held(sb, "ident", [P, P], F32)
         make_identity(nc, ident[:])
 
         w_raw = {}
         tab = {}
 
-        def load_w(pool, name, a, lo, hi):
-            w_raw[name] = held(pool, "raw_" + name, [P, 4, hi - lo], F32)
+        def load_w(pool, piece, a, lo, hi):
+            w_raw[piece] = held(pool, "raw_" + piece, [P, 4, hi - lo], F32)
             rows = wab[512 * a : 512 * (a + 1), lo:hi].rearrange("(p i) c -> p i c", i=4)
-            nc.sync.dma_start(w_raw[name][:], rows)
+            nc.sync.dma_start(w_raw[piece][:], rows)
 
         def load_tab(pool, a):
             tab[a] = held(pool, "tab%d" % a, [P, T], I32)
@@ -79,13 +87,12 @@ def tile_list_bell_envelope_chart_kernel(
 
         pages = {}
 
-        def clear_page(page, engine, tag=None):
-            pages[page] = held(sb, "page%d" % page, [P, T2], F32, tag=tag)
+        def clear_page(pool, page, engine):
+            pages[page] = held(pool, "page%d" % page, [P, T2], F32)
             engine.memset(pages[page][:], 0.0)
 
-        clear_page(0, nc.vector)
-        clear_page(1, nc.vector)
-        clear_page(2, nc.vector)
+        for page in range(EARLY_PAGES):
+            clear_page(sb, page, nc.vector)
 
         v_scales = held(sb, "v_scales", [P, S], U8)
         with tc.tile_pool(name="picked", bufs=1) as picked_pool:
@@ -113,111 +120,106 @@ def tile_list_bell_envelope_chart_kernel(
                 wc_scales[0, 4 * d : 4 * d + 4, :].bitcast(I32),
             )
 
-
         w_codes = {name: held(third, "codes_" + name, [P, H], U32) for name in ("a0", "b0", "a1", "b1")}
         w_scales = {name: held(sb, "scales_" + name, [P, H], U8) for name in ("a0", "b0", "a1", "b1")}
 
-        def round_w(name, grouped):
-            width = grouped.shape[1]
-            split = SCALAR_CAST_COLUMNS[name]
-            for lo, hi, copy in ((0, split, nc.scalar.copy), (split, width, nc.vector.tensor_copy)):
-                if hi > lo:
-                    copy(
-                        grouped[:, lo:hi, :].rearrange("p (c u) i -> p c i u", u=4),
-                        w_raw[name][:, :, lo:hi].rearrange("p i (c u) -> p c i u", u=4),
-                    )
+        def round_w(piece, grouped, copy):
+            copy(
+                grouped.rearrange("p (c u) i -> p c i u", u=4),
+                w_raw[piece][:].rearrange("p i (c u) -> p c i u", u=4),
+            )
 
-        def pack_w(grouped, target, first_col):
+        def pack_w(grouped, name, first_col):
             cols = slice(first_col, first_col + grouped.shape[1])
             nc.vector.quantize_mx(
-                out=w_codes[target][:, cols].bitcast(FP8X4),
-                scales=w_scales[target][:, cols],
+                out=w_codes[name][:, cols].bitcast(FP8X4),
+                scales=w_scales[name][:, cols],
                 in_=grouped.rearrange("p c i -> p (c i)"),
             )
 
-        def quantise_w(pool, name, target, first_col, width):
-            grouped = held(pool, "bf_" + name, [P, width, 4], BF16, tag="bf" + name[1])
-            round_w(name, grouped[:])
-            pack_w(grouped[:], target, first_col)
+        def quantise_w(pool, piece, first_col, width, copy):
+            grouped = held(pool, "bf_" + piece, [P, width, 4], BF16, tag="bf" + piece[1])
+            round_w(piece, grouped[:], copy)
+            pack_w(grouped[:], piece[0:2], first_col)
 
         v_codes = {}
 
         def gather_words(pool, a, lo, hi, tag=None):
             words = held(pool, "v_codes%d_%d" % (a, lo), [P, hi - lo], U32, tag=tag)
             nc.vector.tensor_copy(words[:], tab[a][:].bitcast(U32).indirect(pick[:, lo // 16 : hi // 16]))
-            for jt in range(lo // P, hi // P):
-                v_codes[a, jt] = words[:, P * jt - lo : P * (jt + 1) - lo]
+            for strip in range(lo // P, hi // P):
+                v_codes[a, strip] = words[:, P * strip - lo : P * (strip + 1) - lo]
 
-        def filter_pass(jt, f, a, bank, lo=0, hi=H, at=0, first=None, last=None):
+        def filter_pass(strip, f, a, bank, start, stop, lo=0, hi=H, at=0):
             name = f + str(a)
             nc.tensor.matmul_mx(
                 out=banks[bank][:, at : at + hi - lo],
-                lhsT=v_codes[a, jt].bitcast(FP8X4),
-                lhsT_scale=v_scales[4 * a : P, P * jt : P * (jt + 1)],
+                lhsT=v_codes[a, strip].bitcast(FP8X4),
+                lhsT_scale=v_scales[4 * a : P, P * strip : P * (strip + 1)],
                 rhs=w_codes[name][:, lo:hi].bitcast(FP8X4),
                 rhs_scale=w_scales[name][:, lo:hi],
-                start=(a == 0) if first is None else first,
-                stop=(a == 1) if last is None else last,
+                start=start,
+                stop=stop,
             )
 
         squares = {}
 
-        def square(jt, f, bank, lo=0, hi=H, at=0):
-            if (jt, f) not in squares:
-                squares[jt, f] = held(sb, "squares%d%s" % (jt, f), [P, BANK], F32, tag="sq%d%s" % (jt, f))
+        def square(strip, f, bank, lo=0, hi=H, at=0):
+            if (strip, f) not in squares:
+                squares[strip, f] = held(sb, "sq%d%s" % (strip, f), [P, BANK], F32)
             nc.scalar.activation(
-                squares[jt, f][:, 0:BANK].rearrange("j (i p) -> j i p", i=4)[:, :, lo // 4 : hi // 4],
+                squares[strip, f][:, 0:BANK].rearrange("j (i p) -> j i p", i=4)[:, :, lo // 4 : hi // 4],
                 banks[bank][:, at : at + hi - lo].rearrange("j (p i) -> j i p", i=4),
                 ACT.Square,
             )
 
-        def filters(jt, bank_a, bank_b):
-            for f, bank in (("a", bank_a), ("b", bank_b)):
-                filter_pass(jt, f, 0, bank)
-                filter_pass(jt, f, 1, bank)
-                square(jt, f, bank)
+        def filter_squared(strip, f, bank):
+            for a in range(2):
+                filter_pass(strip, f, a, bank, a == 0, a == 1)
+            square(strip, f, bank)
 
-        def add_turned(source, bank, first, last):
-            for i in range(4):
-                cols = slice(P * i, P * (i + 1))
-                nc.tensor.matmul(
-                    banks[bank][:, cols], source[:, cols], ident[:], is_transpose=True,
-                    start=(first and i == 0), stop=(last and i == 3),
-                )
-
-        def envelope(jt, bank, h_bf):
-            terms = [eps_rows, squares[jt, "a"], squares[jt, "b"]]
-            if jt >= 2:
-                terms = [squares[jt, "b"], eps_rows, squares[jt, "a"]]
+        def envelope(bank, terms, h_bf):
             for n, term in enumerate(terms):
-                add_turned(term, bank, n == 0, n == 2)
+                for i in range(4):
+                    cols = slice(P * i, P * (i + 1))
+                    nc.tensor.matmul(
+                        banks[bank][:, cols], term[:, cols], ident[:], is_transpose=True,
+                        start=(n == 0 and i == 0), stop=(n == 2 and i == 3),
+                    )
             nc.scalar.activation(
                 h_bf.rearrange("p (j i) -> p j i", i=4), banks[bank][:].rearrange("p (i j) -> p j i", i=4), ACT.Sqrt
             )
 
+        def later_envelope(strip, bank, h_bf):
+            envelope(bank, [squares[strip, "b"], eps_rows, squares[strip, "a"]], h_bf)
+
         h_codes = {}
         h_scales = {}
 
-        def quantise_h(start, lo, hi, h_bf, width):
-            if start not in h_codes:
-                h_codes[start] = held(sb, "h_codes%d" % start, [P, width], U32)
-                h_scales[start] = held(sb, "h_scales%d" % start, [P, width], U8)
-            cols = slice(lo - start, hi - start)
-            nc.vector.quantize_mx(out=h_codes[start][:, cols].bitcast(FP8X4), scales=h_scales[start][:, cols], in_=h_bf)
+        def quantise_h(phase, lo, hi, h_bf):
+            if phase not in h_codes:
+                h_codes[phase] = held(sb, "h_codes%d" % phase[0], [P, phase[1] - phase[0]], U32)
+                h_scales[phase] = held(sb, "h_scales%d" % phase[0], [P, phase[1] - phase[0]], U8)
+            cols = slice(lo - phase[0], hi - phase[0])
+            nc.vector.quantize_mx(out=h_codes[phase][:, cols].bitcast(FP8X4), scales=h_scales[phase][:, cols], in_=h_bf)
 
-        out_pages = out.rearrange("(b p i) t -> b i p t", b=2, i=4)
+        def quantise_three_strips(phase, h_bf):
+            cut = phase[0] + 2 * P
+            quantise_h(phase, phase[0], cut, h_bf[:, 0 : 2 * BANK])
+            quantise_h(phase, cut, phase[1], h_bf[:, 2 * BANK :])
 
-        def products(pieces, start, bank):
+        def products(parts, phase, bank):
             at = 0
-            for page, lo, hi in pieces:
-                for width in (512, 256, 128):
+            for page, lo, hi in parts:
+                for width in (2 * P, P):
                     if hi - lo >= width:
+                        cols = slice(lo - phase[0], lo - phase[0] + width)
                         nc.tensor.matmul_mx(
                             out=banks[bank][:, at : at + width],
                             lhsT=wc_codes[:, 2 * P * page : 2 * P * (page + 1)].bitcast(FP4X4),
                             lhsT_scale=wc_planes[:, P * page : P * (page + 1)],
-                            rhs=h_codes[start][:, lo - start : lo - start + width].bitcast(FP8X4),
-                            rhs_scale=h_scales[start][:, lo - start : lo - start + width],
+                            rhs=h_codes[phase][:, cols].bitcast(FP8X4),
+                            rhs_scale=h_scales[phase][:, cols],
                             start=True,
                             stop=True,
                         )
@@ -225,28 +227,29 @@ def tile_list_bell_envelope_chart_kernel(
                         at = at + width
             return at
 
-        def features(pieces, start, bank, y, tag=None):
-            total = products(pieces, start, bank)
+        def log1p(y, size):
+            nc.scalar.activation(y, size, ACT.Ln, bias=one[:])
+
+        def features(parts, phase, bank, y, tag=None):
+            total = products(parts, phase, bank)
             if tag is None:
                 size = ring.tile([P, BANK], F32, name="size")
             else:
                 size = held(sb, "size_" + tag, [P, BANK], F32, tag=tag)
             nc.scalar.activation(size[:, 0:total], banks[bank][:, 0:total], ACT.Abs)
-            nc.scalar.activation(y, size[:, 0:total], ACT.Ln, bias=1.0)
+            log1p(y, size[:, 0:total])
 
-        def scatter(pieces, y):
+        def scatter_part(page, lo, hi, y, weights):
+            nc.vector.tensor_tensor(pages[page][:].indirect(place[:, lo // 16 : hi // 16]), y, weights, MULT)
+
+        def scatter(parts, y):
             at = 0
-            for page, lo, hi in pieces:
-                nc.vector.tensor_tensor(
-                    pages[page][:].indirect(place[:, lo // 16 : hi // 16]),
-                    y[:, at : at + hi - lo],
-                    wgo_sb[:, lo:hi],
-                    MULT,
-                )
+            for page, lo, hi in parts:
+                scatter_part(page, lo, hi, y[:, at : at + hi - lo], wgo_sb[:, lo:hi])
                 at = at + hi - lo
 
         with tc.tile_pool(name="rounded", bufs=1) as rounded:
-            quantise_w(rounded, "a0", "a0", 0, H)
+            quantise_w(rounded, "a0", 0, H, nc.scalar.copy)
             eps_rows = held(sb, "eps_rows", [P, BANK], F32, tag="raw_a0")
             for i in range(4):
                 nc.tensor.transpose(
@@ -254,37 +257,35 @@ def tile_list_bell_envelope_chart_kernel(
                 )
             nc.scalar.copy(eps_rows[:], banks[7][:])
             gather_words(third, 0, 0, S)
-            gather_words(third, 1, 0, 2 * HALF)
-            grouped = held(rounded, "bf_a1", [P, H, 4], BF16, tag="bf1")
-            round_w("a1lo", grouped[:, 0:HALF, :])
-            round_w("a1hi", grouped[:, HALF:H, :])
-            pack_w(grouped[:], "a1", 0)
+            gather_words(third, 1, 0, 4 * P)
+            grouped_a1 = held(rounded, "bf_a1", [P, H, 4], BF16, tag="bf1")
+            round_w("a1lo", grouped_a1[:, 0:HALF, :], nc.scalar.copy)
+            round_w("a1hi", grouped_a1[:, HALF:H, :], nc.scalar.copy)
+            pack_w(grouped_a1[:], "a1", 0)
         fourth = ctx.enter_context(tc.tile_pool(name="fourth", bufs=1))
         wgo_sb = held(fourth, "wgo_sb", [P, S], F32)
         nc.sync.dma_start(wgo_sb[:], wgo)
-        quantise_w(third, "b0lo", "b0", 0, HALF)
-        first_squares = held(third, "first_squares", [P, 4 * BANK], F32, tag="raw_b0lo")
-        for jt in range(4):
-            squares[jt, "a"] = first_squares[:, BANK * jt : BANK * (jt + 1)]
-        for jt in range(3):
-            for a in range(2):
-                filter_pass(jt, "a", a, jt)
-            square(jt, "a", jt)
-        quantise_w(fourth, "b1lo", "b1", 0, HALF)
+
+        quantise_w(third, "b0lo", 0, HALF, nc.scalar.copy)
+        early_squares = held(third, "early_squares", [P, 4 * BANK], F32, tag="raw_b0lo")
+        for strip in range(4):
+            squares[strip, "a"] = early_squares[:, BANK * strip : BANK * (strip + 1)]
+        for strip in range(3):
+            filter_squared(strip, "a", strip)
+        quantise_w(fourth, "b1lo", 0, HALF, nc.vector.tensor_copy)
         for a in range(2):
-            for jt in range(2):
-                filter_pass(jt, "b", a, 3, 0, HALF, at=HALF * jt, first=(a, jt) == (0, 0), last=(a, jt) == (1, 1))
-        for jt in range(2):
-            square(jt, "b", 3, 0, HALF, at=HALF * jt)
+            for strip in range(2):
+                filter_pass(strip, "b", a, 3, (a, strip) == (0, 0), (a, strip) == (1, 1), 0, HALF, HALF * strip)
+        for strip in range(2):
+            square(strip, "b", 3, 0, HALF, HALF * strip)
+        filter_squared(3, "a", 0)
         for a in range(2):
-            filter_pass(3, "a", a, 0)
-        square(3, "a", 0)
-        for a in range(2):
-            quantise_w(fourth, "b%dhi" % a, "b%d" % a, HALF, HALF)
-            for jt in range(2):
-                filter_pass(jt, "b", a, 4 + jt, HALF, H)
-        for jt in range(2):
-            square(jt, "b", 4 + jt, HALF, H)
+            quantise_w(fourth, "b%dhi" % a, HALF, HALF, nc.vector.tensor_copy)
+            for strip in range(2):
+                filter_pass(strip, "b", a, 4 + strip, a == 0, a == 1, HALF, H)
+        for strip in range(2):
+            square(strip, "b", 4 + strip, HALF, H)
+
         wc_codes = held(fourth, "wc_codes", [P, 2 * N], U8, tag="bf1")
         nc.vector.tensor_copy(
             wc_codes[:].bitcast(U16).rearrange("p (b i m) -> p b i m", b=2, i=4),
@@ -295,81 +296,90 @@ def tile_list_bell_envelope_chart_kernel(
             wc_planes[:].rearrange("p (b i m) -> p b i m", b=2, i=4),
             wc_scale_raw[:].rearrange("p (b m i) -> p b i m", b=2, i=4),
         )
-        gather_words(third, 1, 2 * HALF, 3 * HALF, tag="wc_scale_raw")
-        h_first = [held(sb, "h_first0", [P, BANK], BF16, tag="page4"), held(sb, "h_first1", [P, BANK], BF16, tag="page3")]
-        for jt in range(2):
-            envelope(jt, 6 + jt, h_first[jt][:])
-            quantise_h(0, P * jt, P * (jt + 1), h_first[jt][:], 256)
-        log_warm = held(sb, "log_warm", [P, 1], F32, tag="page5")
-        nc.scalar.activation(log_warm[:], h_first[1][:, 0:1], ACT.Ln, bias=h_first[0][:, 0:1])
-        for page in (3, 4, 5):
-            clear_page(page, nc.gpsimd)
+        gather_words(third, 1, 4 * P, 6 * P, tag="wc_scale_raw")
 
-        y1 = held(second, "y1", [P, 8 * 256], F32, tag="tab0")
-        products([(0, 0, P)], 0, 1)
+        log_warm = held(sb, "log_warm", [P, 1], F32)
+        with tc.tile_pool(name="first_roots", bufs=1) as first_roots:
+            for strip in range(2):
+                h_strip = held(first_roots, "h_strip%d" % strip, [P, BANK], BF16)
+                envelope(6 + strip, [eps_rows, squares[strip, "a"], squares[strip, "b"]], h_strip[:])
+                quantise_h(PHASE1, P * strip, P * (strip + 1), h_strip[:])
+            nc.scalar.activation(log_warm[:], h_strip[:, 0:1], ACT.Ln)
+        late_pages = ctx.enter_context(tc.tile_pool(name="late_pages", bufs=1))
+        for page in range(EARLY_PAGES, PAGES):
+            clear_page(late_pages, page, nc.gpsimd)
+
+        y1 = held(second, "y1", [P, PAGES * WIDTH1], F32, tag="tab0")
+        products([(0, 0, P)], PHASE1, 1)
         negated = held(sb, "negated", [P, P], F32)
         nc.vector.tensor_scalar(negated[:], banks[1][:, 0:P], -1.0, None, MULT)
-        size = held(sb, "size_first", [P, P], F32, tag="page6")
-        nc.vector.tensor_tensor(size[:], banks[1][:, 0:P], negated[:], MAX)
-        gather_words(sb, 1, 3 * HALF, S, tag="negated")
-        nc.scalar.activation(y1[:, 0:P], size[:], ACT.Ln, bias=1.0)
+        size_first = held(sb, "size_first", [P, P], F32)
+        nc.vector.tensor_tensor(size_first[:], banks[1][:, 0:P], negated[:], MAX)
+        gather_words(sb, 1, 6 * P, S, tag="negated")
+        log1p(y1[:, 0:P], size_first[:])
         scatter([(0, 0, P)], y1[:, 0:P])
-        clear_page(6, nc.gpsimd)
-        groups = (
-            [(1, 0, 256), (0, P, 256)],
-            [(2, 0, 256), (3, 0, 256)],
-            [(4, 0, 256), (5, 0, 256)],
-            [(6, 0, 256), (7, 0, P)],
-        )
+
         at = P
-        for n, group in enumerate(groups):
+        for group, tag in (
+            ([(1, 0, WIDTH1), (0, P, WIDTH1)], "late_squares"),
+            ([(2, 0, WIDTH1), (3, 0, WIDTH1)], None),
+            ([(4, 0, WIDTH1), (5, 0, WIDTH1)], None),
+        ):
             total = sum(hi - lo for page, lo, hi in group)
-            if n == 3:
-                products([(7, P, 256)], 0, 0)
-                size_last = held(sb, "size_last", [P, P], F32)
-                nc.scalar.activation(size_last[:], banks[0][:, 0:P], ACT.Abs)
-            features(group, 0, 0, y1[:, at : at + total], tag=("late_squares", "page7", None, "h_second")[n])
-            if n == 1:
-                clear_page(7, nc.gpsimd)
-            scatter(group if n < 3 else [(6, 0, P)], y1[:, at : at + total])
+            features(group, PHASE1, 0, y1[:, at : at + total], tag)
+            scatter(group, y1[:, at : at + total])
             at = at + total
+        products([(7, P, WIDTH1)], PHASE1, 0)
+        size_last = held(sb, "size_last", [P, P], F32)
+        nc.scalar.activation(size_last[:], banks[0][:, 0:P], ACT.Abs)
+        y_page6 = y1[:, at : at + WIDTH1]
+        y_page7 = y1[:, at + WIDTH1 : at + WIDTH1 + P]
+        features([(6, 0, WIDTH1), (7, 0, P)], PHASE1, 0, y1[:, at : at + WIDTH1 + P], "h_phase2")
+        scatter([(6, 0, P)], y_page6)
+
         late = ((2, "b", 7), (3, "b", 6), (4, "a", 5), (4, "b", 4))
         late_squares = held(sb, "late_squares", [P, len(late) * BANK], F32)
-        for n, (jt, f, bank) in enumerate(late):
-            squares[jt, f] = late_squares[:, BANK * n : BANK * (n + 1)]
-            for a in range(2):
-                filter_pass(jt, f, a, bank)
-            square(jt, f, bank)
-        h_second = held(sb, "h_second", [P, 3 * BANK], BF16)
-        for jt, bank in ((2, 3), (3, 1), (4, 2)):
-            envelope(jt, bank, h_second[:, BANK * (jt - 2) : BANK * (jt - 1)])
-        quantise_h(256, 256, 512, h_second[:, 0 : 2 * BANK], 384)
-        quantise_h(256, 512, 640, h_second[:, 2 * BANK :], 384)
-        last = held(sb, "last", [P, 256 + P], F32, tag="late_squares")
-        nc.scalar.copy(last[:, 0:256], wgo_sb[:, 0:256])
-        nc.scalar.activation(last[:, 256:], size_last[:], ACT.Ln, bias=1.0)
-        nc.vector.tensor_tensor(pages[7][:].indirect(place[:, 0:8]), y1[:, 256 * 7 : 256 * 7 + P], last[:, 0:P], MULT)
-        nc.vector.tensor_tensor(pages[6][:].indirect(place[:, 8:16]), y1[:, 256 * 6 + P : 256 * 7], last[:, P:256], MULT)
-        nc.vector.tensor_tensor(pages[7][:].indirect(place[:, 8:16]), last[:, 256:], wgo_sb[:, P:256], MULT)
+        for n, (strip, f, bank) in enumerate(late):
+            squares[strip, f] = late_squares[:, BANK * n : BANK * (n + 1)]
+            filter_squared(strip, f, bank)
+        h_phase2 = held(sb, "h_phase2", [P, 3 * BANK], BF16)
+        for strip, bank in ((2, 3), (3, 1), (4, 2)):
+            later_envelope(strip, bank, h_phase2[:, BANK * (strip - 2) : BANK * (strip - 1)])
+        quantise_three_strips(PHASE2, h_phase2)
+        kept = held(sb, "kept", [P, WIDTH1 + P], F32, tag="late_squares")
+        nc.scalar.copy(kept[:, 0:WIDTH1], wgo_sb[:, 0:WIDTH1])
+        log1p(kept[:, WIDTH1:], size_last[:])
+        scatter_part(7, 0, P, y_page7, kept[:, 0:P])
+        scatter_part(6, P, WIDTH1, y_page6[:, P:WIDTH1], kept[:, P:WIDTH1])
+        scatter_part(7, P, WIDTH1, kept[:, WIDTH1:], wgo_sb[:, P:WIDTH1])
 
-        y2 = [held(sb, "y2a", [P, 4 * 384], F32, tag="y_other"), held(second, "y2b", [P, 4 * 384], F32, tag="tab1")]
-        for page in range(7):
-            y = y2[page // 4][:, 384 * (page % 4) : 384 * (page % 4 + 1)]
-            features([(page, 256, 640)], 256, 2, y, tag={0: "sq5a", 1: "sq5b", 6: "h_third"}.get(page))
-            scatter([(page, 256, 640)], y)
-        for jt in (5, 6, 7):
-            filters(jt, 6, 7)
-        h_third = held(sb, "h_third", [P, 3 * BANK], BF16)
-        for jt in (5, 6, 7):
-            envelope(jt, (1, 4, 3)[jt - 5], h_third[:, BANK * (jt - 5) : BANK * (jt - 4)])
-        quantise_h(640, 640, 896, h_third[:, 0 : 2 * BANK], 384)
-        quantise_h(640, 896, S, h_third[:, 2 * BANK :], 384)
-        features([(7, 256, 640)], 256, 3, y2[1][:, 384 * 3 :])
-        scatter([(7, 256, 640)], y2[1][:, 384 * 3 :])
+        def page_columns(y_tiles, page):
+            return y_tiles[page // 4][:, WIDTH23 * (page % 4) : WIDTH23 * (page % 4 + 1)]
 
-        y3 = [held(second, "y3a", [P, 4 * 384], F32, tag="tab0"), held(sb, "y3b", [P, 4 * 384], F32, tag="y_other")]
-        for page in range(8):
-            y = y3[page // 4][:, 384 * (page % 4) : 384 * (page % 4 + 1)]
-            features([(page, 640, S)], 640, 3, y)
-            scatter([(page, 640, S)], y)
+        y2 = [
+            held(sb, "y2a", [P, 4 * WIDTH23], F32, tag="y_spare"),
+            held(second, "y2b", [P, 4 * WIDTH23], F32, tag="tab1"),
+        ]
+        waits_for_log = {0: "sq5a", 1: "sq5b", 6: "h_phase3"}
+        for page in range(PAGES - 1):
+            features([(page, *PHASE2)], PHASE2, 2, page_columns(y2, page), waits_for_log.get(page))
+            scatter([(page, *PHASE2)], page_columns(y2, page))
+        for strip in (5, 6, 7):
+            filter_squared(strip, "a", 6)
+            filter_squared(strip, "b", 7)
+        h_phase3 = held(sb, "h_phase3", [P, 3 * BANK], BF16)
+        for strip, bank in ((5, 1), (6, 4), (7, 3)):
+            later_envelope(strip, bank, h_phase3[:, BANK * (strip - 5) : BANK * (strip - 4)])
+        quantise_three_strips(PHASE3, h_phase3)
+        features([(PAGES - 1, *PHASE2)], PHASE2, 3, page_columns(y2, PAGES - 1))
+        scatter([(PAGES - 1, *PHASE2)], page_columns(y2, PAGES - 1))
+
+        out_pages = out.rearrange("(b p i) t -> b i p t", b=2, i=4)
+        y3 = [
+            held(second, "y3a", [P, 4 * WIDTH23], F32, tag="tab0"),
+            held(sb, "y3b", [P, 4 * WIDTH23], F32, tag="y_spare"),
+        ]
+        for page in range(PAGES):
+            features([(page, *PHASE3)], PHASE3, 3, page_columns(y3, page))
+            scatter([(page, *PHASE3)], page_columns(y3, page))
             nc.sync.dma_start(out_pages[page // 4, page % 4], pages[page][:])

@@ -28,6 +28,10 @@ WIDTH1 = PHASE1[1] - PHASE1[0]
 WIDTH23 = PHASE2[1] - PHASE2[0]
 
 EARLY_PAGES = 3
+FIRST_PARTS = 2
+
+B0_VECTOR = 64
+A1_VECTOR = 224
 
 
 def tile_list_bell_envelope_chart_kernel(
@@ -48,12 +52,12 @@ def tile_list_bell_envelope_chart_kernel(
         place = lists.tile([P, S // 16], U16, name="place")
 
         scale_window = held(sb, "scale_window", [P, T], U8)
-        nc.gpsimd.memset(scale_window[:].bitcast(I32), 0)
         one = held(sb, "one", [P, 1], F32)
         with tc.tile_pool(name="first", bufs=1) as first:
             one_made = first.tile([P, 1], F32, name="one_made")
-            nc.vector.memset(one_made[:], 1.0)
-            nc.vector.tensor_copy(one[:], one_made[:])
+            nc.gpsimd.memset(one_made[:], 1.0)
+            nc.gpsimd.memset(scale_window[:].bitcast(I32), 0)
+            nc.gpsimd.tensor_copy(one[:], one_made[:])
         second = ctx.enter_context(tc.tile_pool(name="second", bufs=1))
         root_warm = held(sb, "root_warm", [P, 1], F32)
         nc.scalar.activation(root_warm[:], one[:], ACT.Sqrt)
@@ -72,18 +76,18 @@ def tile_list_bell_envelope_chart_kernel(
             tab[a] = held(pool, "tab%d" % a, [P, T], I32)
             nc.sync.dma_start(tab[a][:], tab_words[a].rearrange("p t i -> p (t i)").bitcast(I32))
 
-        load_w(sb, "a0", 0, 0, H)
+        load_w(sb, "a0lo", 0, 0, HALF)
         nc.sync.dma_start(pick[:], offs)
         nc.sync.dma_start(place[:], offs2)
-        for a in range(2):
-            rows = tab_scales[a].bitcast(I32).rearrange("(g e) t -> e g t", e=2)
-            for e in range(2):
-                nc.sync.dma_start(scale_window[4 * a + e : P : 16, :].bitcast(I32), rows[e])
+        rows = tab_scales.bitcast(I32).rearrange("a (g e) t -> e g a t", e=2)
+        for e in range(2):
+            nc.sync.dma_start(scale_window[e:P:8, :].bitcast(I32), rows[e])
+        load_w(second, "a0hi", 0, HALF, H)
         load_tab(second, 0)
         eps_sb = held(second, "eps_sb", [P, 4], F32)
         nc.sync.dma_start(eps_sb[:], eps.rearrange("(p i) -> p i", i=4))
-        load_tab(second, 1)
-        load_w(second, "a1lo", 1, 0, HALF)
+        load_w(second, "b0", 0, H, 2 * H)
+        load_w(second, "a1", 1, 0, H)
 
         pages = {}
 
@@ -92,7 +96,7 @@ def tile_list_bell_envelope_chart_kernel(
             engine.memset(pages[page][:], 0.0)
 
         for page in range(EARLY_PAGES):
-            clear_page(sb, page, nc.vector)
+            clear_page(second, page, nc.vector)
 
         v_scales = held(sb, "v_scales", [P, S], U8)
         with tc.tile_pool(name="picked", bufs=1) as picked_pool:
@@ -103,13 +107,13 @@ def tile_list_bell_envelope_chart_kernel(
         for a in range(2):
             for e in range(2):
                 nc.sync.dma_start(
-                    v_scales[4 * a + 2 + e : P : 32, :].bitcast(I32),
-                    v_scales[16 + 4 * a + e : P : 32, :].bitcast(I32),
+                    v_scales[8 * a + 2 + e : P : 32, :].bitcast(I32),
+                    v_scales[16 + 8 * a + e : P : 32, :].bitcast(I32),
                 )
-        load_w(third, "a1hi", 1, HALF, H)
-        for half, lo in (("lo", H), ("hi", H + HALF)):
-            for a in range(2):
-                load_w(third, "b%d%s" % (a, half), a, lo, lo + HALF)
+        load_tab(third, 1)
+        load_w(third, "b1lo", 1, H, H + HALF)
+        for n in range(2):
+            load_w(third, "b1hi%d" % n, 1, H + HALF + P * n, H + HALF + P * (n + 1))
         wc_raw = held(third, "wc_raw", [P, 2 * N], U8)
         nc.sync.dma_start(wc_raw[:].bitcast(I32), wc_words[0].bitcast(I32))
         wc_scale_raw = held(third, "wc_scale_raw", [P, N], U8)
@@ -123,10 +127,10 @@ def tile_list_bell_envelope_chart_kernel(
         w_codes = {name: held(third, "codes_" + name, [P, H], U32) for name in ("a0", "b0", "a1", "b1")}
         w_scales = {name: held(sb, "scales_" + name, [P, H], U8) for name in ("a0", "b0", "a1", "b1")}
 
-        def round_w(piece, grouped, copy):
+        def round_w(raw, grouped, copy):
             copy(
                 grouped.rearrange("p (c u) i -> p c i u", u=4),
-                w_raw[piece][:].rearrange("p i (c u) -> p c i u", u=4),
+                raw.rearrange("p i (c u) -> p c i u", u=4),
             )
 
         def pack_w(grouped, name, first_col):
@@ -139,23 +143,28 @@ def tile_list_bell_envelope_chart_kernel(
 
         def quantise_w(pool, piece, first_col, width, copy):
             grouped = held(pool, "bf_" + piece, [P, width, 4], BF16, tag="bf" + piece[1])
-            round_w(piece, grouped[:], copy)
+            round_w(w_raw[piece][:], grouped[:], copy)
             pack_w(grouped[:], piece[0:2], first_col)
 
         v_codes = {}
 
-        def gather_words(pool, a, lo, hi, tag=None):
-            words = held(pool, "v_codes%d_%d" % (a, lo), [P, hi - lo], U32, tag=tag)
-            nc.vector.tensor_copy(words[:], tab[a][:].bitcast(U32).indirect(pick[:, lo // 16 : hi // 16]))
-            for strip in range(lo // P, hi // P):
-                v_codes[a, strip] = words[:, P * strip - lo : P * (strip + 1) - lo]
+        def gather_words(pool, parts, tag=None):
+            total = sum(hi - lo for a, lo, hi in parts)
+            words = held(pool, "v_codes%d_%d" % parts[0][0:2], [P, total], U32, tag=tag)
+            at = 0
+            for a, lo, hi in parts:
+                window = tab[a][:].bitcast(U32)
+                nc.vector.tensor_copy(words[:, at : at + hi - lo], window.indirect(pick[:, lo // 16 : hi // 16]))
+                for strip in range(lo // P, hi // P):
+                    v_codes[a, strip] = words[:, at + P * strip - lo : at + P * (strip + 1) - lo]
+                at = at + hi - lo
 
         def filter_pass(strip, f, a, bank, start, stop, lo=0, hi=H, at=0):
             name = f + str(a)
             nc.tensor.matmul_mx(
                 out=banks[bank][:, at : at + hi - lo],
                 lhsT=v_codes[a, strip].bitcast(FP8X4),
-                lhsT_scale=v_scales[4 * a : P, P * strip : P * (strip + 1)],
+                lhsT_scale=v_scales[8 * a : P, P * strip : P * (strip + 1)],
                 rhs=w_codes[name][:, lo:hi].bitcast(FP8X4),
                 rhs_scale=w_scales[name][:, lo:hi],
                 start=start,
@@ -178,20 +187,24 @@ def tile_list_bell_envelope_chart_kernel(
                 filter_pass(strip, f, a, bank, a == 0, a == 1)
             square(strip, f, bank)
 
-        def envelope(bank, terms, h_bf):
-            for n, term in enumerate(terms):
-                for i in range(4):
-                    cols = slice(P * i, P * (i + 1))
-                    nc.tensor.matmul(
-                        banks[bank][:, cols], term[:, cols], ident[:], is_transpose=True,
-                        start=(n == 0 and i == 0), stop=(n == 2 and i == 3),
-                    )
+        def add_term(bank, term, start=False, stop=False, identity=ident):
+            for i in range(4):
+                cols = slice(P * i, P * (i + 1))
+                nc.tensor.matmul(
+                    banks[bank][:, cols], term[:, cols], identity[:], is_transpose=True,
+                    start=(start and i == 0), stop=(stop and i == 3),
+                )
+
+        def root(bank, h_bf):
             nc.scalar.activation(
                 h_bf.rearrange("p (j i) -> p j i", i=4), banks[bank][:].rearrange("p (i j) -> p j i", i=4), ACT.Sqrt
             )
 
-        def later_envelope(strip, bank, h_bf):
-            envelope(bank, [squares[strip, "b"], eps_rows, squares[strip, "a"]], h_bf)
+        def later_envelope(strip, bank, h_bf, first, last):
+            add_term(bank, squares[strip, first], start=True)
+            add_term(bank, eps_rows)
+            add_term(bank, squares[strip, last], stop=True)
+            root(bank, h_bf)
 
         h_codes = {}
         h_scales = {}
@@ -209,33 +222,35 @@ def tile_list_bell_envelope_chart_kernel(
             quantise_h(phase, cut, phase[1], h_bf[:, 2 * BANK :])
 
         def products(parts, phase, bank):
+            passes = []
             at = 0
             for page, lo, hi in parts:
                 for width in (2 * P, P):
                     if hi - lo >= width:
-                        cols = slice(lo - phase[0], lo - phase[0] + width)
-                        nc.tensor.matmul_mx(
-                            out=banks[bank][:, at : at + width],
-                            lhsT=wc_codes[:, 2 * P * page : 2 * P * (page + 1)].bitcast(FP4X4),
-                            lhsT_scale=wc_planes[:, P * page : P * (page + 1)],
-                            rhs=h_codes[phase][:, cols].bitcast(FP8X4),
-                            rhs_scale=h_scales[phase][:, cols],
-                            start=True,
-                            stop=True,
-                        )
+                        passes.append((page, lo - phase[0], width, at))
                         lo = lo + width
                         at = at + width
+            for page, first, width, column in reversed(passes):
+                nc.tensor.matmul_mx(
+                    out=banks[bank][:, column : column + width],
+                    lhsT=wc_codes[:, 2 * P * page : 2 * P * (page + 1)].bitcast(FP4X4),
+                    lhsT_scale=wc_planes[:, P * page : P * (page + 1)],
+                    rhs=h_codes[phase][:, first : first + width].bitcast(FP8X4),
+                    rhs_scale=h_scales[phase][:, first : first + width],
+                    start=True,
+                    stop=True,
+                )
             return at
 
         def log1p(y, size):
             nc.scalar.activation(y, size, ACT.Ln, bias=one[:])
 
-        def features(parts, phase, bank, y, tag=None):
+        def features(parts, phase, bank, y, tag=None, pool=sb):
             total = products(parts, phase, bank)
             if tag is None:
                 size = ring.tile([P, BANK], F32, name="size")
             else:
-                size = held(sb, "size_" + tag, [P, BANK], F32, tag=tag)
+                size = held(pool, "size_" + tag, [P, BANK], F32, tag=tag)
             nc.scalar.activation(size[:, 0:total], banks[bank][:, 0:total], ACT.Abs)
             log1p(y, size[:, 0:total])
 
@@ -248,43 +263,67 @@ def tile_list_bell_envelope_chart_kernel(
                 scatter_part(page, lo, hi, y[:, at : at + hi - lo], wgo_sb[:, lo:hi])
                 at = at + hi - lo
 
+        gather_words(third, [(0, 0, S)])
         with tc.tile_pool(name="rounded", bufs=1) as rounded:
-            quantise_w(rounded, "a0", 0, H, nc.scalar.copy)
-            eps_rows = held(sb, "eps_rows", [P, BANK], F32, tag="raw_a0")
-            for i in range(4):
-                nc.tensor.transpose(
-                    banks[7][:, P * i : P * (i + 1)], eps_sb[:, i : i + 1].to_broadcast([P, P]), ident[:]
-                )
-            nc.scalar.copy(eps_rows[:], banks[7][:])
-            gather_words(third, 0, 0, S)
-            gather_words(third, 1, 0, 4 * P)
-            grouped_a1 = held(rounded, "bf_a1", [P, H, 4], BF16, tag="bf1")
-            round_w("a1lo", grouped_a1[:, 0:HALF, :], nc.scalar.copy)
-            round_w("a1hi", grouped_a1[:, HALF:H, :], nc.scalar.copy)
-            pack_w(grouped_a1[:], "a1", 0)
+            grouped = {name: held(rounded, "bf_" + name, [P, H, 4], BF16) for name in ("a0", "b0", "a1")}
+            round_w(w_raw["a0lo"][:], grouped["a0"][:, 0:HALF, :], nc.scalar.copy)
+            round_w(w_raw["a0hi"][:], grouped["a0"][:, HALF:, :], nc.scalar.copy)
+            pack_w(grouped["a0"][:], "a0", 0)
+            round_w(w_raw["b0"][:, :, 0:B0_VECTOR], grouped["b0"][:, 0:B0_VECTOR, :], nc.vector.tensor_copy)
+            round_w(w_raw["b0"][:, :, B0_VECTOR:], grouped["b0"][:, B0_VECTOR:, :], nc.scalar.copy)
+            pack_w(grouped["b0"][:], "b0", 0)
+            round_w(w_raw["a1"][:, :, 0:A1_VECTOR], grouped["a1"][:, 0:A1_VECTOR, :], nc.vector.tensor_copy)
+            round_w(w_raw["a1"][:, :, A1_VECTOR:], grouped["a1"][:, A1_VECTOR:, :], nc.scalar.copy)
+            pack_w(grouped["a1"][:], "a1", 0)
         fourth = ctx.enter_context(tc.tile_pool(name="fourth", bufs=1))
         wgo_sb = held(fourth, "wgo_sb", [P, S], F32)
         nc.sync.dma_start(wgo_sb[:], wgo)
-
-        quantise_w(third, "b0lo", 0, HALF, nc.scalar.copy)
-        early_squares = held(third, "early_squares", [P, 4 * BANK], F32, tag="raw_b0lo")
-        for strip in range(4):
-            squares[strip, "a"] = early_squares[:, BANK * strip : BANK * (strip + 1)]
+        eps_rows = held(second, "eps_rows", [P, BANK], F32, tag="raw_a0hi")
+        for i in range(4):
+            nc.tensor.transpose(banks[7][:, P * i : P * (i + 1)], eps_sb[:, i : i + 1].to_broadcast([P, P]), ident[:])
+        nc.scalar.copy(eps_rows[:], banks[7][:])
+        for strip in range(2):
+            add_term(6 + strip, eps_rows, start=True)
         for strip in range(3):
-            filter_squared(strip, "a", strip)
+            filter_pass(strip, "a", 0, strip, True, False)
+        filter_pass(0, "b", 0, 3, True, False, 0, HALF)
+        filter_pass(0, "b", 0, 4, True, False, HALF, H)
+        filter_pass(1, "b", 0, 5, True, False)
+        for half in range(2):
+            filter_pass(3, "a", 0, 3 + half, False, False, HALF * half, HALF * (half + 1), HALF)
+        gather_words(third, [(1, 0, 2 * P)])
+        gather_words(third, [(1, 2 * P, 4 * P)])
+        early_squares = held(second, "early_squares", [P, 2 * BANK], F32, tag="raw_b0")
+        for strip in range(2):
+            squares[strip, "a"] = early_squares[:, BANK * strip : BANK * (strip + 1)]
+        for strip in range(2):
+            filter_pass(strip, "a", 1, strip, False, True)
+            square(strip, "a", strip)
+        filter_pass(2, "a", 1, 2, False, True)
+        for half in range(2):
+            filter_pass(3, "a", 1, 3 + half, False, False, HALF * half, HALF * (half + 1), HALF)
+        add_term(6, squares[0, "a"])
+
         quantise_w(fourth, "b1lo", 0, HALF, nc.vector.tensor_copy)
-        for a in range(2):
-            for strip in range(2):
-                filter_pass(strip, "b", a, 3, (a, strip) == (0, 0), (a, strip) == (1, 1), 0, HALF, HALF * strip)
-        for strip in range(2):
-            square(strip, "b", 3, 0, HALF, HALF * strip)
-        filter_squared(3, "a", 0)
-        for a in range(2):
-            quantise_w(fourth, "b%dhi" % a, HALF, HALF, nc.vector.tensor_copy)
-            for strip in range(2):
-                filter_pass(strip, "b", a, 4 + strip, a == 0, a == 1, HALF, H)
-        for strip in range(2):
-            square(strip, "b", 4 + strip, HALF, H)
+        filter_pass(0, "b", 1, 3, False, True, 0, HALF)
+        filter_pass(1, "b", 1, 5, False, False, 0, HALF)
+        square(0, "b", 3, 0, HALF)
+        square(2, "a", 2)
+        grouped_hi = [held(fourth, "bf_b1hi0", [P, P, 4], BF16), held(fourth, "bf_b1hi1", [P, P, 4], BF16, tag="bf1")]
+        for n in range(2):
+            round_w(w_raw["b1hi%d" % n][:], grouped_hi[n][:], nc.vector.tensor_copy)
+        for n in range(2):
+            pack_w(grouped_hi[n][:], "b1", HALF + P * n)
+        filter_pass(0, "b", 1, 4, False, True, HALF, H)
+        filter_pass(1, "b", 1, 5, False, True, HALF, H, HALF)
+        late_ident = held(fourth, "late_ident", [P, P], F32, tag="bf_b1hi0")
+        nc.vector.tensor_copy(late_ident[:], ident[:])
+        add_term(7, squares[1, "a"], identity=late_ident)
+        square(0, "b", 4, HALF, H)
+        square(1, "b", 5)
+        squares[3, "a"] = held(third, "sq3a", [P, BANK], F32, tag="v_codes1_0")
+        for half in range(2):
+            square(3, "a", 3 + half, HALF * half, HALF * (half + 1), HALF)
 
         wc_codes = held(fourth, "wc_codes", [P, 2 * N], U8, tag="bf1")
         nc.vector.tensor_copy(
@@ -296,59 +335,67 @@ def tile_list_bell_envelope_chart_kernel(
             wc_planes[:].rearrange("p (b i m) -> p b i m", b=2, i=4),
             wc_scale_raw[:].rearrange("p (b m i) -> p b i m", b=2, i=4),
         )
-        gather_words(third, 1, 4 * P, 6 * P, tag="wc_scale_raw")
+        gather_words(third, [(1, 4 * P, 6 * P)], tag="wc_scale_raw")
 
-        log_warm = held(sb, "log_warm", [P, 1], F32)
         with tc.tile_pool(name="first_roots", bufs=1) as first_roots:
             for strip in range(2):
                 h_strip = held(first_roots, "h_strip%d" % strip, [P, BANK], BF16)
-                envelope(6 + strip, [eps_rows, squares[strip, "a"], squares[strip, "b"]], h_strip[:])
+                add_term(6 + strip, squares[strip, "b"], stop=True)
+                root(6 + strip, h_strip[:])
                 quantise_h(PHASE1, P * strip, P * (strip + 1), h_strip[:])
-            nc.scalar.activation(log_warm[:], h_strip[:, 0:1], ACT.Ln)
         late_pages = ctx.enter_context(tc.tile_pool(name="late_pages", bufs=1))
         for page in range(EARLY_PAGES, PAGES):
             clear_page(late_pages, page, nc.gpsimd)
 
         y1 = held(second, "y1", [P, PAGES * WIDTH1], F32, tag="tab0")
-        products([(0, 0, P)], PHASE1, 1)
-        negated = held(sb, "negated", [P, P], F32)
-        nc.vector.tensor_scalar(negated[:], banks[1][:, 0:P], -1.0, None, MULT)
-        size_first = held(sb, "size_first", [P, P], F32)
-        nc.vector.tensor_tensor(size_first[:], banks[1][:, 0:P], negated[:], MAX)
-        gather_words(sb, 1, 6 * P, S, tag="negated")
-        log1p(y1[:, 0:P], size_first[:])
-        scatter([(0, 0, P)], y1[:, 0:P])
+        first_parts = [(page, 0, P) for page in range(FIRST_PARTS)]
+        total = products(first_parts, PHASE1, 6)
+        negated = held(sb, "negated", [P, total], F32)
+        nc.vector.tensor_scalar(negated[:], banks[6][:, 0:total], -1.0, None, MULT)
+        with tc.tile_pool(name="first_sizes", bufs=1) as first_sizes:
+            size_first = held(first_sizes, "size_first", [P, total], F32)
+            nc.vector.tensor_tensor(size_first[:], banks[6][:, 0:total], negated[:], MAX)
+            gather_words(sb, [(1, 6 * P, S)], tag="negated")
+            log1p(y1[:, 0:P], size_first[:, 0:P])
+            log1p(y1[:, P:total], size_first[:, P:total])
+        scatter(first_parts, y1[:, 0:total])
+        at = total
 
-        at = P
-        for group, tag in (
-            ([(1, 0, WIDTH1), (0, P, WIDTH1)], "late_squares"),
-            ([(2, 0, WIDTH1), (3, 0, WIDTH1)], None),
-            ([(4, 0, WIDTH1), (5, 0, WIDTH1)], None),
-        ):
+        def group_of_parts(group, bank, at, tag, pool):
             total = sum(hi - lo for page, lo, hi in group)
-            features(group, PHASE1, 0, y1[:, at : at + total], tag)
+            features(group, PHASE1, bank, y1[:, at : at + total], tag, pool)
             scatter(group, y1[:, at : at + total])
-            at = at + total
-        products([(7, P, WIDTH1)], PHASE1, 0)
-        size_last = held(sb, "size_last", [P, P], F32)
-        nc.scalar.activation(size_last[:], banks[0][:, 0:P], ACT.Abs)
-        y_page6 = y1[:, at : at + WIDTH1]
-        y_page7 = y1[:, at + WIDTH1 : at + WIDTH1 + P]
-        features([(6, 0, WIDTH1), (7, 0, P)], PHASE1, 0, y1[:, at : at + WIDTH1 + P], "h_phase2")
-        scatter([(6, 0, P)], y_page6)
+            return at + total
 
-        late = ((2, "b", 7), (3, "b", 6), (4, "a", 5), (4, "b", 4))
-        late_squares = held(sb, "late_squares", [P, len(late) * BANK], F32)
+        behind = ctx.enter_context(tc.tile_pool(name="behind", bufs=1))
+        late = ((2, "b", 6), (3, "b", 7), (4, "a", 0), (4, "b", 1))
+        late_squares = held(behind, "late_squares", [P, len(late) * BANK], F32)
         for n, (strip, f, bank) in enumerate(late):
             squares[strip, f] = late_squares[:, BANK * n : BANK * (n + 1)]
-            filter_squared(strip, f, bank)
-        h_phase2 = held(sb, "h_phase2", [P, 3 * BANK], BF16)
-        for strip, bank in ((2, 3), (3, 1), (4, 2)):
-            later_envelope(strip, bank, h_phase2[:, BANK * (strip - 2) : BANK * (strip - 1)])
+        at = group_of_parts([(0, P, WIDTH1), (1, P, WIDTH1), (2, 0, WIDTH1)], 7, at, "second_size", behind)
+        products([(7, 0, WIDTH1)], PHASE1, 0)
+        size_last = held(behind, "size_last", [P, WIDTH1], F32)
+        nc.scalar.activation(size_last[:], banks[0][:, 0:WIDTH1], ACT.Abs)
+        for step in late[0:2]:
+            filter_squared(*step)
+        at = group_of_parts([(3, 0, WIDTH1), (4, 0, WIDTH1)], 1, at, "third_size", behind)
+        for step in late[2:]:
+            filter_squared(*step)
+        y_page7 = y1[:, at : at + P]
+        log1p(y_page7, size_last[:, 0:P])
+        y_page5 = y1[:, at + P : at + P + WIDTH1]
+        y_page6 = y1[:, at + P + WIDTH1 : at + P + 2 * WIDTH1]
+        features([(5, 0, WIDTH1), (6, 0, WIDTH1)], PHASE1, 2, y1[:, at + P : at + P + 2 * WIDTH1], "h_phase2", behind)
+        scatter([(5, 0, WIDTH1)], y_page5)
+        scatter([(6, 0, P)], y_page6)
+
+        h_phase2 = held(behind, "h_phase2", [P, 3 * BANK], BF16)
+        for strip, bank, first, last in ((2, 5, "b", "a"), (3, 3, "b", "a"), (4, 4, "a", "b")):
+            later_envelope(strip, bank, h_phase2[:, BANK * (strip - 2) : BANK * (strip - 1)], first, last)
         quantise_three_strips(PHASE2, h_phase2)
-        kept = held(sb, "kept", [P, WIDTH1 + P], F32, tag="late_squares")
-        nc.scalar.copy(kept[:, 0:WIDTH1], wgo_sb[:, 0:WIDTH1])
-        log1p(kept[:, WIDTH1:], size_last[:])
+        kept = held(behind, "kept", [P, WIDTH1 + P], F32, tag="late_squares")
+        nc.sync.dma_start(kept[:, 0:WIDTH1], wgo[:, 0:WIDTH1])
+        log1p(kept[:, WIDTH1:], size_last[:, P:])
         scatter_part(7, 0, P, y_page7, kept[:, 0:P])
         scatter_part(6, P, WIDTH1, y_page6[:, P:WIDTH1], kept[:, P:WIDTH1])
         scatter_part(7, P, WIDTH1, kept[:, WIDTH1:], wgo_sb[:, P:WIDTH1])
@@ -358,20 +405,27 @@ def tile_list_bell_envelope_chart_kernel(
 
         y2 = [
             held(sb, "y2a", [P, 4 * WIDTH23], F32, tag="y_spare"),
-            held(second, "y2b", [P, 4 * WIDTH23], F32, tag="tab1"),
+            held(third, "y2b", [P, 4 * WIDTH23], F32, tag="tab1"),
         ]
-        waits_for_log = {0: "sq5a", 1: "sq5b", 6: "h_phase3"}
-        for page in range(PAGES - 1):
-            features([(page, *PHASE2)], PHASE2, 2, page_columns(y2, page), waits_for_log.get(page))
-            scatter([(page, *PHASE2)], page_columns(y2, page))
+        lo, hi = PHASE2
+        groups = [([(0, lo, lo + P)], 4), ([(1, lo, lo + 2 * P)], 5), ([(0, lo + P, hi), (1, lo + 2 * P, hi)], 4)]
+        groups.extend(([(page, lo, hi)], 4) for page in range(2, PAGES - 1))
+        waits_for_log = {2: "sq5a", 3: "sq5b", len(groups) - 1: "h_phase3"}
+        at = 0
+        for n, (group, bank) in enumerate(groups):
+            total = sum(end - first for page, first, end in group)
+            y = y2[at // (4 * WIDTH23)][:, at % (4 * WIDTH23) : at % (4 * WIDTH23) + total]
+            features(group, PHASE2, bank, y, waits_for_log.get(n))
+            scatter(group, y)
+            at = at + total
         for strip in (5, 6, 7):
             filter_squared(strip, "a", 6)
             filter_squared(strip, "b", 7)
         h_phase3 = held(sb, "h_phase3", [P, 3 * BANK], BF16)
-        for strip, bank in ((5, 1), (6, 4), (7, 3)):
-            later_envelope(strip, bank, h_phase3[:, BANK * (strip - 5) : BANK * (strip - 4)])
+        for strip, bank in ((5, 1), (6, 2), (7, 3)):
+            later_envelope(strip, bank, h_phase3[:, BANK * (strip - 5) : BANK * (strip - 4)], "a", "b")
         quantise_three_strips(PHASE3, h_phase3)
-        features([(PAGES - 1, *PHASE2)], PHASE2, 3, page_columns(y2, PAGES - 1))
+        features([(PAGES - 1, *PHASE2)], PHASE2, 3, page_columns(y2, PAGES - 1), "turn_size")
         scatter([(PAGES - 1, *PHASE2)], page_columns(y2, PAGES - 1))
 
         out_pages = out.rearrange("(b p i) t -> b i p t", b=2, i=4)
@@ -379,7 +433,18 @@ def tile_list_bell_envelope_chart_kernel(
             held(second, "y3a", [P, 4 * WIDTH23], F32, tag="tab0"),
             held(sb, "y3b", [P, 4 * WIDTH23], F32, tag="y_spare"),
         ]
-        for page in range(PAGES):
-            features([(page, *PHASE3)], PHASE3, 3, page_columns(y3, page))
-            scatter([(page, *PHASE3)], page_columns(y3, page))
-            nc.sync.dma_start(out_pages[page // 4, page % 4], pages[page][:])
+        lo, hi = PHASE3
+        groups = [((0, lo, lo + P), 3), ((1, lo, hi), 1), ((0, lo + P, hi), 3)]
+        groups.extend(((page, lo, hi), 3) for page in range(2, PAGES))
+        for (page, first, end), bank in groups:
+            y = page_columns(y3, page)[:, first - lo : end - lo]
+            features([(page, first, end)], PHASE3, bank, y, "turn_size" if page == 1 else None)
+            scatter([(page, first, end)], y)
+            if end < hi:
+                continue
+            rows = out_pages[page // 4, page % 4]
+            if page < PAGES - 1:
+                nc.sync.dma_start(rows, pages[page][:])
+            else:
+                nc.sync.dma_start(rows[:, 0 : T2 // 2], pages[page][:, 0 : T2 // 2])
+                nc.scalar.dma_start(rows[:, T2 // 2 :], pages[page][:, T2 // 2 :])

@@ -30,7 +30,6 @@ WIDTH23 = PHASE2[1] - PHASE2[0]
 EARLY_PAGES = 3
 FIRST_PARTS = 2
 
-B0_VECTOR = 64
 A1_VECTOR = 224
 
 
@@ -86,7 +85,6 @@ def tile_list_bell_envelope_chart_kernel(
         load_tab(second, 0)
         eps_sb = held(second, "eps_sb", [P, 4], F32)
         nc.sync.dma_start(eps_sb[:], eps.rearrange("(p i) -> p i", i=4))
-        load_w(second, "b0", 0, H, 2 * H)
         load_w(second, "a1", 1, 0, H)
 
         pages = {}
@@ -95,7 +93,7 @@ def tile_list_bell_envelope_chart_kernel(
             pages[page] = held(pool, "page%d" % page, [P, T2], F32)
             engine.memset(pages[page][:], 0.0)
 
-        for page in range(EARLY_PAGES):
+        for page in range(EARLY_PAGES - 1):
             clear_page(second, page, nc.vector)
 
         v_scales = held(sb, "v_scales", [P, S], U8)
@@ -110,7 +108,9 @@ def tile_list_bell_envelope_chart_kernel(
                     v_scales[8 * a + 2 + e : P : 32, :].bitcast(I32),
                     v_scales[16 + 8 * a + e : P : 32, :].bitcast(I32),
                 )
+        clear_page(third, EARLY_PAGES - 1, nc.vector)
         load_tab(third, 1)
+        load_w(third, "b0", 0, H, 2 * H)
         load_w(third, "b1lo", 1, H, H + HALF)
         for n in range(2):
             load_w(third, "b1hi%d" % n, 1, H + HALF + P * n, H + HALF + P * (n + 1))
@@ -187,11 +187,11 @@ def tile_list_bell_envelope_chart_kernel(
                 filter_pass(strip, f, a, bank, a == 0, a == 1)
             square(strip, f, bank)
 
-        def add_term(bank, term, start=False, stop=False, identity=ident):
+        def add_term(bank, term, start=False, stop=False):
             for i in range(4):
                 cols = slice(P * i, P * (i + 1))
                 nc.tensor.matmul(
-                    banks[bank][:, cols], term[:, cols], identity[:], is_transpose=True,
+                    banks[bank][:, cols], term[:, cols], ident[:], is_transpose=True,
                     start=(start and i == 0), stop=(stop and i == 3),
                 )
 
@@ -263,15 +263,12 @@ def tile_list_bell_envelope_chart_kernel(
                 scatter_part(page, lo, hi, y[:, at : at + hi - lo], wgo_sb[:, lo:hi])
                 at = at + hi - lo
 
-        gather_words(third, [(0, 0, S)])
+        gather_words(third, [(0, 0, 5 * P)])
         with tc.tile_pool(name="rounded", bufs=1) as rounded:
-            grouped = {name: held(rounded, "bf_" + name, [P, H, 4], BF16) for name in ("a0", "b0", "a1")}
+            grouped = {name: held(rounded, "bf_" + name, [P, H, 4], BF16) for name in ("a0", "a1")}
             round_w(w_raw["a0lo"][:], grouped["a0"][:, 0:HALF, :], nc.scalar.copy)
             round_w(w_raw["a0hi"][:], grouped["a0"][:, HALF:, :], nc.scalar.copy)
             pack_w(grouped["a0"][:], "a0", 0)
-            round_w(w_raw["b0"][:, :, 0:B0_VECTOR], grouped["b0"][:, 0:B0_VECTOR, :], nc.vector.tensor_copy)
-            round_w(w_raw["b0"][:, :, B0_VECTOR:], grouped["b0"][:, B0_VECTOR:, :], nc.scalar.copy)
-            pack_w(grouped["b0"][:], "b0", 0)
             round_w(w_raw["a1"][:, :, 0:A1_VECTOR], grouped["a1"][:, 0:A1_VECTOR, :], nc.vector.tensor_copy)
             round_w(w_raw["a1"][:, :, A1_VECTOR:], grouped["a1"][:, A1_VECTOR:, :], nc.scalar.copy)
             pack_w(grouped["a1"][:], "a1", 0)
@@ -282,50 +279,52 @@ def tile_list_bell_envelope_chart_kernel(
         for i in range(4):
             nc.tensor.transpose(banks[7][:, P * i : P * (i + 1)], eps_sb[:, i : i + 1].to_broadcast([P, P]), ident[:])
         nc.scalar.copy(eps_rows[:], banks[7][:])
-        for strip in range(2):
-            add_term(6 + strip, eps_rows, start=True)
-        for strip in range(3):
-            filter_pass(strip, "a", 0, strip, True, False)
-        filter_pass(0, "b", 0, 3, True, False, 0, HALF)
-        filter_pass(0, "b", 0, 4, True, False, HALF, H)
-        filter_pass(1, "b", 0, 5, True, False)
-        for half in range(2):
-            filter_pass(3, "a", 0, 3 + half, False, False, HALF * half, HALF * (half + 1), HALF)
         gather_words(third, [(1, 0, 2 * P)])
         gather_words(third, [(1, 2 * P, 4 * P)])
-        early_squares = held(second, "early_squares", [P, 2 * BANK], F32, tag="raw_b0")
-        for strip in range(2):
-            squares[strip, "a"] = early_squares[:, BANK * strip : BANK * (strip + 1)]
-        for strip in range(2):
-            filter_pass(strip, "a", 1, strip, False, True)
-            square(strip, "a", strip)
-        filter_pass(2, "a", 1, 2, False, True)
-        for half in range(2):
-            filter_pass(3, "a", 1, 3 + half, False, False, HALF * half, HALF * (half + 1), HALF)
-        add_term(6, squares[0, "a"])
+        gather_words(third, [(1, 4 * P, S)])
+        for strip in range(4):
+            for a in range(2):
+                filter_pass(strip, "a", a, strip, a == 0, a == 1)
 
+        def open_sum(strip):
+            square(strip, "a", strip)
+            add_term(strip, eps_rows, start=True)
+            add_term(strip, squares[strip, "a"])
+
+        open_sum(0)
+        open_sum(1)
+
+        grouped_b0 = [held(fourth, "bf_b0%d" % n, [P, HALF, 4], BF16) for n in range(2)]
+        for n, copy in enumerate((nc.vector.tensor_copy, nc.scalar.copy)):
+            round_w(w_raw["b0"][:, :, HALF * n : HALF * (n + 1)], grouped_b0[n][:], copy)
+            pack_w(grouped_b0[n][:], "b0", HALF * n)
+        for strip in range(2):
+            filter_pass(strip, "b", 0, 4, strip == 0, False, 0, HALF, HALF * strip)
+        for strip in range(2):
+            filter_pass(strip, "b", 0, 5 + strip, True, False, HALF, H)
+        filter_pass(2, "b", 0, 7, True, False)
         quantise_w(fourth, "b1lo", 0, HALF, nc.vector.tensor_copy)
-        filter_pass(0, "b", 1, 3, False, True, 0, HALF)
-        filter_pass(1, "b", 1, 5, False, False, 0, HALF)
-        square(0, "b", 3, 0, HALF)
+        for strip in range(2):
+            filter_pass(strip, "b", 1, 4, False, strip == 1, 0, HALF, HALF * strip)
+        for strip in range(2):
+            square(strip, "b", 4, 0, HALF, HALF * strip)
+        grouped_hi = [held(fourth, "bf_b1hi0", [P, P, 4], BF16), held(fourth, "bf_b1hi1", [P, P, 4], BF16)]
+        for n, copy in enumerate((nc.scalar.copy, nc.vector.tensor_copy)):
+            round_w(w_raw["b1hi%d" % n][:], grouped_hi[n][:], copy)
+        squares[2, "a"] = held(third, "sq2a", [P, BANK], F32, tag="raw_b1hi0")
         square(2, "a", 2)
-        grouped_hi = [held(fourth, "bf_b1hi0", [P, P, 4], BF16), held(fourth, "bf_b1hi1", [P, P, 4], BF16, tag="bf1")]
-        for n in range(2):
-            round_w(w_raw["b1hi%d" % n][:], grouped_hi[n][:], nc.vector.tensor_copy)
         for n in range(2):
             pack_w(grouped_hi[n][:], "b1", HALF + P * n)
-        filter_pass(0, "b", 1, 4, False, True, HALF, H)
-        filter_pass(1, "b", 1, 5, False, True, HALF, H, HALF)
-        late_ident = held(fourth, "late_ident", [P, P], F32, tag="bf_b1hi0")
-        nc.vector.tensor_copy(late_ident[:], ident[:])
-        add_term(7, squares[1, "a"], identity=late_ident)
-        square(0, "b", 4, HALF, H)
-        square(1, "b", 5)
+        for strip in range(2):
+            filter_pass(strip, "b", 1, 5 + strip, False, True, HALF, H)
+        filter_pass(2, "b", 1, 7, False, True)
+        for strip in range(2):
+            square(strip, "b", 5 + strip, HALF, H)
         squares[3, "a"] = held(third, "sq3a", [P, BANK], F32, tag="v_codes1_0")
-        for half in range(2):
-            square(3, "a", 3 + half, HALF * half, HALF * (half + 1), HALF)
+        square(3, "a", 3)
 
-        wc_codes = held(fourth, "wc_codes", [P, 2 * N], U8, tag="bf1")
+        gather_words(fourth, [(0, 5 * P, S)], tag="bf_b1hi0")
+        wc_codes = held(fourth, "wc_codes", [P, 2 * N], U8, tag="bf_b1hi1")
         nc.vector.tensor_copy(
             wc_codes[:].bitcast(U16).rearrange("p (b i m) -> p b i m", b=2, i=4),
             wc_raw[:].bitcast(U16).rearrange("p (b m i) -> p b i m", b=2, i=4),
@@ -335,13 +334,12 @@ def tile_list_bell_envelope_chart_kernel(
             wc_planes[:].rearrange("p (b i m) -> p b i m", b=2, i=4),
             wc_scale_raw[:].rearrange("p (b m i) -> p b i m", b=2, i=4),
         )
-        gather_words(third, [(1, 4 * P, 6 * P)], tag="wc_scale_raw")
 
         with tc.tile_pool(name="first_roots", bufs=1) as first_roots:
             for strip in range(2):
                 h_strip = held(first_roots, "h_strip%d" % strip, [P, BANK], BF16)
-                add_term(6 + strip, squares[strip, "b"], stop=True)
-                root(6 + strip, h_strip[:])
+                add_term(strip, squares[strip, "b"], stop=True)
+                root(strip, h_strip[:])
                 quantise_h(PHASE1, P * strip, P * (strip + 1), h_strip[:])
         late_pages = ctx.enter_context(tc.tile_pool(name="late_pages", bufs=1))
         for page in range(EARLY_PAGES, PAGES):
@@ -349,13 +347,12 @@ def tile_list_bell_envelope_chart_kernel(
 
         y1 = held(second, "y1", [P, PAGES * WIDTH1], F32, tag="tab0")
         first_parts = [(page, 0, P) for page in range(FIRST_PARTS)]
-        total = products(first_parts, PHASE1, 6)
+        total = products(first_parts, PHASE1, 4)
         negated = held(sb, "negated", [P, total], F32)
-        nc.vector.tensor_scalar(negated[:], banks[6][:, 0:total], -1.0, None, MULT)
+        nc.vector.tensor_scalar(negated[:], banks[4][:, 0:total], -1.0, None, MULT)
         with tc.tile_pool(name="first_sizes", bufs=1) as first_sizes:
             size_first = held(first_sizes, "size_first", [P, total], F32)
-            nc.vector.tensor_tensor(size_first[:], banks[6][:, 0:total], negated[:], MAX)
-            gather_words(sb, [(1, 6 * P, S)], tag="negated")
+            nc.vector.tensor_tensor(size_first[:], banks[4][:, 0:total], negated[:], MAX)
             log1p(y1[:, 0:P], size_first[:, 0:P])
             log1p(y1[:, P:total], size_first[:, P:total])
         scatter(first_parts, y1[:, 0:total])
@@ -368,17 +365,17 @@ def tile_list_bell_envelope_chart_kernel(
             return at + total
 
         behind = ctx.enter_context(tc.tile_pool(name="behind", bufs=1))
-        late = ((2, "b", 6), (3, "b", 7), (4, "a", 0), (4, "b", 1))
+        late = ((2, "b", 7), (3, "b", 4), (4, "a", 6), (4, "b", 5))
         late_squares = held(behind, "late_squares", [P, len(late) * BANK], F32)
         for n, (strip, f, bank) in enumerate(late):
             squares[strip, f] = late_squares[:, BANK * n : BANK * (n + 1)]
-        at = group_of_parts([(0, P, WIDTH1), (1, P, WIDTH1), (2, 0, WIDTH1)], 7, at, "second_size", behind)
-        products([(7, 0, WIDTH1)], PHASE1, 0)
+        at = group_of_parts([(0, P, WIDTH1), (1, P, WIDTH1), (2, 0, WIDTH1)], 5, at, "second_size", behind)
+        products([(7, 0, WIDTH1)], PHASE1, 6)
         size_last = held(behind, "size_last", [P, WIDTH1], F32)
-        nc.scalar.activation(size_last[:], banks[0][:, 0:WIDTH1], ACT.Abs)
-        for step in late[0:2]:
-            filter_squared(*step)
-        at = group_of_parts([(3, 0, WIDTH1), (4, 0, WIDTH1)], 1, at, "third_size", behind)
+        nc.scalar.activation(size_last[:], banks[6][:, 0:WIDTH1], ACT.Abs)
+        square(*late[0])
+        filter_squared(*late[1])
+        at = group_of_parts([(3, 0, WIDTH1), (4, 0, WIDTH1)], 3, at, "third_size", behind)
         for step in late[2:]:
             filter_squared(*step)
         y_page7 = y1[:, at : at + P]
@@ -390,7 +387,7 @@ def tile_list_bell_envelope_chart_kernel(
         scatter([(6, 0, P)], y_page6)
 
         h_phase2 = held(behind, "h_phase2", [P, 3 * BANK], BF16)
-        for strip, bank, first, last in ((2, 5, "b", "a"), (3, 3, "b", "a"), (4, 4, "a", "b")):
+        for strip, bank, first, last in ((2, 0, "b", "a"), (3, 1, "b", "a"), (4, 3, "a", "b")):
             later_envelope(strip, bank, h_phase2[:, BANK * (strip - 2) : BANK * (strip - 1)], first, last)
         quantise_three_strips(PHASE2, h_phase2)
         kept = held(behind, "kept", [P, WIDTH1 + P], F32, tag="late_squares")
@@ -408,8 +405,8 @@ def tile_list_bell_envelope_chart_kernel(
             held(third, "y2b", [P, 4 * WIDTH23], F32, tag="tab1"),
         ]
         lo, hi = PHASE2
-        groups = [([(0, lo, lo + P)], 4), ([(1, lo, lo + 2 * P)], 5), ([(0, lo + P, hi), (1, lo + 2 * P, hi)], 4)]
-        groups.extend(([(page, lo, hi)], 4) for page in range(2, PAGES - 1))
+        groups = [([(0, lo, lo + P)], 3), ([(1, lo, lo + 2 * P)], 0), ([(0, lo + P, hi), (1, lo + 2 * P, hi)], 3)]
+        groups.extend(([(page, lo, hi)], 3) for page in range(2, PAGES - 1))
         waits_for_log = {2: "sq5a", 3: "sq5b", len(groups) - 1: "h_phase3"}
         at = 0
         for n, (group, bank) in enumerate(groups):
@@ -422,10 +419,10 @@ def tile_list_bell_envelope_chart_kernel(
             filter_squared(strip, "a", 6)
             filter_squared(strip, "b", 7)
         h_phase3 = held(sb, "h_phase3", [P, 3 * BANK], BF16)
-        for strip, bank in ((5, 1), (6, 2), (7, 3)):
+        for strip, bank in ((5, 4), (6, 5), (7, 2)):
             later_envelope(strip, bank, h_phase3[:, BANK * (strip - 5) : BANK * (strip - 4)], "a", "b")
         quantise_three_strips(PHASE3, h_phase3)
-        features([(PAGES - 1, *PHASE2)], PHASE2, 3, page_columns(y2, PAGES - 1), "turn_size")
+        features([(PAGES - 1, *PHASE2)], PHASE2, 2, page_columns(y2, PAGES - 1), "turn_size")
         scatter([(PAGES - 1, *PHASE2)], page_columns(y2, PAGES - 1))
 
         out_pages = out.rearrange("(b p i) t -> b i p t", b=2, i=4)
@@ -434,8 +431,8 @@ def tile_list_bell_envelope_chart_kernel(
             held(sb, "y3b", [P, 4 * WIDTH23], F32, tag="y_spare"),
         ]
         lo, hi = PHASE3
-        groups = [((0, lo, lo + P), 3), ((1, lo, hi), 1), ((0, lo + P, hi), 3)]
-        groups.extend(((page, lo, hi), 3) for page in range(2, PAGES))
+        groups = [((0, lo, lo + P), 2), ((1, lo, hi), 4), ((0, lo + P, hi), 2)]
+        groups.extend(((page, lo, hi), 2) for page in range(2, PAGES))
         for (page, first, end), bank in groups:
             y = page_columns(y3, page)[:, first - lo : end - lo]
             features([(page, first, end)], PHASE3, bank, y, "turn_size" if page == 1 else None)

@@ -75,13 +75,18 @@ def tile_list_bell_envelope_chart_kernel(
             tab[a] = held(pool, "tab%d" % a, [P, T], I32)
             nc.sync.dma_start(tab[a][:], tab_words[a].rearrange("p t i -> p (t i)").bitcast(I32))
 
-        load_w(sb, "a0lo", 0, 0, HALF)
+        def load_a0_rows(pool, n):
+            w_raw["a0", n] = held(pool, "raw_a0_%d" % n, [P, 2, H], F32)
+            rows = wab[0:512, 0:H].rearrange("(p i) c -> p i c", i=4)
+            nc.sync.dma_start(w_raw["a0", n][:], rows[:, 2 * n : 2 * n + 2, :])
+
+        load_a0_rows(sb, 0)
         nc.sync.dma_start(pick[:], offs)
         nc.sync.dma_start(place[:], offs2)
         rows = tab_scales.bitcast(I32).rearrange("a (g e) t -> e g a t", e=2)
         for e in range(2):
             nc.sync.dma_start(scale_window[e:P:8, :].bitcast(I32), rows[e])
-        load_w(second, "a0hi", 0, HALF, H)
+        load_a0_rows(second, 1)
         load_tab(second, 0)
         eps_sb = held(second, "eps_sb", [P, 4], F32)
         nc.sync.dma_start(eps_sb[:], eps.rearrange("(p i) -> p i", i=4))
@@ -266,8 +271,8 @@ def tile_list_bell_envelope_chart_kernel(
         gather_words(third, [(0, 0, 5 * P)])
         with tc.tile_pool(name="rounded", bufs=1) as rounded:
             grouped = {name: held(rounded, "bf_" + name, [P, H, 4], BF16) for name in ("a0", "a1")}
-            round_w(w_raw["a0lo"][:], grouped["a0"][:, 0:HALF, :], nc.scalar.copy)
-            round_w(w_raw["a0hi"][:], grouped["a0"][:, HALF:, :], nc.scalar.copy)
+            for n in range(2):
+                round_w(w_raw["a0", n][:], grouped["a0"][:, :, 2 * n : 2 * n + 2], nc.scalar.copy)
             pack_w(grouped["a0"][:], "a0", 0)
             round_w(w_raw["a1"][:, :, 0:A1_VECTOR], grouped["a1"][:, 0:A1_VECTOR, :], nc.vector.tensor_copy)
             round_w(w_raw["a1"][:, :, A1_VECTOR:], grouped["a1"][:, A1_VECTOR:, :], nc.scalar.copy)
@@ -275,7 +280,7 @@ def tile_list_bell_envelope_chart_kernel(
         fourth = ctx.enter_context(tc.tile_pool(name="fourth", bufs=1))
         wgo_sb = held(fourth, "wgo_sb", [P, S], F32)
         nc.sync.dma_start(wgo_sb[:], wgo)
-        eps_rows = held(second, "eps_rows", [P, BANK], F32, tag="raw_a0hi")
+        eps_rows = held(second, "eps_rows", [P, BANK], F32, tag="raw_a0_1")
         for i in range(4):
             nc.tensor.transpose(banks[7][:, P * i : P * (i + 1)], eps_sb[:, i : i + 1].to_broadcast([P, P]), ident[:])
         nc.scalar.copy(eps_rows[:], banks[7][:])

@@ -1,7 +1,6 @@
 from contextlib import ExitStack
 
 import concourse.mybir as mybir
-from concourse.masks import make_identity
 
 K, T, S, H, N, T2 = 1024, 2048, 1024, 512, 1024, 2048
 FLOPS = 2 * K * 2 * H * S + 2 * H * N * S
@@ -28,9 +27,9 @@ WIDTH1 = PHASE1[1] - PHASE1[0]
 WIDTH23 = PHASE2[1] - PHASE2[0]
 
 EARLY_PAGES = 3
-FIRST_PARTS = 2
+FIRST_PARTS = 4
 
-A1_VECTOR = 224
+A1_VECTOR = 256
 
 
 def tile_list_bell_envelope_chart_kernel(
@@ -61,7 +60,12 @@ def tile_list_bell_envelope_chart_kernel(
         root_warm = held(sb, "root_warm", [P, 1], F32)
         nc.scalar.activation(root_warm[:], one[:], ACT.Sqrt)
         ident = held(sb, "ident", [P, P], F32)
-        make_identity(nc, ident[:])
+        zeros = held(second, "zeros", [P, P], F32, tag="page%d" % (EARLY_PAGES - 1))
+        nc.vector.memset(zeros[:], 0.0)
+        nc.gpsimd.affine_select(
+            out=ident[:], in_=zeros[:], compare_op=mybir.AluOpType.not_equal, fill=1.0,
+            base=0, pattern=[[-1, P]], channel_multiplier=1,
+        )
 
         w_raw = {}
         tab = {}
@@ -100,6 +104,7 @@ def tile_list_bell_envelope_chart_kernel(
 
         for page in range(EARLY_PAGES - 1):
             clear_page(second, page, nc.vector)
+        clear_page(second, EARLY_PAGES - 1, nc.gpsimd)
 
         v_scales = held(sb, "v_scales", [P, S], U8)
         with tc.tile_pool(name="picked", bufs=1) as picked_pool:
@@ -113,21 +118,14 @@ def tile_list_bell_envelope_chart_kernel(
                     v_scales[8 * a + 2 + e : P : 32, :].bitcast(I32),
                     v_scales[16 + 8 * a + e : P : 32, :].bitcast(I32),
                 )
-        clear_page(third, EARLY_PAGES - 1, nc.vector)
         load_tab(third, 1)
-        load_w(third, "b0", 0, H, 2 * H)
+        load_w(third, "b0lo", 0, H, H + HALF)
         load_w(third, "b1lo", 1, H, H + HALF)
+        load_w(third, "b0hi", 0, H + HALF, 2 * H)
         for n in range(2):
             load_w(third, "b1hi%d" % n, 1, H + HALF + P * n, H + HALF + P * (n + 1))
         wc_raw = held(third, "wc_raw", [P, 2 * N], U8)
         nc.sync.dma_start(wc_raw[:].bitcast(I32), wc_words[0].bitcast(I32))
-        wc_scale_raw = held(third, "wc_scale_raw", [P, N], U8)
-        nc.gpsimd.memset(wc_scale_raw[:].bitcast(I32), 0)
-        for d in range(4):
-            nc.sync.dma_start(
-                wc_scale_raw[32 * d : 32 * d + 4, :].bitcast(I32),
-                wc_scales[0, 4 * d : 4 * d + 4, :].bitcast(I32),
-            )
 
         w_codes = {name: held(third, "codes_" + name, [P, H], U32) for name in ("a0", "b0", "a1", "b1")}
         w_scales = {name: held(sb, "scales_" + name, [P, H], U8) for name in ("a0", "b0", "a1", "b1")}
@@ -145,11 +143,6 @@ def tile_list_bell_envelope_chart_kernel(
                 scales=w_scales[name][:, cols],
                 in_=grouped.rearrange("p c i -> p (c i)"),
             )
-
-        def quantise_w(pool, piece, first_col, width, copy):
-            grouped = held(pool, "bf_" + piece, [P, width, 4], BF16, tag="bf" + piece[1])
-            round_w(w_raw[piece][:], grouped[:], copy)
-            pack_w(grouped[:], piece[0:2], first_col)
 
         v_codes = {}
 
@@ -221,11 +214,6 @@ def tile_list_bell_envelope_chart_kernel(
             cols = slice(lo - phase[0], hi - phase[0])
             nc.vector.quantize_mx(out=h_codes[phase][:, cols].bitcast(FP8X4), scales=h_scales[phase][:, cols], in_=h_bf)
 
-        def quantise_three_strips(phase, h_bf):
-            cut = phase[0] + 2 * P
-            quantise_h(phase, phase[0], cut, h_bf[:, 0 : 2 * BANK])
-            quantise_h(phase, cut, phase[1], h_bf[:, 2 * BANK :])
-
         def products(parts, phase, bank):
             passes = []
             at = 0
@@ -268,16 +256,23 @@ def tile_list_bell_envelope_chart_kernel(
                 scatter_part(page, lo, hi, y[:, at : at + hi - lo], wgo_sb[:, lo:hi])
                 at = at + hi - lo
 
-        gather_words(third, [(0, 0, 5 * P)])
         with tc.tile_pool(name="rounded", bufs=1) as rounded:
             grouped = {name: held(rounded, "bf_" + name, [P, H, 4], BF16) for name in ("a0", "a1")}
             for n in range(2):
                 round_w(w_raw["a0", n][:], grouped["a0"][:, :, 2 * n : 2 * n + 2], nc.scalar.copy)
             pack_w(grouped["a0"][:], "a0", 0)
+            gather_words(third, [(0, 0, S)])
             round_w(w_raw["a1"][:, :, 0:A1_VECTOR], grouped["a1"][:, 0:A1_VECTOR, :], nc.vector.tensor_copy)
             round_w(w_raw["a1"][:, :, A1_VECTOR:], grouped["a1"][:, A1_VECTOR:, :], nc.scalar.copy)
             pack_w(grouped["a1"][:], "a1", 0)
         fourth = ctx.enter_context(tc.tile_pool(name="fourth", bufs=1))
+        wc_scale_raw = held(fourth, "wc_scale_raw", [P, N], U8)
+        nc.gpsimd.memset(wc_scale_raw[:].bitcast(I32), 0)
+        for d in range(4):
+            nc.sync.dma_start(
+                wc_scale_raw[32 * d : 32 * d + 4, :].bitcast(I32),
+                wc_scales[0, 4 * d : 4 * d + 4, :].bitcast(I32),
+            )
         wgo_sb = held(fourth, "wgo_sb", [P, S], F32)
         nc.sync.dma_start(wgo_sb[:], wgo)
         eps_rows = held(second, "eps_rows", [P, BANK], F32, tag="raw_a0_1")
@@ -286,7 +281,6 @@ def tile_list_bell_envelope_chart_kernel(
         nc.scalar.copy(eps_rows[:], banks[7][:])
         gather_words(third, [(1, 0, 2 * P)])
         gather_words(third, [(1, 2 * P, 4 * P)])
-        gather_words(third, [(1, 4 * P, S)])
         for strip in range(4):
             for a in range(2):
                 filter_pass(strip, "a", a, strip, a == 0, a == 1)
@@ -298,26 +292,33 @@ def tile_list_bell_envelope_chart_kernel(
 
         open_sum(0)
         open_sum(1)
+        square(2, "a", 2)
 
-        grouped_b0 = [held(fourth, "bf_b0%d" % n, [P, HALF, 4], BF16) for n in range(2)]
+        def quantise_half(piece, first_col):
+            grouped = held(fourth, "bf_" + piece, [P, HALF, 4], BF16)
+            round_w(w_raw[piece][:], grouped[:], nc.vector.tensor_copy)
+            pack_w(grouped[:], piece[0:2], first_col)
+
+        for a in range(2):
+            quantise_half("b%dlo" % a, 0)
+            for strip in range(2):
+                filter_pass(strip, "b", a, 4, a + strip == 0, a + strip == 2, 0, HALF, HALF * strip)
+        grouped_b0hi = held(fourth, "bf_b0hi", [P, HALF, 4], BF16)
         for n, copy in enumerate((nc.vector.tensor_copy, nc.scalar.copy)):
-            round_w(w_raw["b0"][:, :, HALF * n : HALF * (n + 1)], grouped_b0[n][:], copy)
-            pack_w(grouped_b0[n][:], "b0", HALF * n)
-        for strip in range(2):
-            filter_pass(strip, "b", 0, 4, strip == 0, False, 0, HALF, HALF * strip)
+            round_w(w_raw["b0hi"][:, :, P * n : P * (n + 1)], grouped_b0hi[:, P * n : P * (n + 1), :], copy)
+        pack_w(grouped_b0hi[:], "b0", HALF)
         for strip in range(2):
             filter_pass(strip, "b", 0, 5 + strip, True, False, HALF, H)
         filter_pass(2, "b", 0, 7, True, False)
-        quantise_w(fourth, "b1lo", 0, HALF, nc.vector.tensor_copy)
-        for strip in range(2):
-            filter_pass(strip, "b", 1, 4, False, strip == 1, 0, HALF, HALF * strip)
-        for strip in range(2):
-            square(strip, "b", 4, 0, HALF, HALF * strip)
         grouped_hi = [held(fourth, "bf_b1hi0", [P, P, 4], BF16), held(fourth, "bf_b1hi1", [P, P, 4], BF16)]
         for n, copy in enumerate((nc.scalar.copy, nc.vector.tensor_copy)):
             round_w(w_raw["b1hi%d" % n][:], grouped_hi[n][:], copy)
-        squares[2, "a"] = held(third, "sq2a", [P, BANK], F32, tag="raw_b1hi0")
-        square(2, "a", 2)
+        b_squares = held(third, "b_squares", [P, 3 * BANK], F32, tag="raw_b1hi0")
+        for strip in range(2):
+            squares[strip, "b"] = b_squares[:, BANK * strip : BANK * (strip + 1)]
+            square(strip, "b", 4, 0, HALF, HALF * strip)
+        squares[3, "a"] = b_squares[:, 2 * BANK :]
+        square(3, "a", 3)
         for n in range(2):
             pack_w(grouped_hi[n][:], "b1", HALF + P * n)
         for strip in range(2):
@@ -325,10 +326,8 @@ def tile_list_bell_envelope_chart_kernel(
         filter_pass(2, "b", 1, 7, False, True)
         for strip in range(2):
             square(strip, "b", 5 + strip, HALF, H)
-        squares[3, "a"] = held(third, "sq3a", [P, BANK], F32, tag="v_codes1_0")
-        square(3, "a", 3)
 
-        gather_words(fourth, [(0, 5 * P, S)], tag="bf_b1hi0")
+        gather_words(fourth, [(1, 4 * P, S)], tag="bf_b1hi0")
         wc_codes = held(fourth, "wc_codes", [P, 2 * N], U8, tag="bf_b1hi1")
         nc.vector.tensor_copy(
             wc_codes[:].bitcast(U16).rearrange("p (b i m) -> p b i m", b=2, i=4),
@@ -352,14 +351,17 @@ def tile_list_bell_envelope_chart_kernel(
 
         y1 = held(second, "y1", [P, PAGES * WIDTH1], F32, tag="tab0")
         first_parts = [(page, 0, P) for page in range(FIRST_PARTS)]
-        total = products(first_parts, PHASE1, 4)
+        total = FIRST_PARTS * P
+        spans = ((first_parts[0:1], 4, slice(0, P)), (first_parts[1:], 5, slice(P, total)))
         negated = held(sb, "negated", [P, total], F32)
-        nc.vector.tensor_scalar(negated[:], banks[4][:, 0:total], -1.0, None, MULT)
+        for parts, bank, cols in spans:
+            width = products(parts, PHASE1, bank)
+            nc.vector.tensor_scalar(negated[:, cols], banks[bank][:, 0:width], -1.0, None, MULT)
         with tc.tile_pool(name="first_sizes", bufs=1) as first_sizes:
             size_first = held(first_sizes, "size_first", [P, total], F32)
-            nc.vector.tensor_tensor(size_first[:], banks[4][:, 0:total], negated[:], MAX)
-            log1p(y1[:, 0:P], size_first[:, 0:P])
-            log1p(y1[:, P:total], size_first[:, P:total])
+            for parts, bank, cols in spans:
+                nc.vector.tensor_tensor(size_first[:, cols], banks[bank][:, 0 : P * len(parts)], negated[:, cols], MAX)
+                log1p(y1[:, cols], size_first[:, cols])
         scatter(first_parts, y1[:, 0:total])
         at = total
 
@@ -370,31 +372,28 @@ def tile_list_bell_envelope_chart_kernel(
             return at + total
 
         behind = ctx.enter_context(tc.tile_pool(name="behind", bufs=1))
-        late = ((2, "b", 7), (3, "b", 4), (4, "a", 6), (4, "b", 5))
+        late = ((2, "b", 7), (3, "b", 4), (4, "a", 5), (4, "b", 6))
         late_squares = held(behind, "late_squares", [P, len(late) * BANK], F32)
         for n, (strip, f, bank) in enumerate(late):
             squares[strip, f] = late_squares[:, BANK * n : BANK * (n + 1)]
-        at = group_of_parts([(0, P, WIDTH1), (1, P, WIDTH1), (2, 0, WIDTH1)], 5, at, "second_size", behind)
-        products([(7, 0, WIDTH1)], PHASE1, 6)
+        at = group_of_parts([(page, P, WIDTH1) for page in range(FIRST_PARTS)], 6, at, "second_size", behind)
+        products([(7, 0, WIDTH1)], PHASE1, 2)
         size_last = held(behind, "size_last", [P, WIDTH1], F32)
-        nc.scalar.activation(size_last[:], banks[6][:, 0:WIDTH1], ACT.Abs)
+        nc.scalar.activation(size_last[:], banks[2][:, 0:WIDTH1], ACT.Abs)
         square(*late[0])
-        filter_squared(*late[1])
-        at = group_of_parts([(3, 0, WIDTH1), (4, 0, WIDTH1)], 3, at, "third_size", behind)
-        for step in late[2:]:
+        at = group_of_parts([(4, 0, WIDTH1), (5, 0, WIDTH1)], 2, at, "third_size", behind)
+        for step in late[1:]:
             filter_squared(*step)
         y_page7 = y1[:, at : at + P]
         log1p(y_page7, size_last[:, 0:P])
-        y_page5 = y1[:, at + P : at + P + WIDTH1]
-        y_page6 = y1[:, at + P + WIDTH1 : at + P + 2 * WIDTH1]
-        features([(5, 0, WIDTH1), (6, 0, WIDTH1)], PHASE1, 2, y1[:, at + P : at + P + 2 * WIDTH1], "h_phase2", behind)
-        scatter([(5, 0, WIDTH1)], y_page5)
+        y_page6 = y1[:, at + P : at + P + WIDTH1]
+        features([(6, 0, WIDTH1)], PHASE1, 7, y_page6, "h_phase2", behind)
         scatter([(6, 0, P)], y_page6)
 
         h_phase2 = held(behind, "h_phase2", [P, 3 * BANK], BF16)
         for strip, bank, first, last in ((2, 0, "b", "a"), (3, 1, "b", "a"), (4, 3, "a", "b")):
             later_envelope(strip, bank, h_phase2[:, BANK * (strip - 2) : BANK * (strip - 1)], first, last)
-        quantise_three_strips(PHASE2, h_phase2)
+        quantise_h(PHASE2, *PHASE2, h_phase2[:])
         kept = held(behind, "kept", [P, WIDTH1 + P], F32, tag="late_squares")
         nc.sync.dma_start(kept[:, 0:WIDTH1], wgo[:, 0:WIDTH1])
         log1p(kept[:, WIDTH1:], size_last[:, P:])
@@ -426,7 +425,7 @@ def tile_list_bell_envelope_chart_kernel(
         h_phase3 = held(sb, "h_phase3", [P, 3 * BANK], BF16)
         for strip, bank in ((5, 4), (6, 5), (7, 2)):
             later_envelope(strip, bank, h_phase3[:, BANK * (strip - 5) : BANK * (strip - 4)], "a", "b")
-        quantise_three_strips(PHASE3, h_phase3)
+        quantise_h(PHASE3, *PHASE3, h_phase3[:])
         features([(PAGES - 1, *PHASE2)], PHASE2, 2, page_columns(y2, PAGES - 1), "turn_size")
         scatter([(PAGES - 1, *PHASE2)], page_columns(y2, PAGES - 1))
 

@@ -28,8 +28,10 @@ WIDTH23 = PHASE2[1] - PHASE2[0]
 
 EARLY_PAGES = 3
 FIRST_PARTS = 4
+SPLIT_PAGE = 5
 
 A1_VECTOR = 256
+LAST_VECTOR = 64
 
 
 def tile_list_bell_envelope_chart_kernel(
@@ -42,8 +44,8 @@ def tile_list_bell_envelope_chart_kernel(
         ring = ctx.enter_context(tc.tile_pool(name="ring", bufs=2))
         psum = ctx.enter_context(tc.psum_pool(name="psum", bufs=1))
 
-        def held(pool, name, shape, dtype, tag=None):
-            return pool.tile(shape, dtype, name=name, tag=tag or name, align_bytes=64)
+        def held(pool, name, shape, dtype, tag=None, offset=None):
+            return pool.tile(shape, dtype, name=name, tag=tag or name, align_bytes=64, offset=offset)
 
         banks = [psum.tile([P, BANK], F32, name="bank%d" % b) for b in range(8)]
         pick = lists.tile([P, S // 16], U16, name="pick")
@@ -124,8 +126,6 @@ def tile_list_bell_envelope_chart_kernel(
         load_w(third, "b0hi", 0, H + HALF, 2 * H)
         for n in range(2):
             load_w(third, "b1hi%d" % n, 1, H + HALF + P * n, H + HALF + P * (n + 1))
-        wc_raw = held(third, "wc_raw", [P, 2 * N], U8)
-        nc.sync.dma_start(wc_raw[:].bitcast(I32), wc_words[0].bitcast(I32))
 
         w_codes = {name: held(third, "codes_" + name, [P, H], U32) for name in ("a0", "b0", "a1", "b1")}
         w_scales = {name: held(sb, "scales_" + name, [P, H], U8) for name in ("a0", "b0", "a1", "b1")}
@@ -146,9 +146,9 @@ def tile_list_bell_envelope_chart_kernel(
 
         v_codes = {}
 
-        def gather_words(pool, parts, tag=None):
+        def gather_words(pool, parts, offset=None):
             total = sum(hi - lo for a, lo, hi in parts)
-            words = held(pool, "v_codes%d_%d" % parts[0][0:2], [P, total], U32, tag=tag)
+            words = held(pool, "v_codes%d_%d" % parts[0][0:2], [P, total], U32, offset=offset)
             at = 0
             for a, lo, hi in parts:
                 window = tab[a][:].bitcast(U32)
@@ -265,6 +265,9 @@ def tile_list_bell_envelope_chart_kernel(
             round_w(w_raw["a1"][:, :, 0:A1_VECTOR], grouped["a1"][:, 0:A1_VECTOR, :], nc.vector.tensor_copy)
             round_w(w_raw["a1"][:, :, A1_VECTOR:], grouped["a1"][:, A1_VECTOR:, :], nc.scalar.copy)
             pack_w(grouped["a1"][:], "a1", 0)
+        chain = ctx.enter_context(tc.tile_pool(name="chain", bufs=1))
+        wc_raw = chain.tile([P, 2 * N], U8, name="wc_raw", align_bytes=64, offset=N - 64)
+        nc.sync.dma_start(wc_raw[:].bitcast(I32), wc_words[0].bitcast(I32))
         fourth = ctx.enter_context(tc.tile_pool(name="fourth", bufs=1))
         wc_scale_raw = held(fourth, "wc_scale_raw", [P, N], U8)
         nc.gpsimd.memset(wc_scale_raw[:].bitcast(I32), 0)
@@ -299,42 +302,56 @@ def tile_list_bell_envelope_chart_kernel(
             round_w(w_raw[piece][:], grouped[:], nc.vector.tensor_copy)
             pack_w(grouped[:], piece[0:2], first_col)
 
+        def pair_passes(a, bank, lo, hi):
+            for strip in range(2):
+                filter_pass(strip, "b", a, bank, a + strip == 0, a + strip == 2, lo, hi, (hi - lo) * strip)
+
+        def square_pair(pair, bank, lo, hi):
+            nc.scalar.activation(
+                pair[:].rearrange("j (s i p) -> j s i p", s=2, i=4)[:, :, :, lo // 4 : hi // 4],
+                banks[bank][:, 0 : 2 * (hi - lo)].rearrange("j (s p i) -> j s i p", s=2, i=4),
+                ACT.Square,
+            )
+
         for a in range(2):
             quantise_half("b%dlo" % a, 0)
-            for strip in range(2):
-                filter_pass(strip, "b", a, 4, a + strip == 0, a + strip == 2, 0, HALF, HALF * strip)
+            pair_passes(a, 4, 0, HALF)
         grouped_b0hi = held(fourth, "bf_b0hi", [P, HALF, 4], BF16)
         for n, copy in enumerate((nc.vector.tensor_copy, nc.scalar.copy)):
             round_w(w_raw["b0hi"][:, :, P * n : P * (n + 1)], grouped_b0hi[:, P * n : P * (n + 1), :], copy)
-        pack_w(grouped_b0hi[:], "b0", HALF)
-        for strip in range(2):
-            filter_pass(strip, "b", 0, 5 + strip, True, False, HALF, H)
-        filter_pass(2, "b", 0, 7, True, False)
         grouped_hi = [held(fourth, "bf_b1hi0", [P, P, 4], BF16), held(fourth, "bf_b1hi1", [P, P, 4], BF16)]
-        for n, copy in enumerate((nc.scalar.copy, nc.vector.tensor_copy)):
-            round_w(w_raw["b1hi%d" % n][:], grouped_hi[n][:], copy)
-        b_squares = held(third, "b_squares", [P, 3 * BANK], F32, tag="raw_b1hi0")
+        round_w(w_raw["b1hi0"][:], grouped_hi[0][:], nc.vector.tensor_copy)
+        pack_w(grouped_b0hi[:], "b0", HALF)
+        pack_w(grouped_hi[0][:], "b1", HALF)
+        squares[3, "a"] = held(third, "sq3a", [P, BANK], F32, tag="raw_b0hi")
+        square(3, "a", 3)
+        for a in range(2):
+            pair_passes(a, 2, HALF, HALF + P)
+        for strip in range(2):
+            filter_pass(strip, "b", 0, 5 + strip, True, False, HALF + P, H)
+        filter_pass(2, "b", 0, 7, True, False)
+        round_w(w_raw["b1hi1"][:, :, 0:LAST_VECTOR], grouped_hi[1][:, 0:LAST_VECTOR, :], nc.vector.tensor_copy)
+        round_w(w_raw["b1hi1"][:, :, LAST_VECTOR:], grouped_hi[1][:, LAST_VECTOR:, :], nc.scalar.copy)
+        pack_w(grouped_hi[1][:], "b1", HALF + P)
+        b_squares = held(third, "b_squares", [P, 2 * BANK], F32, tag="raw_b1hi1")
         for strip in range(2):
             squares[strip, "b"] = b_squares[:, BANK * strip : BANK * (strip + 1)]
-            square(strip, "b", 4, 0, HALF, HALF * strip)
-        squares[3, "a"] = b_squares[:, 2 * BANK :]
-        square(3, "a", 3)
-        for n in range(2):
-            pack_w(grouped_hi[n][:], "b1", HALF + P * n)
+        square_pair(b_squares, 4, 0, HALF)
         for strip in range(2):
-            filter_pass(strip, "b", 1, 5 + strip, False, True, HALF, H)
+            filter_pass(strip, "b", 1, 5 + strip, False, True, HALF + P, H)
         filter_pass(2, "b", 1, 7, False, True)
+        square_pair(b_squares, 2, HALF, HALF + P)
         for strip in range(2):
-            square(strip, "b", 5 + strip, HALF, H)
+            square(strip, "b", 5 + strip, HALF + P, H)
 
-        gather_words(fourth, [(1, 4 * P, S)], tag="bf_b1hi0")
         wc_codes = held(fourth, "wc_codes", [P, 2 * N], U8, tag="bf_b1hi1")
         nc.vector.tensor_copy(
             wc_codes[:].bitcast(U16).rearrange("p (b i m) -> p b i m", b=2, i=4),
             wc_raw[:].bitcast(U16).rearrange("p (b m i) -> p b i m", b=2, i=4),
         )
-        wc_planes = held(third, "wc_planes", [P, N], U8, tag="wc_raw")
-        nc.vector.tensor_copy(
+        gather_words(chain, [(1, 4 * P, S)], offset=3 * N - 128)
+        wc_planes = held(chain, "wc_planes", [P, N], U8, offset=0)
+        nc.gpsimd.tensor_copy(
             wc_planes[:].rearrange("p (b i m) -> p b i m", b=2, i=4),
             wc_scale_raw[:].rearrange("p (b m i) -> p b i m", b=2, i=4),
         )
@@ -345,6 +362,8 @@ def tile_list_bell_envelope_chart_kernel(
                 add_term(strip, squares[strip, "b"], stop=True)
                 root(strip, h_strip[:])
                 quantise_h(PHASE1, P * strip, P * (strip + 1), h_strip[:])
+        add_term(6, eps_rows, start=True)
+        add_term(6, squares[2, "a"])
         late_pages = ctx.enter_context(tc.tile_pool(name="late_pages", bufs=1))
         for page in range(EARLY_PAGES, PAGES):
             clear_page(late_pages, page, nc.gpsimd)
@@ -372,11 +391,11 @@ def tile_list_bell_envelope_chart_kernel(
             return at + total
 
         behind = ctx.enter_context(tc.tile_pool(name="behind", bufs=1))
-        late = ((2, "b", 7), (3, "b", 4), (4, "a", 5), (4, "b", 6))
+        late = ((2, "b", 7), (3, "b", 4), (4, "a", 5), (4, "b", 3))
         late_squares = held(behind, "late_squares", [P, len(late) * BANK], F32)
         for n, (strip, f, bank) in enumerate(late):
             squares[strip, f] = late_squares[:, BANK * n : BANK * (n + 1)]
-        at = group_of_parts([(page, P, WIDTH1) for page in range(FIRST_PARTS)], 6, at, "second_size", behind)
+        at = group_of_parts([(page, P, WIDTH1) for page in range(FIRST_PARTS)], 3, at, "second_size", behind)
         products([(7, 0, WIDTH1)], PHASE1, 2)
         size_last = held(behind, "size_last", [P, WIDTH1], F32)
         nc.scalar.activation(size_last[:], banks[2][:, 0:WIDTH1], ACT.Abs)
@@ -391,7 +410,9 @@ def tile_list_bell_envelope_chart_kernel(
         scatter([(6, 0, P)], y_page6)
 
         h_phase2 = held(behind, "h_phase2", [P, 3 * BANK], BF16)
-        for strip, bank, first, last in ((2, 0, "b", "a"), (3, 1, "b", "a"), (4, 3, "a", "b")):
+        add_term(6, squares[2, "b"], stop=True)
+        root(6, h_phase2[:, 0:BANK])
+        for strip, bank, first, last in ((3, 1, "b", "a"), (4, 0, "a", "b")):
             later_envelope(strip, bank, h_phase2[:, BANK * (strip - 2) : BANK * (strip - 1)], first, last)
         quantise_h(PHASE2, *PHASE2, h_phase2[:])
         kept = held(behind, "kept", [P, WIDTH1 + P], F32, tag="late_squares")
@@ -410,8 +431,8 @@ def tile_list_bell_envelope_chart_kernel(
         ]
         lo, hi = PHASE2
         groups = [([(0, lo, lo + P)], 3), ([(1, lo, lo + 2 * P)], 0), ([(0, lo + P, hi), (1, lo + 2 * P, hi)], 3)]
-        groups.extend(([(page, lo, hi)], 3) for page in range(2, PAGES - 1))
-        waits_for_log = {2: "sq5a", 3: "sq5b", len(groups) - 1: "h_phase3"}
+        groups.extend(([(page, lo, hi)], 3) for page in range(2, SPLIT_PAGE))
+        waits_for_log = {2: "sq5a", 3: "sq5b"}
         at = 0
         for n, (group, bank) in enumerate(groups):
             total = sum(end - first for page, first, end in group)
@@ -419,6 +440,16 @@ def tile_list_bell_envelope_chart_kernel(
             features(group, PHASE2, bank, y, waits_for_log.get(n))
             scatter(group, y)
             at = at + total
+        y5, y6, y7 = (page_columns(y2, page) for page in range(SPLIT_PAGE, PAGES))
+        products([(SPLIT_PAGE, lo, hi)], PHASE2, 3)
+        size_split = held(sb, "size_split", [P, WIDTH23], F32, tag="turn_size")
+        nc.scalar.activation(size_split[:], banks[3][:, 0:WIDTH23], ACT.Abs)
+        log1p(y5[:, 0 : 2 * P], size_split[:, 0 : 2 * P])
+        scatter([(SPLIT_PAGE, lo, hi - P)], y5)
+        features([(6, lo, hi)], PHASE2, 3, y6)
+        scatter([(6, lo, hi)], y6)
+        features([(7, lo, hi)], PHASE2, 3, y7, "h_phase3")
+        scatter([(7, lo, lo + P)], y7)
         for strip in (5, 6, 7):
             filter_squared(strip, "a", 6)
             filter_squared(strip, "b", 7)
@@ -426,8 +457,11 @@ def tile_list_bell_envelope_chart_kernel(
         for strip, bank in ((5, 4), (6, 5), (7, 2)):
             later_envelope(strip, bank, h_phase3[:, BANK * (strip - 5) : BANK * (strip - 4)], "a", "b")
         quantise_h(PHASE3, *PHASE3, h_phase3[:])
-        features([(PAGES - 1, *PHASE2)], PHASE2, 2, page_columns(y2, PAGES - 1), "turn_size")
-        scatter([(PAGES - 1, *PHASE2)], page_columns(y2, PAGES - 1))
+        kept_late = held(sb, "kept_late", [P, WIDTH23], F32, tag="sq7b")
+        nc.sync.dma_start(kept_late[:, 0 : 2 * P], wgo[:, lo + P : hi])
+        log1p(kept_late[:, 2 * P :], size_split[:, 2 * P :])
+        scatter_part(7, lo + P, hi, y7[:, P:], kept_late[:, 0 : 2 * P])
+        scatter_part(SPLIT_PAGE, hi - P, hi, kept_late[:, 2 * P :], wgo_sb[:, hi - P : hi])
 
         out_pages = out.rearrange("(b p i) t -> b i p t", b=2, i=4)
         y3 = [

from contextlib import ExitStack

import concourse.mybir as mybir

K, T, S, H, N, T2 = 1024, 2048, 1024, 512, 1024, 2048
FLOPS = 2 * K * 2 * H * S + 2 * H * N * S

F32 = mybir.dt.float32
BF16 = mybir.dt.bfloat16
I32 = mybir.dt.int32
U32 = mybir.dt.uint32
U16 = mybir.dt.uint16
U8 = mybir.dt.uint8
FP8X4 = mybir.dt.float8_e4m3fn_x4
FP4X4 = mybir.dt.float4_e2m1fn_x4
ACT = mybir.ActivationFunctionType
MULT = mybir.AluOpType.mult
MAX = mybir.AluOpType.max

P = 128
BANK = 512
HALF = H // 2
PAGES = 8

PHASE1, PHASE2, PHASE3 = (0, 256), (256, 640), (640, S)
WIDTH1 = PHASE1[1] - PHASE1[0]
WIDTH23 = PHASE2[1] - PHASE2[0]

EARLY_PAGES = 3
FIRST_PARTS = 4
SPLIT_PAGE = 5

A1_VECTOR = 256
LAST_VECTOR = 64


def tile_list_bell_envelope_chart_kernel(
    tc, tab_words, tab_scales, offs, wab, eps, wc_words, wc_scales, wgo, offs2, out
):
    nc = tc.nc
    with ExitStack() as ctx:
        lists = ctx.enter_context(tc.tile_pool(name="lists", bufs=1))
        sb = ctx.enter_context(tc.tile_pool(name="sb", bufs=1))
        ring = ctx.enter_context(tc.tile_pool(name="ring", bufs=2))
        psum = ctx.enter_context(tc.psum_pool(name="psum", bufs=1))

        def held(pool, name, shape, dtype, tag=None, offset=None):
            return pool.tile(shape, dtype, name=name, tag=tag or name, align_bytes=64, offset=offset)

        banks = [psum.tile([P, BANK], F32, name="bank%d" % b) for b in range(8)]
        pick = lists.tile([P, S // 16], U16, name="pick")
        place = lists.tile([P, S // 16], U16, name="place")

        scale_window = held(sb, "scale_window", [P, T], U8)
        one = held(sb, "one", [P, 1], F32)
        with tc.tile_pool(name="first", bufs=1) as first:
            one_made = first.tile([P, 1], F32, name="one_made")
            nc.gpsimd.memset(one_made[:], 1.0)
            nc.gpsimd.memset(scale_window[:].bitcast(I32), 0)
            nc.gpsimd.tensor_copy(one[:], one_made[:])
        second = ctx.enter_context(tc.tile_pool(name="second", bufs=1))
        root_warm = held(sb, "root_warm", [P, 1], F32)
        nc.scalar.activation(root_warm[:], one[:], ACT.Sqrt)
        ident = held(sb, "ident", [P, P], F32)
        zeros = held(second, "zeros", [P, P], F32, tag="page%d" % (EARLY_PAGES - 1))
        nc.vector.memset(zeros[:], 0.0)
        nc.gpsimd.affine_select(
            out=ident[:], in_=zeros[:], compare_op=mybir.AluOpType.not_equal, fill=1.0,
            base=0, pattern=[[-1, P]], channel_multiplier=1,
        )

        w_raw = {}
        tab = {}

        def load_w(pool, piece, a, lo, hi):
            w_raw[piece] = held(pool, "raw_" + piece, [P, 4, hi - lo], F32)
            rows = wab[512 * a : 512 * (a + 1), lo:hi].rearrange("(p i) c -> p i c", i=4)
            nc.sync.dma_start(w_raw[piece][:], rows)

        def load_tab(pool, a):
            tab[a] = held(pool, "tab%d" % a, [P, T], I32)
            nc.sync.dma_start(tab[a][:], tab_words[a].rearrange("p t i -> p (t i)").bitcast(I32))

        def load_a0_rows(pool, n):
            w_raw["a0", n] = held(pool, "raw_a0_%d" % n, [P, 2, H], F32)
            rows = wab[0:512, 0:H].rearrange("(p i) c -> p i c", i=4)
            nc.sync.dma_start(w_raw["a0", n][:], rows[:, 2 * n : 2 * n + 2, :])

        load_a0_rows(sb, 0)
        nc.sync.dma_start(pick[:], offs)
        nc.sync.dma_start(place[:], offs2)
        rows = tab_scales.bitcast(I32).rearrange("a (g e) t -> e g a t", e=2)
        for e in range(2):
            nc.sync.dma_start(scale_window[e:P:8, :].bitcast(I32), rows[e])
        load_a0_rows(second, 1)
        load_tab(second, 0)
        eps_sb = held(second, "eps_sb", [P, 4], F32)
        nc.sync.dma_start(eps_sb[:], eps.rearrange("(p i) -> p i", i=4))
        load_w(second, "a1", 1, 0, H)

        pages = {}

        def clear_page(pool, page, engine):
            pages[page] = held(pool, "page%d" % page, [P, T2], F32)
            engine.memset(pages[page][:], 0.0)

        for page in range(EARLY_PAGES - 1):
            clear_page(second, page, nc.vector)
        clear_page(second, EARLY_PAGES - 1, nc.gpsimd)

        v_scales = held(sb, "v_scales", [P, S], U8)
        with tc.tile_pool(name="picked", bufs=1) as picked_pool:
            picked = held(picked_pool, "picked_scales", [P, S], U8)
            nc.vector.tensor_copy(picked[:], scale_window[:].indirect(pick[:]))
            nc.vector.tensor_copy(v_scales[:].bitcast(I32), picked[:].bitcast(I32))
        third = ctx.enter_context(tc.tile_pool(name="third", bufs=1))
        for a in range(2):
            for e in range(2):
                nc.sync.dma_start(
                    v_scales[8 * a + 2 + e : P : 32, :].bitcast(I32),
                    v_scales[16 + 8 * a + e : P : 32, :].bitcast(I32),
                )
        load_tab(third, 1)
        load_w(third, "b0lo", 0, H, H + HALF)
        load_w(third, "b1lo", 1, H, H + HALF)
        load_w(third, "b0hi", 0, H + HALF, 2 * H)
        for n in range(2):
            load_w(third, "b1hi%d" % n, 1, H + HALF + P * n, H + HALF + P * (n + 1))

        w_codes = {name: held(third, "codes_" + name, [P, H], U32) for name in ("a0", "b0", "a1", "b1")}
        w_scales = {name: held(sb, "scales_" + name, [P, H], U8) for name in ("a0", "b0", "a1", "b1")}

        def round_w(raw, grouped, copy):
            copy(
                grouped.rearrange("p (c u) i -> p c i u", u=4),
                raw.rearrange("p i (c u) -> p c i u", u=4),
            )

        def pack_w(grouped, name, first_col):
            cols = slice(first_col, first_col + grouped.shape[1])
            nc.vector.quantize_mx(
                out=w_codes[name][:, cols].bitcast(FP8X4),
                scales=w_scales[name][:, cols],
                in_=grouped.rearrange("p c i -> p (c i)"),
            )

        v_codes = {}

        def gather_words(pool, parts, offset=None):
            total = sum(hi - lo for a, lo, hi in parts)
            words = held(pool, "v_codes%d_%d" % parts[0][0:2], [P, total], U32, offset=offset)
            at = 0
            for a, lo, hi in parts:
                window = tab[a][:].bitcast(U32)
                nc.vector.tensor_copy(words[:, at : at + hi - lo], window.indirect(pick[:, lo // 16 : hi // 16]))
                for strip in range(lo // P, hi // P):
                    v_codes[a, strip] = words[:, at + P * strip - lo : at + P * (strip + 1) - lo]
                at = at + hi - lo

        def filter_pass(strip, f, a, bank, start, stop, lo=0, hi=H, at=0):
            name = f + str(a)
            nc.tensor.matmul_mx(
                out=banks[bank][:, at : at + hi - lo],
                lhsT=v_codes[a, strip].bitcast(FP8X4),
                lhsT_scale=v_scales[8 * a : P, P * strip : P * (strip + 1)],
                rhs=w_codes[name][:, lo:hi].bitcast(FP8X4),
                rhs_scale=w_scales[name][:, lo:hi],
                start=start,
                stop=stop,
            )

        squares = {}

        def square(strip, f, bank, lo=0, hi=H, at=0):
            if (strip, f) not in squares:
                squares[strip, f] = held(sb, "sq%d%s" % (strip, f), [P, BANK], F32)
            nc.scalar.activation(
                squares[strip, f][:, 0:BANK].rearrange("j (i p) -> j i p", i=4)[:, :, lo // 4 : hi // 4],
                banks[bank][:, at : at + hi - lo].rearrange("j (p i) -> j i p", i=4),
                ACT.Square,
            )

        def filter_squared(strip, f, bank):
            for a in range(2):
                filter_pass(strip, f, a, bank, a == 0, a == 1)
            square(strip, f, bank)

        def add_term(bank, term, start=False, stop=False):
            for i in range(4):
                cols = slice(P * i, P * (i + 1))
                nc.tensor.matmul(
                    banks[bank][:, cols], term[:, cols], ident[:], is_transpose=True,
                    start=(start and i == 0), stop=(stop and i == 3),
                )

        def root(bank, h_bf):
            nc.scalar.activation(
                h_bf.rearrange("p (j i) -> p j i", i=4), banks[bank][:].rearrange("p (i j) -> p j i", i=4), ACT.Sqrt
            )

        def later_envelope(strip, bank, h_bf, first, last):
            add_term(bank, squares[strip, first], start=True)
            add_term(bank, eps_rows)
            add_term(bank, squares[strip, last], stop=True)
            root(bank, h_bf)

        h_codes = {}
        h_scales = {}

        def quantise_h(phase, lo, hi, h_bf):
            if phase not in h_codes:
                h_codes[phase] = held(sb, "h_codes%d" % phase[0], [P, phase[1] - phase[0]], U32)
                h_scales[phase] = held(sb, "h_scales%d" % phase[0], [P, phase[1] - phase[0]], U8)
            cols = slice(lo - phase[0], hi - phase[0])
            nc.vector.quantize_mx(out=h_codes[phase][:, cols].bitcast(FP8X4), scales=h_scales[phase][:, cols], in_=h_bf)

        def products(parts, phase, bank):
            passes = []
            at = 0
            for page, lo, hi in parts:
                for width in (2 * P, P):
                    if hi - lo >= width:
                        passes.append((page, lo - phase[0], width, at))
                        lo = lo + width
                        at = at + width
            for page, first, width, column in reversed(passes):
                nc.tensor.matmul_mx(
                    out=banks[bank][:, column : column + width],
                    lhsT=wc_codes[:, 2 * P * page : 2 * P * (page + 1)].bitcast(FP4X4),
                    lhsT_scale=wc_planes[:, P * page : P * (page + 1)],
                    rhs=h_codes[phase][:, first : first + width].bitcast(FP8X4),
                    rhs_scale=h_scales[phase][:, first : first + width],
                    start=True,
                    stop=True,
                )
            return at

        def log1p(y, size):
            nc.scalar.activation(y, size, ACT.Ln, bias=one[:])

        def features(parts, phase, bank, y, tag=None, pool=sb):
            total = products(parts, phase, bank)
            if tag is None:
                size = ring.tile([P, BANK], F32, name="size")
            else:
                size = held(pool, "size_" + tag, [P, BANK], F32, tag=tag)
            nc.scalar.activation(size[:, 0:total], banks[bank][:, 0:total], ACT.Abs)
            log1p(y, size[:, 0:total])

        def scatter_part(page, lo, hi, y, weights):
            nc.vector.tensor_tensor(pages[page][:].indirect(place[:, lo // 16 : hi // 16]), y, weights, MULT)

        def scatter(parts, y):
            at = 0
            for page, lo, hi in parts:
                scatter_part(page, lo, hi, y[:, at : at + hi - lo], wgo_sb[:, lo:hi])
                at = at + hi - lo

        with tc.tile_pool(name="rounded", bufs=1) as rounded:
            grouped = {name: held(rounded, "bf_" + name, [P, H, 4], BF16) for name in ("a0", "a1")}
            for n in range(2):
                round_w(w_raw["a0", n][:], grouped["a0"][:, :, 2 * n : 2 * n + 2], nc.scalar.copy)
            pack_w(grouped["a0"][:], "a0", 0)
            gather_words(third, [(0, 0, S)])
            round_w(w_raw["a1"][:, :, 0:A1_VECTOR], grouped["a1"][:, 0:A1_VECTOR, :], nc.vector.tensor_copy)
            round_w(w_raw["a1"][:, :, A1_VECTOR:], grouped["a1"][:, A1_VECTOR:, :], nc.scalar.copy)
            pack_w(grouped["a1"][:], "a1", 0)
        chain = ctx.enter_context(tc.tile_pool(name="chain", bufs=1))
        wc_raw = chain.tile([P, 2 * N], U8, name="wc_raw", align_bytes=64, offset=N - 64)
        nc.sync.dma_start(wc_raw[:].bitcast(I32), wc_words[0].bitcast(I32))
        fourth = ctx.enter_context(tc.tile_pool(name="fourth", bufs=1))
        wc_scale_raw = held(fourth, "wc_scale_raw", [P, N], U8)
        nc.gpsimd.memset(wc_scale_raw[:].bitcast(I32), 0)
        for d in range(4):
            nc.sync.dma_start(
                wc_scale_raw[32 * d : 32 * d + 4, :].bitcast(I32),
                wc_scales[0, 4 * d : 4 * d + 4, :].bitcast(I32),
            )
        wgo_sb = held(fourth, "wgo_sb", [P, S], F32)
        nc.sync.dma_start(wgo_sb[:], wgo)
        eps_rows = held(second, "eps_rows", [P, BANK], F32, tag="raw_a0_1")
        for i in range(4):
            nc.tensor.transpose(banks[7][:, P * i : P * (i + 1)], eps_sb[:, i : i + 1].to_broadcast([P, P]), ident[:])
        nc.scalar.copy(eps_rows[:], banks[7][:])
        gather_words(third, [(1, 0, 2 * P)])
        gather_words(third, [(1, 2 * P, 4 * P)])
        for strip in range(4):
            for a in range(2):
                filter_pass(strip, "a", a, strip, a == 0, a == 1)

        def open_sum(strip):
            square(strip, "a", strip)
            add_term(strip, eps_rows, start=True)
            add_term(strip, squares[strip, "a"])

        open_sum(0)
        open_sum(1)
        square(2, "a", 2)

        def quantise_half(piece, first_col):
            grouped = held(fourth, "bf_" + piece, [P, HALF, 4], BF16)
            round_w(w_raw[piece][:], grouped[:], nc.vector.tensor_copy)
            pack_w(grouped[:], piece[0:2], first_col)

        def pair_passes(a, bank, lo, hi):
            for strip in range(2):
                filter_pass(strip, "b", a, bank, a + strip == 0, a + strip == 2, lo, hi, (hi - lo) * strip)

        def square_pair(pair, bank, lo, hi):
            nc.scalar.activation(
                pair[:].rearrange("j (s i p) -> j s i p", s=2, i=4)[:, :, :, lo // 4 : hi // 4],
                banks[bank][:, 0 : 2 * (hi - lo)].rearrange("j (s p i) -> j s i p", s=2, i=4),
                ACT.Square,
            )

        for a in range(2):
            quantise_half("b%dlo" % a, 0)
            pair_passes(a, 4, 0, HALF)
        grouped_b0hi = held(fourth, "bf_b0hi", [P, HALF, 4], BF16)
        for n, copy in enumerate((nc.vector.tensor_copy, nc.scalar.copy)):
            round_w(w_raw["b0hi"][:, :, P * n : P * (n + 1)], grouped_b0hi[:, P * n : P * (n + 1), :], copy)
        grouped_hi = [held(fourth, "bf_b1hi0", [P, P, 4], BF16), held(fourth, "bf_b1hi1", [P, P, 4], BF16)]
        round_w(w_raw["b1hi0"][:], grouped_hi[0][:], nc.vector.tensor_copy)
        pack_w(grouped_b0hi[:], "b0", HALF)
        pack_w(grouped_hi[0][:], "b1", HALF)
        squares[3, "a"] = held(third, "sq3a", [P, BANK], F32, tag="raw_b0hi")
        square(3, "a", 3)
        for a in range(2):
            pair_passes(a, 2, HALF, HALF + P)
        for strip in range(2):
            filter_pass(strip, "b", 0, 5 + strip, True, False, HALF + P, H)
        filter_pass(2, "b", 0, 7, True, False)
        round_w(w_raw["b1hi1"][:, :, 0:LAST_VECTOR], grouped_hi[1][:, 0:LAST_VECTOR, :], nc.vector.tensor_copy)
        round_w(w_raw["b1hi1"][:, :, LAST_VECTOR:], grouped_hi[1][:, LAST_VECTOR:, :], nc.scalar.copy)
        pack_w(grouped_hi[1][:], "b1", HALF + P)
        b_squares = held(third, "b_squares", [P, 2 * BANK], F32, tag="raw_b1hi1")
        for strip in range(2):
            squares[strip, "b"] = b_squares[:, BANK * strip : BANK * (strip + 1)]
        square_pair(b_squares, 4, 0, HALF)
        for strip in range(2):
            filter_pass(strip, "b", 1, 5 + strip, False, True, HALF + P, H)
        filter_pass(2, "b", 1, 7, False, True)
        square_pair(b_squares, 2, HALF, HALF + P)
        for strip in range(2):
            square(strip, "b", 5 + strip, HALF + P, H)

        wc_codes = held(fourth, "wc_codes", [P, 2 * N], U8, tag="bf_b1hi1")
        nc.vector.tensor_copy(
            wc_codes[:].bitcast(U16).rearrange("p (b i m) -> p b i m", b=2, i=4),
            wc_raw[:].bitcast(U16).rearrange("p (b m i) -> p b i m", b=2, i=4),
        )
        gather_words(chain, [(1, 4 * P, S)], offset=3 * N - 128)
        wc_planes = held(chain, "wc_planes", [P, N], U8, offset=0)
        nc.gpsimd.tensor_copy(
            wc_planes[:].rearrange("p (b i m) -> p b i m", b=2, i=4),
            wc_scale_raw[:].rearrange("p (b m i) -> p b i m", b=2, i=4),
        )

        with tc.tile_pool(name="first_roots", bufs=1) as first_roots:
            for strip in range(2):
                h_strip = held(first_roots, "h_strip%d" % strip, [P, BANK], BF16)
                add_term(strip, squares[strip, "b"], stop=True)
                root(strip, h_strip[:])
                quantise_h(PHASE1, P * strip, P * (strip + 1), h_strip[:])
        add_term(6, eps_rows, start=True)
        add_term(6, squares[2, "a"])
        late_pages = ctx.enter_context(tc.tile_pool(name="late_pages", bufs=1))
        for page in range(EARLY_PAGES, PAGES):
            clear_page(late_pages, page, nc.gpsimd)

        y1 = held(second, "y1", [P, PAGES * WIDTH1], F32, tag="tab0")
        first_parts = [(page, 0, P) for page in range(FIRST_PARTS)]
        total = FIRST_PARTS * P
        spans = ((first_parts[0:1], 4, slice(0, P)), (first_parts[1:], 5, slice(P, total)))
        negated = held(sb, "negated", [P, total], F32)
        for parts, bank, cols in spans:
            width = products(parts, PHASE1, bank)
            nc.vector.tensor_scalar(negated[:, cols], banks[bank][:, 0:width], -1.0, None, MULT)
        with tc.tile_pool(name="first_sizes", bufs=1) as first_sizes:
            size_first = held(first_sizes, "size_first", [P, total], F32)
            for parts, bank, cols in spans:
                nc.vector.tensor_tensor(size_first[:, cols], banks[bank][:, 0 : P * len(parts)], negated[:, cols], MAX)
                log1p(y1[:, cols], size_first[:, cols])
        scatter(first_parts, y1[:, 0:total])
        at = total

        def group_of_parts(group, bank, at, tag, pool):
            total = sum(hi - lo for page, lo, hi in group)
            features(group, PHASE1, bank, y1[:, at : at + total], tag, pool)
            scatter(group, y1[:, at : at + total])
            return at + total

        behind = ctx.enter_context(tc.tile_pool(name="behind", bufs=1))
        late = ((2, "b", 7), (3, "b", 4), (4, "a", 5), (4, "b", 3))
        late_squares = held(behind, "late_squares", [P, len(late) * BANK], F32)
        for n, (strip, f, bank) in enumerate(late):
            squares[strip, f] = late_squares[:, BANK * n : BANK * (n + 1)]
        at = group_of_parts([(page, P, WIDTH1) for page in range(FIRST_PARTS)], 3, at, "second_size", behind)
        products([(7, 0, WIDTH1)], PHASE1, 2)
        size_last = held(behind, "size_last", [P, WIDTH1], F32)
        nc.scalar.activation(size_last[:], banks[2][:, 0:WIDTH1], ACT.Abs)
        square(*late[0])
        at = group_of_parts([(4, 0, WIDTH1), (5, 0, WIDTH1)], 2, at, "third_size", behind)
        for step in late[1:]:
            filter_squared(*step)
        y_page7 = y1[:, at : at + P]
        log1p(y_page7, size_last[:, 0:P])
        y_page6 = y1[:, at + P : at + P + WIDTH1]
        features([(6, 0, WIDTH1)], PHASE1, 7, y_page6, "h_phase2", behind)
        scatter([(6, 0, P)], y_page6)

        h_phase2 = held(behind, "h_phase2", [P, 3 * BANK], BF16)
        add_term(6, squares[2, "b"], stop=True)
        root(6, h_phase2[:, 0:BANK])
        for strip, bank, first, last in ((3, 1, "b", "a"), (4, 0, "a", "b")):
            later_envelope(strip, bank, h_phase2[:, BANK * (strip - 2) : BANK * (strip - 1)], first, last)
        quantise_h(PHASE2, *PHASE2, h_phase2[:])
        kept = held(behind, "kept", [P, WIDTH1 + P], F32, tag="late_squares")
        nc.sync.dma_start(kept[:, 0:WIDTH1], wgo[:, 0:WIDTH1])
        log1p(kept[:, WIDTH1:], size_last[:, P:])
        scatter_part(7, 0, P, y_page7, kept[:, 0:P])
        scatter_part(6, P, WIDTH1, y_page6[:, P:WIDTH1], kept[:, P:WIDTH1])
        scatter_part(7, P, WIDTH1, kept[:, WIDTH1:], wgo_sb[:, P:WIDTH1])

        def page_columns(y_tiles, page):
            return y_tiles[page // 4][:, WIDTH23 * (page % 4) : WIDTH23 * (page % 4 + 1)]

        y2 = [
            held(sb, "y2a", [P, 4 * WIDTH23], F32, tag="y_spare"),
            held(third, "y2b", [P, 4 * WIDTH23], F32, tag="tab1"),
        ]
        lo, hi = PHASE2
        groups = [([(0, lo, lo + P)], 3), ([(1, lo, lo + 2 * P)], 0), ([(0, lo + P, hi), (1, lo + 2 * P, hi)], 3)]
        groups.extend(([(page, lo, hi)], 3) for page in range(2, SPLIT_PAGE))
        waits_for_log = {2: "sq5a", 3: "sq5b"}
        at = 0
        for n, (group, bank) in enumerate(groups):
            total = sum(end - first for page, first, end in group)
            y = y2[at // (4 * WIDTH23)][:, at % (4 * WIDTH23) : at % (4 * WIDTH23) + total]
            features(group, PHASE2, bank, y, waits_for_log.get(n))
            scatter(group, y)
            at = at + total
        y5, y6, y7 = (page_columns(y2, page) for page in range(SPLIT_PAGE, PAGES))
        products([(SPLIT_PAGE, lo, hi)], PHASE2, 3)
        size_split = held(sb, "size_split", [P, WIDTH23], F32, tag="turn_size")
        nc.scalar.activation(size_split[:], banks[3][:, 0:WIDTH23], ACT.Abs)
        log1p(y5[:, 0 : 2 * P], size_split[:, 0 : 2 * P])
        scatter([(SPLIT_PAGE, lo, hi - P)], y5)
        features([(6, lo, hi)], PHASE2, 3, y6)
        scatter([(6, lo, hi)], y6)
        features([(7, lo, hi)], PHASE2, 3, y7, "h_phase3")
        scatter([(7, lo, lo + P)], y7)
        for strip in (5, 6, 7):
            filter_squared(strip, "a", 6)
            filter_squared(strip, "b", 7)
        h_phase3 = held(sb, "h_phase3", [P, 3 * BANK], BF16)
        for strip, bank in ((5, 4), (6, 5), (7, 2)):
            later_envelope(strip, bank, h_phase3[:, BANK * (strip - 5) : BANK * (strip - 4)], "a", "b")
        quantise_h(PHASE3, *PHASE3, h_phase3[:])
        kept_late = held(sb, "kept_late", [P, WIDTH23], F32, tag="sq7b")
        nc.sync.dma_start(kept_late[:, 0 : 2 * P], wgo[:, lo + P : hi])
        log1p(kept_late[:, 2 * P :], size_split[:, 2 * P :])
        scatter_part(7, lo + P, hi, y7[:, P:], kept_late[:, 0 : 2 * P])
        scatter_part(SPLIT_PAGE, hi - P, hi, kept_late[:, 2 * P :], wgo_sb[:, hi - P : hi])

        out_pages = out.rearrange("(b p i) t -> b i p t", b=2, i=4)
        y3 = [
            held(second, "y3a", [P, 4 * WIDTH23], F32, tag="tab0"),
            held(sb, "y3b", [P, 4 * WIDTH23], F32, tag="y_spare"),
        ]
        lo, hi = PHASE3
        groups = [((0, lo, lo + P), 2), ((1, lo, hi), 4), ((0, lo + P, hi), 2)]
        groups.extend(((page, lo, hi), 2) for page in range(2, PAGES))
        for (page, first, end), bank in groups:
            y = page_columns(y3, page)[:, first - lo : end - lo]
            features([(page, first, end)], PHASE3, bank, y, "turn_size" if page == 1 else None)
            scatter([(page, first, end)], y)
            if end < hi:
                continue
            rows = out_pages[page // 4, page % 4]
            if page < PAGES - 1:
                nc.sync.dma_start(rows, pages[page][:])
            else:
                nc.sync.dma_start(rows[:, 0 : T2 // 2], pages[page][:, 0 : T2 // 2])
                nc.scalar.dma_start(rows[:, T2 // 2 :], pages[page][:, T2 // 2 :])
